import numpy as np
import ml_dtypes


def mxq(x, axis, fmt="e4m3"):
    dtype, down = {"e4m3": (ml_dtypes.float8_e4m3fn, 7), "e5m2": (ml_dtypes.float8_e5m2, 14)}[fmt]
    v = np.moveaxis(np.asarray(x, np.float32).astype(ml_dtypes.bfloat16).astype(np.float64), axis, -1)
    blocks = v.reshape(v.shape[:-1] + (-1, 32))
    amax = np.abs(blocks).max(-1, keepdims=True)
    byte = np.maximum(np.where(amax > 0, np.frexp(amax)[1] - 1 + 127, 0) - down, 1)
    scale = np.exp2(byte - 127.0)
    codes = (blocks / scale).astype(np.float32).astype(dtype).astype(np.float64)
    return np.moveaxis((codes * scale).reshape(v.shape), -1, axis)


WIDE = False


def mx_kscale(k):
    if not WIDE:
        return np.ones(k)
    levels = np.array([24, -24, 12, -12, 0])
    if k % 512:
        return np.exp2(np.random.permutation(np.resize(levels, k // 32))).repeat(32)
    a = np.empty((k // 512, 16))
    for p in range(k // 512):
        a[p, :8] = np.random.permutation(np.resize(levels, 8))
        for g in range(8):
            far = levels[np.abs(levels - a[p, g]) >= 10]
            a[p, g + 8] = far[np.random.randint(len(far))]
    return np.exp2(a.ravel()).repeat(32)


def f64(x):
    return np.asarray(x).astype(np.float64)


def striped(idx):
    return np.tile(idx.reshape(-1, 16).T, (8, 1)).astype(np.uint16)


def unstriped(offs):
    return offs[:16].T.reshape(-1).astype(np.int64)


E2M1 = np.array([0.0, 0.5, 1.0, 1.5, 2.0, 3.0, 4.0, 6.0, -0.0, -0.5, -1.0, -1.5, -2.0, -3.0, -4.0, -6.0])


def pack_weight(w, fmt):
    k, n = w.shape
    w = f64(np.asarray(w, np.float32).astype(ml_dtypes.bfloat16)).reshape(k // 32, 32, n)
    amax = np.abs(w).max(1)
    if fmt == "e4m3":
        byte = np.frexp(amax)[1] - 1 + 127 - 7
    else:
        mant, ex = np.frexp(amax / 6.0)
        byte = np.where(mant > 0.5, ex, ex - 1) + 127
    byte = np.clip(np.where(amax > 0, byte, 1), 1, 254)
    scaled = (w * np.exp2(127.0 - byte)[:, None, :]).reshape(k, n).astype(np.float32)
    by_word = np.ascontiguousarray(scaled.reshape(k // 512, 128, 4, n).transpose(0, 1, 3, 2))
    if fmt == "e4m3":
        words = by_word.astype(ml_dtypes.float8_e4m3fn).view(np.uint8)
    else:
        c = by_word.astype(ml_dtypes.float4_e2m1fn).view(np.uint8) & 0xF
        words = (c[..., 0::2] | (c[..., 1::2] << 4)).reshape(k // 512, 128, 2 * n)
    return np.ascontiguousarray(words), np.ascontiguousarray(byte.astype(np.uint8).reshape(k // 512, 16, n))


def unpack_weight(words, scales, fmt):
    g, _, n = scales.shape
    words = np.ascontiguousarray(words).reshape(g, 128, n, -1)
    if fmt == "e4m3":
        vals = words.view(ml_dtypes.float8_e4m3fn).astype(np.float64)
    else:
        nib = np.empty((g, 128, n, 4), np.uint8)
        nib[..., 0::2] = words & 0xF
        nib[..., 1::2] = words >> 4
        vals = E2M1[nib]
    vals = vals * np.repeat(np.exp2(scales.astype(np.float64) - 127.0), 8, axis=1)[..., None]
    return vals.transpose(0, 1, 3, 2).reshape(g * 512, n)


def pack_table4(v):
    words, scales = pack_weight(v, "e2m1")
    g, t = words.shape[0] // 2, v.shape[1]
    return np.ascontiguousarray(words.reshape(g, 2, 128, t, 2).transpose(0, 2, 3, 1, 4).reshape(g, 128, t, 4)), scales


def unpack_table4(words, scales):
    g, _, t, _ = words.shape
    return unpack_weight(words.reshape(g, 128, t, 2, 2).transpose(0, 3, 1, 2, 4).reshape(2 * g, 128, 2 * t), scales, "e2m1")


def silu(f):
    return f / (1.0 + np.exp(-np.maximum(f, -700.0)))


K, L, N, T, J = 1024, 1024, 1024, 2048, 1024


def setup_inputs():
    n = np.random.standard_normal
    s = mx_kscale(K)[:, None]
    s2 = mx_kscale(L)[:, None]
    p_tab = pack_table4(n((K, T)) * s)
    return {
        "tab_words": p_tab[0],
        "tab_scales": p_tab[1],
        "wt": (n((K, N)) / np.sqrt(K) / s).astype(np.float32),
        "x": (n((L, J)) * s2).astype(np.float32),
        "wx": (n((L, N)) / np.sqrt(L) / s2).astype(np.float32),
        "b": (0.3 * n(N)).astype(np.float32),
        "offs": striped(np.random.permutation(T)[:J]),
    }


def reference(tab_words, tab_scales, wt, x, wx, b, offs):
    idx = unstriped(offs)
    tab_ = unpack_table4(tab_words, tab_scales)[:, idx]
    wt_q_ = mxq(f64(wt), 0, "e4m3")
    wt_r_ = mxq(f64(wt) - wt_q_, 0, "e4m3")
    x_ = mxq(f64(x), 0, "e4m3")
    wx_ = mxq(f64(wx), 0, "e4m3")
    y = wt_q_.T @ tab_ + wt_r_.T @ tab_ + wx_.T @ x_
    return silu(y + f64(b)[:, None])

@@ -1,0 +1,268 @@
+from contextlib import ExitStack
+
+import concourse.mybir as mybir
+
+K, L, N, T, J = 1024, 1024, 1024, 2048, 1024
+FLOPS = 2 * N * J * (2 * K + L) + 2 * 512 * K * N
+
+F32 = mybir.dt.float32
+BF16 = mybir.dt.bfloat16
+I32 = mybir.dt.int32
+U32 = mybir.dt.uint32
+U16 = mybir.dt.uint16
+U8 = mybir.dt.uint8
+FP8X4 = mybir.dt.float8_e4m3fn_x4
+FP4X4 = mybir.dt.float4_e2m1fn_x4
+SILU = mybir.ActivationFunctionType.Silu
+ALU = mybir.AluOpType
+
+P = 128
+PACK = 4
+K_PASS = P * PACK
+PASSES = K // K_PASS
+CHUNK = 256
+CHUNKS = N // CHUNK
+TILES = CHUNK // P
+HALF = 512
+HALVES = J // HALF
+PAIR = 2
+SHIFT = 4
+SHIFT_ROWS = 112
+
+
+def tile_list_tiert_silu_kernel(tc, tab_words, tab_scales, wt, x, wx, b, offs, out):
+    nc = tc.nc
+    with ExitStack() as ctx:
+        keep = ctx.enter_context(tc.tile_pool(name="keep", bufs=1))
+        stage = ctx.enter_context(tc.tile_pool(name="stage", bufs=12))
+        acc_pool = ctx.enter_context(tc.psum_pool(name="acc", bufs=6))
+        back_pool = ctx.enter_context(tc.psum_pool(name="back", bufs=2))
+
+        def load_rows(src, a, cols, name):
+            raw = keep.tile([P, PACK, cols.stop - cols.start], F32, name=name)
+            nc.sync.dma_start(out=raw[:], in_=src[a * K_PASS : (a + 1) * K_PASS, cols].rearrange("(p t) w -> p t w", t=PACK))
+            return raw
+
+        def woven(ap):
+            return ap.rearrange("p (c i t) -> p c t i", i=PAIR, t=PACK)
+
+        def by_pairs(ap):
+            return ap.rearrange("p t (c i) -> p c t i", i=PAIR)
+
+        def round_rows(raw_ap, on_vector):
+            rounded = stage.tile([P, CHUNK * PACK], BF16, name="rounded", align_bytes=64)
+            if on_vector:
+                nc.vector.tensor_copy(out=woven(rounded[:]), in_=by_pairs(raw_ap))
+            else:
+                nc.scalar.copy(out=woven(rounded[:]), in_=by_pairs(raw_ap))
+            return rounded
+
+        def quantize(rounded_ap, codes_ap, scales_ap):
+            nc.vector.quantize_mx(out=codes_ap.bitcast(FP8X4), scales=scales_ap, in_=rounded_ap)
+
+        def operand(width, name):
+            codes = keep.tile([P, width], U32, name=name + "_codes", align_bytes=64)
+            scales = keep.tile([P, width], U8, name=name + "_scales", align_bytes=64)
+            return codes, scales
+
+        offsets = keep.tile([P, J // 16], U16, name="offsets")
+        nc.sync.dma_start(offsets[:], offs)
+
+        scale_window = keep.tile([P, T], U8, name="scale_window", align_bytes=64)
+        nc.vector.memset(scale_window[:].bitcast(I32), 0)
+        for q in range(4):
+            nc.sync.dma_start(
+                out=scale_window[32 * q : 32 * q + 2 * SHIFT, :].bitcast(I32),
+                in_=tab_scales[:, 4 * q : 4 * q + 4, :].bitcast(I32),
+            )
+        word_window = keep.tile([P, T], U32, name="word_window", align_bytes=64)
+        nc.sync.dma_start(out=word_window[:].bitcast(I32), in_=tab_words[0].rearrange("p t z -> p (t z)").bitcast(I32))
+
+        wt_raw = {}
+        wx_raw = {}
+        x_raw = {}
+        for a in range(PASSES):
+            wt_raw[0, a] = load_rows(wt, a, slice(0, CHUNK), "wt_raw_0_%d" % a)
+
+        zero = keep.tile([P, 1], F32, name="zero")
+        nc.gpsimd.memset(zero[:], 0.0)
+        warm = keep.tile([P, 1], F32, name="warm")
+        nc.scalar.activation(out=warm[:], in_=zero[:], func=SILU)
+
+        row_gap = keep.tile([P, K_PASS], I32, name="row_gap")
+        nc.gpsimd.iota(row_gap[:], pattern=[[1, K_PASS]], base=0, channel_multiplier=-PACK)
+        ones = keep.tile([P, PACK, K_PASS], BF16, name="ones", align_bytes=64)
+        for t in range(PACK):
+            nc.vector.tensor_scalar(out=ones[:, t, :], in0=row_gap[:], scalar1=float(t), scalar2=None, op0=ALU.is_equal)
+        ident_codes, ident_scales = operand(K_PASS, "ident")
+        quantize(ones[:].rearrange("p t w -> p (t w)"), ident_codes[:], ident_scales[:])
+
+        picked_scales = keep.tile([P, J], U8, name="picked_scales", align_bytes=64)
+        nc.vector.tensor_copy(picked_scales[:], scale_window[:].indirect(offsets[:]))
+        moved_scales = keep.tile([P, J], U8, name="moved_scales", align_bytes=64)
+        nc.gpsimd.memset(moved_scales[:].bitcast(I32), 0)
+        nc.scalar.dma_start(
+            out=moved_scales[0:SHIFT_ROWS, :].bitcast(I32),
+            in_=picked_scales[SHIFT : SHIFT + SHIFT_ROWS, :].bitcast(I32),
+        )
+        tab_planes = [picked_scales, moved_scales]
+
+        tab_codes = {}
+
+        def gather_words(h):
+            picked = keep.tile([P, HALF], U32, name="picked_%d" % h, align_bytes=64)
+            nc.vector.tensor_copy(picked[:], word_window[:].indirect(offsets[:, h * HALF // 16 : (h + 1) * HALF // 16]))
+            parted = keep.tile([P, PASSES, 2 * HALF], U8, name="parted_%d" % h, align_bytes=64)
+            nc.vector.tensor_copy(
+                out=parted[:].bitcast(U16),
+                in_=picked[:].bitcast(U16).rearrange("p (s d) -> p d s", d=PASSES),
+            )
+            tab_codes[h] = parted
+
+        wq = {}
+        wr = {}
+        wxq = {}
+        xq = {}
+
+        def make_tiers(c, on_vector):
+            for a in range(PASSES):
+                wq[c, a] = operand(CHUNK, "wq_%d_%d" % (c, a))
+                quantize(round_rows(wt_raw[c, a][:], on_vector)[:], wq[c, a][0][:], wq[c, a][1][:])
+            for a in range(PASSES):
+                rest = stage.tile([P, CHUNK * PACK], BF16, name="rounded", align_bytes=64)
+                for u in range(TILES):
+                    cols = slice(u * P, (u + 1) * P)
+                    back = back_pool.tile([P, PACK, P], F32, name="back")
+                    for t in range(PACK):
+                        nc.tensor.matmul_mx(
+                            out=back[:, t, :],
+                            lhsT=ident_codes[:, t * P : (t + 1) * P].bitcast(FP8X4),
+                            lhsT_scale=ident_scales[:, t * P : (t + 1) * P],
+                            rhs=wq[c, a][0][:, cols].bitcast(FP8X4),
+                            rhs_scale=wq[c, a][1][:, cols],
+                            start=True,
+                            stop=True,
+                        )
+                    nc.vector.tensor_tensor(
+                        out=woven(rest[:, u * P * PACK : (u + 1) * P * PACK]),
+                        in0=by_pairs(wt_raw[c, a][:, :, cols]),
+                        in1=by_pairs(back[:]),
+                        op=ALU.subtract,
+                    )
+                wr[c, a] = operand(CHUNK, "wr_%d_%d" % (c, a))
+                quantize(rest[:], wr[c, a][0][:], wr[c, a][1][:])
+
+        def make_wx(c, on_vector):
+            for a in range(PASSES):
+                wxq[c, a] = operand(CHUNK, "wxq_%d_%d" % (c, a))
+                quantize(round_rows(wx_raw[c, a][:], on_vector)[:], wxq[c, a][0][:], wxq[c, a][1][:])
+
+        def make_x(h, on_vector):
+            for a in range(PASSES):
+                xq[h, a] = operand(HALF, "xq_%d_%d" % (h, a))
+                for s in range(HALF // CHUNK):
+                    cols = slice(s * CHUNK, (s + 1) * CHUNK)
+                    quantize(round_rows(x_raw[h, a][:, :, cols], on_vector)[:], xq[h, a][0][:, cols], xq[h, a][1][:, cols])
+
+        acc = {}
+
+        def table_passes(c, u, h):
+            cols = slice(u * P, (u + 1) * P)
+            acc[c, u, h] = acc_pool.tile([P, HALF], F32, name="acc")
+            for tier in (wq, wr):
+                for a in range(PASSES):
+                    nc.tensor.matmul_mx(
+                        out=acc[c, u, h][:],
+                        lhsT=tier[c, a][0][:, cols].bitcast(FP8X4),
+                        lhsT_scale=tier[c, a][1][:, cols],
+                        rhs=tab_codes[h][:, a, :].bitcast(FP4X4),
+                        rhs_scale=tab_planes[a][:, h * HALF : (h + 1) * HALF],
+                        start=(tier is wq and a == 0),
+                        stop=False,
+                    )
+
+        def finish(c, u, h):
+            cols = slice(u * P, (u + 1) * P)
+            for a in range(PASSES):
+                nc.tensor.matmul_mx(
+                    out=acc[c, u, h][:],
+                    lhsT=wxq[c, a][0][:, cols].bitcast(FP8X4),
+                    lhsT_scale=wxq[c, a][1][:, cols],
+                    rhs=xq[h, a][0][:].bitcast(FP8X4),
+                    rhs_scale=xq[h, a][1][:],
+                    start=False,
+                    stop=(a == PASSES - 1),
+                )
+            n_tile = c * TILES + u
+            result = keep.tile([P, HALF], F32, name="result_%d_%d" % (n_tile, h))
+            nc.scalar.activation(out=result[:], in_=acc[c, u, h][:], func=SILU, bias=bias[:, n_tile : n_tile + 1])
+            nc.sync.dma_start(out=out[n_tile * P : (n_tile + 1) * P, h * HALF : (h + 1) * HALF], in_=result[:])
+
+        def load_chunk(src, raws, c, name):
+            for a in range(PASSES):
+                raws[c, a] = load_rows(src, a, slice(c * CHUNK, (c + 1) * CHUNK), "%s_%d_%d" % (name, c, a))
+
+        def load_x(h):
+            for a in range(PASSES):
+                x_raw[h, a] = load_rows(x, a, slice(h * HALF, (h + 1) * HALF), "x_raw_%d_%d" % (h, a))
+
+        bias = keep.tile([P, N // P], F32, name="bias")
+
+        def load_bias():
+            with nc.allow_non_contiguous_dma(reason="one bias value for each partition and output tile"):
+                nc.sync.dma_start(out=bias[:], in_=b.rearrange("(c p) -> p c", p=P))
+
+        load_x(0)
+        load_bias()
+        load_chunk(wx, wx_raw, 0, "wx_raw")
+        load_chunk(wt, wt_raw, 1, "wt_raw")
+        load_chunk(wx, wx_raw, 1, "wx_raw")
+        load_x(1)
+        load_chunk(wt, wt_raw, 2, "wt_raw")
+        load_chunk(wx, wx_raw, 2, "wx_raw")
+        load_chunk(wt, wt_raw, 3, "wt_raw")
+        load_chunk(wx, wx_raw, 3, "wx_raw")
+        gather_words(0)
+        make_tiers(0, False)
+        table_passes(0, 0, 0)
+        table_passes(0, 1, 0)
+        gather_words(1)
+        table_passes(0, 0, 1)
+        table_passes(0, 1, 1)
+        make_x(0, False)
+        make_wx(0, False)
+        make_tiers(1, False)
+        finish(0, 0, 0)
+        finish(0, 1, 0)
+        table_passes(1, 0, 0)
+        table_passes(1, 1, 0)
+        table_passes(1, 0, 1)
+        table_passes(1, 1, 1)
+        make_wx(1, False)
+        finish(1, 0, 0)
+        finish(1, 1, 0)
+        make_x(1, True)
+        make_tiers(2, False)
+        finish(0, 0, 1)
+        finish(0, 1, 1)
+        finish(1, 0, 1)
+        finish(1, 1, 1)
+        make_wx(2, False)
+        make_tiers(3, False)
+        table_passes(2, 0, 0)
+        finish(2, 0, 0)
+        table_passes(2, 0, 1)
+        finish(2, 0, 1)
+        table_passes(2, 1, 0)
+        finish(2, 1, 0)
+        table_passes(2, 1, 1)
+        finish(2, 1, 1)
+        make_wx(3, False)
+        table_passes(3, 0, 0)
+        finish(3, 0, 0)
+        table_passes(3, 0, 1)
+        finish(3, 0, 1)
+        table_passes(3, 1, 0)
+        finish(3, 1, 0)
+        table_passes(3, 1, 1)
+        finish(3, 1, 1)

@@ -1,6 +1,7 @@
 from contextlib import ExitStack
 
 import concourse.mybir as mybir
+from concourse.masks import make_identity
 
 K, L, N, T, J = 1024, 1024, 1024, 2048, 1024
 FLOPS = 2 * N * J * (2 * K + L) + 2 * 512 * K * N
@@ -26,16 +27,17 @@ TILES = CHUNK // P
 HALF = 512
 HALVES = J // HALF
 PAIR = 2
-SHIFT = 4
+SHIFT = 16
 SHIFT_ROWS = 112
+WARM = 0
 
 
 def tile_list_tiert_silu_kernel(tc, tab_words, tab_scales, wt, x, wx, b, offs, out):
     nc = tc.nc
     with ExitStack() as ctx:
         keep = ctx.enter_context(tc.tile_pool(name="keep", bufs=1))
-        stage = ctx.enter_context(tc.tile_pool(name="stage", bufs=12))
-        acc_pool = ctx.enter_context(tc.psum_pool(name="acc", bufs=6))
+        stage = ctx.enter_context(tc.tile_pool(name="stage", bufs=9))
+        acc_pool = ctx.enter_context(tc.psum_pool(name="acc", bufs=1))
         back_pool = ctx.enter_context(tc.psum_pool(name="back", bufs=2))
 
         def load_rows(src, a, cols, name):
@@ -70,13 +72,11 @@ def tile_list_tiert_silu_kernel(tc, tab_words, tab_scales, wt, x, wx, b, offs, o
 
         scale_window = keep.tile([P, T], U8, name="scale_window", align_bytes=64)
         nc.vector.memset(scale_window[:].bitcast(I32), 0)
-        for q in range(4):
-            nc.sync.dma_start(
-                out=scale_window[32 * q : 32 * q + 2 * SHIFT, :].bitcast(I32),
-                in_=tab_scales[:, 4 * q : 4 * q + 4, :].bitcast(I32),
+        for r in range(4):
+            nc.scalar.dma_start(
+                out=scale_window[r:P:SHIFT, :].bitcast(I32),
+                in_=tab_scales[:, r:16:4, :].rearrange("a q t -> q a t").bitcast(I32),
             )
-        word_window = keep.tile([P, T], U32, name="word_window", align_bytes=64)
-        nc.sync.dma_start(out=word_window[:].bitcast(I32), in_=tab_words[0].rearrange("p t z -> p (t z)").bitcast(I32))
 
         wt_raw = {}
         wx_raw = {}
@@ -84,10 +84,18 @@ def tile_list_tiert_silu_kernel(tc, tab_words, tab_scales, wt, x, wx, b, offs, o
         for a in range(PASSES):
             wt_raw[0, a] = load_rows(wt, a, slice(0, CHUNK), "wt_raw_0_%d" % a)
 
+
+        word_window = keep.tile([P, T], U32, name="word_window", align_bytes=64)
+        nc.sync.dma_start(out=word_window[:].bitcast(I32), in_=tab_words[0].rearrange("p t z -> p (t z)").bitcast(I32))
+
         zero = keep.tile([P, 1], F32, name="zero")
-        nc.gpsimd.memset(zero[:], 0.0)
+        nc.vector.memset(zero[:], 0.0)
         warm = keep.tile([P, 1], F32, name="warm")
         nc.scalar.activation(out=warm[:], in_=zero[:], func=SILU)
+
+        bias_rows = keep.tile([P, P], F32, name="bias_rows")
+        nc.vector.memset(bias_rows[:], 0.0)
+        nc.scalar.dma_start(out=bias_rows[0 : N // P, :], in_=b.rearrange("(c p) -> c p", p=P))
 
         row_gap = keep.tile([P, K_PASS], I32, name="row_gap")
         nc.gpsimd.iota(row_gap[:], pattern=[[1, K_PASS]], base=0, channel_multiplier=-PACK)
@@ -97,11 +105,30 @@ def tile_list_tiert_silu_kernel(tc, tab_words, tab_scales, wt, x, wx, b, offs, o
         ident_codes, ident_scales = operand(K_PASS, "ident")
         quantize(ones[:].rearrange("p t w -> p (t w)"), ident_codes[:], ident_scales[:])
 
+        for i in range(WARM):
+            idle = back_pool.tile([P, PACK, P], F32, name="back")
+            nc.tensor.matmul_mx(
+                out=idle[:].rearrange("p t w -> p (t w)"),
+                lhsT=ident_codes[:, 0:P].bitcast(FP8X4),
+                lhsT_scale=ident_scales[:, 0:P],
+                rhs=ident_codes[:].bitcast(FP8X4),
+                rhs_scale=ident_scales[:],
+                start=True,
+                stop=True,
+            )
+
+        unit = keep.tile([P, P], F32, name="unit")
+        make_identity(nc, unit[:])
+        turned = back_pool.tile([P, PACK, P], F32, name="back")
+        nc.tensor.transpose(turned[:, 0, :], bias_rows[:], unit[:])
+        bias = keep.tile([P, N // P], F32, name="bias")
+        nc.scalar.copy(out=bias[:], in_=turned[:, 0, 0 : N // P])
+
         picked_scales = keep.tile([P, J], U8, name="picked_scales", align_bytes=64)
         nc.vector.tensor_copy(picked_scales[:], scale_window[:].indirect(offsets[:]))
         moved_scales = keep.tile([P, J], U8, name="moved_scales", align_bytes=64)
         nc.gpsimd.memset(moved_scales[:].bitcast(I32), 0)
-        nc.scalar.dma_start(
+        nc.sync.dma_start(
             out=moved_scales[0:SHIFT_ROWS, :].bitcast(I32),
             in_=picked_scales[SHIFT : SHIFT + SHIFT_ROWS, :].bitcast(I32),
         )
@@ -127,9 +154,9 @@ def tile_list_tiert_silu_kernel(tc, tab_words, tab_scales, wt, x, wx, b, offs, o
         def make_tiers(c, on_vector):
             for a in range(PASSES):
                 wq[c, a] = operand(CHUNK, "wq_%d_%d" % (c, a))
-                quantize(round_rows(wt_raw[c, a][:], on_vector)[:], wq[c, a][0][:], wq[c, a][1][:])
+                quantize(round_rows(wt_raw[c, a][:], on_vector[a])[:], wq[c, a][0][:], wq[c, a][1][:])
             for a in range(PASSES):
-                rest = stage.tile([P, CHUNK * PACK], BF16, name="rounded", align_bytes=64)
+                rest = stage.tile([P, CHUNK * PACK], BF16, name="rest", bufs=3, align_bytes=64)
                 for u in range(TILES):
                     cols = slice(u * P, (u + 1) * P)
                     back = back_pool.tile([P, PACK, P], F32, name="back")
@@ -155,20 +182,23 @@ def tile_list_tiert_silu_kernel(tc, tab_words, tab_scales, wt, x, wx, b, offs, o
         def make_wx(c, on_vector):
             for a in range(PASSES):
                 wxq[c, a] = operand(CHUNK, "wxq_%d_%d" % (c, a))
-                quantize(round_rows(wx_raw[c, a][:], on_vector)[:], wxq[c, a][0][:], wxq[c, a][1][:])
+                quantize(round_rows(wx_raw[c, a][:], on_vector[a])[:], wxq[c, a][0][:], wxq[c, a][1][:])
 
         def make_x(h, on_vector):
             for a in range(PASSES):
                 xq[h, a] = operand(HALF, "xq_%d_%d" % (h, a))
                 for s in range(HALF // CHUNK):
                     cols = slice(s * CHUNK, (s + 1) * CHUNK)
-                    quantize(round_rows(x_raw[h, a][:, :, cols], on_vector)[:], xq[h, a][0][:, cols], xq[h, a][1][:, cols])
+                    quantize(round_rows(x_raw[h, a][:, :, cols], on_vector[2 * a + s])[:], xq[h, a][0][:, cols], xq[h, a][1][:, cols])
 
         acc = {}
+        bank_of = {}
+        free_banks = ["acc_%d" % i for i in range(6)]
 
         def table_passes(c, u, h):
             cols = slice(u * P, (u + 1) * P)
-            acc[c, u, h] = acc_pool.tile([P, HALF], F32, name="acc")
+            bank_of[c, u, h] = free_banks.pop(0)
+            acc[c, u, h] = acc_pool.tile([P, HALF], F32, name=bank_of[c, u, h])
             for tier in (wq, wr):
                 for a in range(PASSES):
                     nc.tensor.matmul_mx(
@@ -193,6 +223,7 @@ def tile_list_tiert_silu_kernel(tc, tab_words, tab_scales, wt, x, wx, b, offs, o
                     start=False,
                     stop=(a == PASSES - 1),
                 )
+            free_banks.append(bank_of[c, u, h])
             n_tile = c * TILES + u
             result = keep.tile([P, HALF], F32, name="result_%d_%d" % (n_tile, h))
             nc.scalar.activation(out=result[:], in_=acc[c, u, h][:], func=SILU, bias=bias[:, n_tile : n_tile + 1])
@@ -206,16 +237,10 @@ def tile_list_tiert_silu_kernel(tc, tab_words, tab_scales, wt, x, wx, b, offs, o
             for a in range(PASSES):
                 x_raw[h, a] = load_rows(x, a, slice(h * HALF, (h + 1) * HALF), "x_raw_%d_%d" % (h, a))
 
-        bias = keep.tile([P, N // P], F32, name="bias")
-
-        def load_bias():
-            with nc.allow_non_contiguous_dma(reason="one bias value for each partition and output tile"):
-                nc.sync.dma_start(out=bias[:], in_=b.rearrange("(c p) -> p c", p=P))
 
         load_x(0)
-        load_bias()
-        load_chunk(wx, wx_raw, 0, "wx_raw")
         load_chunk(wt, wt_raw, 1, "wt_raw")
+        load_chunk(wx, wx_raw, 0, "wx_raw")
         load_chunk(wx, wx_raw, 1, "wx_raw")
         load_x(1)
         load_chunk(wt, wt_raw, 2, "wt_raw")
@@ -223,32 +248,32 @@ def tile_list_tiert_silu_kernel(tc, tab_words, tab_scales, wt, x, wx, b, offs, o
         load_chunk(wt, wt_raw, 3, "wt_raw")
         load_chunk(wx, wx_raw, 3, "wx_raw")
         gather_words(0)
-        make_tiers(0, False)
+        make_tiers(0, (False, False))
         table_passes(0, 0, 0)
         table_passes(0, 1, 0)
         gather_words(1)
         table_passes(0, 0, 1)
         table_passes(0, 1, 1)
-        make_x(0, False)
-        make_wx(0, False)
-        make_tiers(1, False)
-        finish(0, 0, 0)
-        finish(0, 1, 0)
+        make_x(0, (False, False, False, False))
+        make_tiers(1, (False, False))
         table_passes(1, 0, 0)
         table_passes(1, 1, 0)
+        make_wx(0, (False, False))
+        finish(0, 0, 0)
+        finish(0, 1, 0)
         table_passes(1, 0, 1)
         table_passes(1, 1, 1)
-        make_wx(1, False)
+        make_wx(1, (False, False))
         finish(1, 0, 0)
         finish(1, 1, 0)
-        make_x(1, True)
-        make_tiers(2, False)
+        make_x(1, (True, True, True, True))
+        make_tiers(2, (True, True))
         finish(0, 0, 1)
         finish(0, 1, 1)
         finish(1, 0, 1)
         finish(1, 1, 1)
-        make_wx(2, False)
-        make_tiers(3, False)
+        make_wx(2, (False, False))
+        make_tiers(3, (False, False))
         table_passes(2, 0, 0)
         finish(2, 0, 0)
         table_passes(2, 0, 1)
@@ -257,7 +282,7 @@ def tile_list_tiert_silu_kernel(tc, tab_words, tab_scales, wt, x, wx, b, offs, o
         finish(2, 1, 0)
         table_passes(2, 1, 1)
         finish(2, 1, 1)
-        make_wx(3, False)
+        make_wx(3, (False, False))
         table_passes(3, 0, 0)
         finish(3, 0, 0)
         table_passes(3, 0, 1)

@@ -1,7 +1,6 @@
 from contextlib import ExitStack
 
 import concourse.mybir as mybir
-from concourse.masks import make_identity
 
 K, L, N, T, J = 1024, 1024, 1024, 2048, 1024
 FLOPS = 2 * N * J * (2 * K + L) + 2 * 512 * K * N
@@ -26,9 +25,25 @@ CHUNKS = N // CHUNK
 TILES = CHUNK // P
 HALF = 512
 HALVES = J // HALF
-PAIR = 2
+RUN = 4
+SUM_BANKS = 6
+BACK_BANKS = 2
+ROUND_BUFS = 12
+REST_BUFS = 4
+OPEN_ORDER = [(c, h) for h in range(HALVES) for c in range(CHUNKS)]
+CLOSE_ORDER = [(c, h) for h in range(HALVES) for c in range(CHUNKS)]
+ON_VECTOR = {("x",1,0),("x",1,1),("wt",2,0),("wt",2,1)}
+TABLE_AT = 2
+BIAS_AT = 1
 SHIFT = 16
-SHIFT_ROWS = 112
+SHIFT_ON_SYNC = True
+HOLD = ["picked_0", "picked_1"]
+LOADS = "wt_0 x_0 wt_1 wx_0 wx_1 x_1 wt_2 wx_2 wt_3 wx_3"
+WIDE = {}
+FULL = 7
+LOOK = 1
+AHEAD = 6
+STEPS = "pick_0 wt_0 open_0_0 pick_1 open_0_1 x_0 wt_1 open_1_0 wx_0 close_0_0 open_1_1 wx_1 close_1_0 x_1 wt_2 close_0_1 close_1_1 wx_2 wt_3 open_2_0_0 close_2_0_0 open_2_1_0 close_2_1_0 open_2_0_1 close_2_0_1 open_2_1_1 close_2_1_1 wx_3 open_3_0_0 close_3_0_0 open_3_1_0 close_3_1_0 open_3_0_1 close_3_0_1 open_3_1_1 close_3_1_1"
 WARM = 0
 
 
@@ -36,27 +51,100 @@ def tile_list_tiert_silu_kernel(tc, tab_words, tab_scales, wt, x, wx, b, offs, o
     nc = tc.nc
     with ExitStack() as ctx:
         keep = ctx.enter_context(tc.tile_pool(name="keep", bufs=1))
-        stage = ctx.enter_context(tc.tile_pool(name="stage", bufs=9))
-        acc_pool = ctx.enter_context(tc.psum_pool(name="acc", bufs=1))
-        back_pool = ctx.enter_context(tc.psum_pool(name="back", bufs=2))
+        stage = ctx.enter_context(tc.tile_pool(name="stage", bufs=ROUND_BUFS))
+        sum_pool = ctx.enter_context(tc.psum_pool(name="sums", bufs=1))
+        back_pool = ctx.enter_context(tc.psum_pool(name="back", bufs=BACK_BANKS))
 
-        def load_rows(src, a, cols, name):
-            raw = keep.tile([P, PACK, cols.stop - cols.start], F32, name=name)
-            nc.sync.dma_start(out=raw[:], in_=src[a * K_PASS : (a + 1) * K_PASS, cols].rearrange("(p t) w -> p t w", t=PACK))
-            return raw
+        ahead = AHEAD
+        opens = [(c, h, u) for c, h in OPEN_ORDER for u in range(TILES)]
+        closes = [(c, h, u) for c, h in CLOSE_ORDER for u in range(TILES)]
+        steps = []
+        sums_order = []
+        for s in range(len(opens) + ahead):
+            if s >= ahead:
+                sums_order.append(("close",) + closes[s - ahead])
+            if s < len(opens):
+                sums_order.append(("open",) + opens[s])
+        def needs(kind, c, h, u):
+            return [("pick", h), ("wt", c)] if kind == "open" else [("x", h), ("wx", c)]
+
+        for s, step in enumerate(sums_order):
+            steps.extend(needs(*step))
+            if step[0] == "close":
+                steps.append(step)
+            for later in sums_order[s + 1 : s + 1 + LOOK]:
+                steps.extend(needs(*later))
+            steps.append(step)
+        if STEPS:
+            steps = [(w.split("_")[0],) + tuple(int(z) for z in w.split("_")[1:]) for w in STEPS.split()]
+
+        offsets = keep.tile([P, J // 16], U16, name="offsets")
+        nc.sync.dma_start(offsets[:], offs)
+        scale_window = keep.tile([P, T], U8, name="scale_window", align_bytes=64)
+        nc.vector.memset(scale_window[:].bitcast(I32), 0)
+        bias_rows = keep.tile([P, P], F32, name="bias_rows")
+        nc.vector.memset(bias_rows[:], 0.0)
+        moved_scales = keep.tile([P, J], U8, name="moved_scales", align_bytes=64)
+        nc.vector.memset(moved_scales[:].bitcast(I32), 0)
+        word_window = keep.tile([P, T], U32, name="word_window", align_bytes=64)
+
+        def load_scales():
+            for r in range(4):
+                nc.scalar.dma_start(
+                    out=scale_window[r:P:SHIFT, :].bitcast(I32),
+                    in_=tab_scales[:, r:16:4, :].rearrange("a q t -> q a t").bitcast(I32),
+                )
+
+        picked_scales = keep.tile([P, J], U8, name="picked_scales", align_bytes=64)
+        tab_planes = [picked_scales, moved_scales]
+
+        def pick_scales():
+            nc.vector.tensor_copy(picked_scales[:], scale_window[:].indirect(offsets[:]))
+            nc.sync.dma_start(
+                out=moved_scales[0 : P - SHIFT, :].bitcast(I32),
+                in_=picked_scales[SHIFT:P, :].bitcast(I32),
+            )
+
+        def load_table():
+            nc.sync.dma_start(out=word_window[:].bitcast(I32), in_=tab_words[0].rearrange("p t z -> p (t z)").bitcast(I32))
+
+        sources = {"wt": (wt, CHUNK), "wx": (wx, CHUNK), "x": (x, HALF)}
+        raw = {}
+        loads = [(step[0], step[1], a) for step in steps if step[0] in sources for a in range(PASSES)]
+        if LOADS:
+            loads = [(w.split("_")[0], int(w.split("_")[1]), a) for w in LOADS.split() for a in range(PASSES)]
+        for place, (name, i, a) in enumerate(loads):
+            if place == 0:
+                load_scales()
+                pick_scales()
+            if place == TABLE_AT:
+                load_table()
+            if place == BIAS_AT:
+                nc.sync.dma_start(out=bias_rows[0 : N // P, :], in_=b.rearrange("(c p) -> c p", p=P))
+            if (name, i, a) in raw:
+                continue
+            src, width = sources[name]
+            count = WIDE.get((name, i), 1)
+            rows = keep.tile([P, PACK, count * width], F32, name="raw_%s_%d_%d" % (name, i, a), align_bytes=64)
+            nc.sync.dma_start(
+                out=rows[:],
+                in_=src[a * K_PASS : (a + 1) * K_PASS, i * width : (i + count) * width].rearrange("(p t) w -> p t w", t=PACK),
+            )
+            for k in range(count):
+                raw[name, i + k, a] = rows[:, :, k * width : (k + 1) * width]
 
         def woven(ap):
-            return ap.rearrange("p (c i t) -> p c t i", i=PAIR, t=PACK)
+            return ap.rearrange("p (c i t) -> p c t i", i=RUN, t=PACK)
 
-        def by_pairs(ap):
-            return ap.rearrange("p t (c i) -> p c t i", i=PAIR)
+        def by_runs(ap):
+            return ap.rearrange("p t (c i) -> p c t i", i=RUN)
 
         def round_rows(raw_ap, on_vector):
             rounded = stage.tile([P, CHUNK * PACK], BF16, name="rounded", align_bytes=64)
             if on_vector:
-                nc.vector.tensor_copy(out=woven(rounded[:]), in_=by_pairs(raw_ap))
+                nc.vector.tensor_copy(out=woven(rounded[:]), in_=by_runs(raw_ap))
             else:
-                nc.scalar.copy(out=woven(rounded[:]), in_=by_pairs(raw_ap))
+                nc.scalar.copy(out=woven(rounded[:]), in_=by_runs(raw_ap))
             return rounded
 
         def quantize(rounded_ap, codes_ap, scales_ap):
@@ -67,35 +155,10 @@ def tile_list_tiert_silu_kernel(tc, tab_words, tab_scales, wt, x, wx, b, offs, o
             scales = keep.tile([P, width], U8, name=name + "_scales", align_bytes=64)
             return codes, scales
 
-        offsets = keep.tile([P, J // 16], U16, name="offsets")
-        nc.sync.dma_start(offsets[:], offs)
-
-        scale_window = keep.tile([P, T], U8, name="scale_window", align_bytes=64)
-        nc.vector.memset(scale_window[:].bitcast(I32), 0)
-        for r in range(4):
-            nc.scalar.dma_start(
-                out=scale_window[r:P:SHIFT, :].bitcast(I32),
-                in_=tab_scales[:, r:16:4, :].rearrange("a q t -> q a t").bitcast(I32),
-            )
-
-        wt_raw = {}
-        wx_raw = {}
-        x_raw = {}
-        for a in range(PASSES):
-            wt_raw[0, a] = load_rows(wt, a, slice(0, CHUNK), "wt_raw_0_%d" % a)
-
-
-        word_window = keep.tile([P, T], U32, name="word_window", align_bytes=64)
-        nc.sync.dma_start(out=word_window[:].bitcast(I32), in_=tab_words[0].rearrange("p t z -> p (t z)").bitcast(I32))
-
         zero = keep.tile([P, 1], F32, name="zero")
         nc.vector.memset(zero[:], 0.0)
         warm = keep.tile([P, 1], F32, name="warm")
         nc.scalar.activation(out=warm[:], in_=zero[:], func=SILU)
-
-        bias_rows = keep.tile([P, P], F32, name="bias_rows")
-        nc.vector.memset(bias_rows[:], 0.0)
-        nc.scalar.dma_start(out=bias_rows[0 : N // P, :], in_=b.rearrange("(c p) -> c p", p=P))
 
         row_gap = keep.tile([P, K_PASS], I32, name="row_gap")
         nc.gpsimd.iota(row_gap[:], pattern=[[1, K_PASS]], base=0, channel_multiplier=-PACK)
@@ -118,45 +181,40 @@ def tile_list_tiert_silu_kernel(tc, tab_words, tab_scales, wt, x, wx, b, offs, o
             )
 
         unit = keep.tile([P, P], F32, name="unit")
-        make_identity(nc, unit[:])
+        nc.vector.tensor_scalar(out=unit[:], in0=row_gap[:, 0:K_PASS:PACK], scalar1=0.0, scalar2=None, op0=ALU.is_equal)
         turned = back_pool.tile([P, PACK, P], F32, name="back")
         nc.tensor.transpose(turned[:, 0, :], bias_rows[:], unit[:])
         bias = keep.tile([P, N // P], F32, name="bias")
         nc.scalar.copy(out=bias[:], in_=turned[:, 0, 0 : N // P])
 
-        picked_scales = keep.tile([P, J], U8, name="picked_scales", align_bytes=64)
-        nc.vector.tensor_copy(picked_scales[:], scale_window[:].indirect(offsets[:]))
-        moved_scales = keep.tile([P, J], U8, name="moved_scales", align_bytes=64)
-        nc.gpsimd.memset(moved_scales[:].bitcast(I32), 0)
-        nc.sync.dma_start(
-            out=moved_scales[0:SHIFT_ROWS, :].bitcast(I32),
-            in_=picked_scales[SHIFT : SHIFT + SHIFT_ROWS, :].bitcast(I32),
-        )
-        tab_planes = [picked_scales, moved_scales]
-
         tab_codes = {}
 
-        def gather_words(h):
-            picked = keep.tile([P, HALF], U32, name="picked_%d" % h, align_bytes=64)
-            nc.vector.tensor_copy(picked[:], word_window[:].indirect(offsets[:, h * HALF // 16 : (h + 1) * HALF // 16]))
-            parted = keep.tile([P, PASSES, 2 * HALF], U8, name="parted_%d" % h, align_bytes=64)
+        def pick(h):
+            entries = offsets[:, h * HALF // 16 : (h + 1) * HALF // 16]
+            picked = keep.tile([P, HALF], U32, name="picked_%d" % h, tag=HOLD[h], align_bytes=64)
+            nc.vector.tensor_copy(picked[:], word_window[:].indirect(entries))
+            tab_codes[h] = keep.tile([P, PASSES, 2 * HALF], U8, name="parted_%d" % h, align_bytes=64)
             nc.vector.tensor_copy(
-                out=parted[:].bitcast(U16),
+                out=tab_codes[h][:].bitcast(U16),
                 in_=picked[:].bitcast(U16).rearrange("p (s d) -> p d s", d=PASSES),
             )
-            tab_codes[h] = parted
 
-        wq = {}
-        wr = {}
-        wxq = {}
-        xq = {}
+        quantized = {}
 
-        def make_tiers(c, on_vector):
+        def make_operand(name, i):
+            width = sources[name][1]
             for a in range(PASSES):
-                wq[c, a] = operand(CHUNK, "wq_%d_%d" % (c, a))
-                quantize(round_rows(wt_raw[c, a][:], on_vector[a])[:], wq[c, a][0][:], wq[c, a][1][:])
+                codes, scales = operand(width, "%s_%d_%d" % (name, i, a))
+                quantized[name, i, a] = codes, scales
+                for s in range(width // CHUNK):
+                    cols = slice(s * CHUNK, (s + 1) * CHUNK)
+                    rounded = round_rows(raw[name, i, a][:, :, cols], (name, i, a) in ON_VECTOR or (name, i, a, s) in ON_VECTOR)
+                    quantize(rounded[:], codes[:, cols], scales[:, cols])
+
+        def make_rest(c):
             for a in range(PASSES):
-                rest = stage.tile([P, CHUNK * PACK], BF16, name="rest", bufs=3, align_bytes=64)
+                rest = stage.tile([P, CHUNK * PACK], BF16, name="rest", bufs=REST_BUFS, align_bytes=64)
+                codes, scales = quantized["wt", c, a]
                 for u in range(TILES):
                     cols = slice(u * P, (u + 1) * P)
                     back = back_pool.tile([P, PACK, P], F32, name="back")
@@ -165,129 +223,72 @@ def tile_list_tiert_silu_kernel(tc, tab_words, tab_scales, wt, x, wx, b, offs, o
                             out=back[:, t, :],
                             lhsT=ident_codes[:, t * P : (t + 1) * P].bitcast(FP8X4),
                             lhsT_scale=ident_scales[:, t * P : (t + 1) * P],
-                            rhs=wq[c, a][0][:, cols].bitcast(FP8X4),
-                            rhs_scale=wq[c, a][1][:, cols],
+                            rhs=codes[:, cols].bitcast(FP8X4),
+                            rhs_scale=scales[:, cols],
                             start=True,
                             stop=True,
                         )
                     nc.vector.tensor_tensor(
                         out=woven(rest[:, u * P * PACK : (u + 1) * P * PACK]),
-                        in0=by_pairs(wt_raw[c, a][:, :, cols]),
-                        in1=by_pairs(back[:]),
+                        in0=by_runs(raw["wt", c, a][:, :, cols]),
+                        in1=by_runs(back[:]),
                         op=ALU.subtract,
                     )
-                wr[c, a] = operand(CHUNK, "wr_%d_%d" % (c, a))
-                quantize(rest[:], wr[c, a][0][:], wr[c, a][1][:])
+                quantized["rest", c, a] = operand(CHUNK, "rest_%d_%d" % (c, a))
+                quantize(rest[:], quantized["rest", c, a][0][:], quantized["rest", c, a][1][:])
 
-        def make_wx(c, on_vector):
-            for a in range(PASSES):
-                wxq[c, a] = operand(CHUNK, "wxq_%d_%d" % (c, a))
-                quantize(round_rows(wx_raw[c, a][:], on_vector[a])[:], wxq[c, a][0][:], wxq[c, a][1][:])
+        sums = {}
+        results = {}
+        free_banks = ["sum_%d" % i for i in range(SUM_BANKS)]
 
-        def make_x(h, on_vector):
-            for a in range(PASSES):
-                xq[h, a] = operand(HALF, "xq_%d_%d" % (h, a))
-                for s in range(HALF // CHUNK):
-                    cols = slice(s * CHUNK, (s + 1) * CHUNK)
-                    quantize(round_rows(x_raw[h, a][:, :, cols], on_vector[2 * a + s])[:], xq[h, a][0][:, cols], xq[h, a][1][:, cols])
-
-        acc = {}
-        bank_of = {}
-        free_banks = ["acc_%d" % i for i in range(6)]
-
-        def table_passes(c, u, h):
+        def add_pass(acc, weights, u, rhs, rhs_scale, start, stop):
             cols = slice(u * P, (u + 1) * P)
-            bank_of[c, u, h] = free_banks.pop(0)
-            acc[c, u, h] = acc_pool.tile([P, HALF], F32, name=bank_of[c, u, h])
-            for tier in (wq, wr):
+            nc.tensor.matmul_mx(
+                out=acc[:],
+                lhsT=weights[0][:, cols].bitcast(FP8X4),
+                lhsT_scale=weights[1][:, cols],
+                rhs=rhs,
+                rhs_scale=rhs_scale,
+                start=start,
+                stop=stop,
+            )
+
+        def open_sums(c, h, *tiles):
+            for u in tiles or range(TILES):
+                bank = free_banks.pop(0)
+                acc = sum_pool.tile([P, HALF], F32, name=bank)
+                sums[c, h, u] = bank, acc
+                for tier in ("wt", "rest"):
+                    for a in range(PASSES):
+                        rhs = tab_codes[h][:, a, :].bitcast(FP4X4)
+                        add_pass(acc, quantized[tier, c, a], u, rhs, tab_planes[a][:, h * HALF : (h + 1) * HALF], tier == "wt" and a == 0, False)
+
+        def close_sums(c, h, *tiles):
+            for u in tiles or range(TILES):
+                bank, acc = sums[c, h, u]
                 for a in range(PASSES):
-                    nc.tensor.matmul_mx(
-                        out=acc[c, u, h][:],
-                        lhsT=tier[c, a][0][:, cols].bitcast(FP8X4),
-                        lhsT_scale=tier[c, a][1][:, cols],
-                        rhs=tab_codes[h][:, a, :].bitcast(FP4X4),
-                        rhs_scale=tab_planes[a][:, h * HALF : (h + 1) * HALF],
-                        start=(tier is wq and a == 0),
-                        stop=False,
-                    )
+                    codes, scales = quantized["x", h, a]
+                    add_pass(acc, quantized["wx", c, a], u, codes[:].bitcast(FP8X4), scales[:], False, a == PASSES - 1)
+                free_banks.append(bank)
+                n_tile = c * TILES + u
+                if n_tile not in results:
+                    results[n_tile] = keep.tile([P, J], F32, name="result_%d" % n_tile)
+                result = results[n_tile]
+                cols = slice(h * HALF, (h + 1) * HALF)
+                nc.scalar.activation(out=result[:, cols], in_=acc[:], func=SILU, bias=bias[:, n_tile : n_tile + 1])
+                if n_tile >= FULL:
+                    nc.sync.dma_start(out=out[n_tile * P : (n_tile + 1) * P, cols], in_=result[:, cols])
+                elif h == HALVES - 1:
+                    nc.sync.dma_start(out=out[n_tile * P : (n_tile + 1) * P, :], in_=result[:])
 
-        def finish(c, u, h):
-            cols = slice(u * P, (u + 1) * P)
-            for a in range(PASSES):
-                nc.tensor.matmul_mx(
-                    out=acc[c, u, h][:],
-                    lhsT=wxq[c, a][0][:, cols].bitcast(FP8X4),
-                    lhsT_scale=wxq[c, a][1][:, cols],
-                    rhs=xq[h, a][0][:].bitcast(FP8X4),
-                    rhs_scale=xq[h, a][1][:],
-                    start=False,
-                    stop=(a == PASSES - 1),
-                )
-            free_banks.append(bank_of[c, u, h])
-            n_tile = c * TILES + u
-            result = keep.tile([P, HALF], F32, name="result_%d_%d" % (n_tile, h))
-            nc.scalar.activation(out=result[:], in_=acc[c, u, h][:], func=SILU, bias=bias[:, n_tile : n_tile + 1])
-            nc.sync.dma_start(out=out[n_tile * P : (n_tile + 1) * P, h * HALF : (h + 1) * HALF], in_=result[:])
-
-        def load_chunk(src, raws, c, name):
-            for a in range(PASSES):
-                raws[c, a] = load_rows(src, a, slice(c * CHUNK, (c + 1) * CHUNK), "%s_%d_%d" % (name, c, a))
-
-        def load_x(h):
-            for a in range(PASSES):
-                x_raw[h, a] = load_rows(x, a, slice(h * HALF, (h + 1) * HALF), "x_raw_%d_%d" % (h, a))
-
-
-        load_x(0)
-        load_chunk(wt, wt_raw, 1, "wt_raw")
-        load_chunk(wx, wx_raw, 0, "wx_raw")
-        load_chunk(wx, wx_raw, 1, "wx_raw")
-        load_x(1)
-        load_chunk(wt, wt_raw, 2, "wt_raw")
-        load_chunk(wx, wx_raw, 2, "wx_raw")
-        load_chunk(wt, wt_raw, 3, "wt_raw")
-        load_chunk(wx, wx_raw, 3, "wx_raw")
-        gather_words(0)
-        make_tiers(0, (False, False))
-        table_passes(0, 0, 0)
-        table_passes(0, 1, 0)
-        gather_words(1)
-        table_passes(0, 0, 1)
-        table_passes(0, 1, 1)
-        make_x(0, (False, False, False, False))
-        make_tiers(1, (False, False))
-        table_passes(1, 0, 0)
-        table_passes(1, 1, 0)
-        make_wx(0, (False, False))
-        finish(0, 0, 0)
-        finish(0, 1, 0)
-        table_passes(1, 0, 1)
-        table_passes(1, 1, 1)
-        make_wx(1, (False, False))
-        finish(1, 0, 0)
-        finish(1, 1, 0)
-        make_x(1, (True, True, True, True))
-        make_tiers(2, (True, True))
-        finish(0, 0, 1)
-        finish(0, 1, 1)
-        finish(1, 0, 1)
-        finish(1, 1, 1)
-        make_wx(2, (False, False))
-        make_tiers(3, (False, False))
-        table_passes(2, 0, 0)
-        finish(2, 0, 0)
-        table_passes(2, 0, 1)
-        finish(2, 0, 1)
-        table_passes(2, 1, 0)
-        finish(2, 1, 0)
-        table_passes(2, 1, 1)
-        finish(2, 1, 1)
-        make_wx(3, (False, False))
-        table_passes(3, 0, 0)
-        finish(3, 0, 0)
-        table_passes(3, 0, 1)
-        finish(3, 0, 1)
-        table_passes(3, 1, 0)
-        finish(3, 1, 0)
-        table_passes(3, 1, 1)
-        finish(3, 1, 1)
+        for step in steps:
+            if step[0] == "pick":
+                pick(step[1])
+            elif step[0] == "open":
+                open_sums(*step[1:])
+            elif step[0] == "close":
+                close_sums(*step[1:])
+            else:
+                make_operand(step[0], step[1])
+                if step[0] == "wt":
+                    make_rest(step[1])

@@ -17,34 +17,22 @@ SILU = mybir.ActivationFunctionType.Silu
 ALU = mybir.AluOpType
 
 P = 128
+QUAD = 32
 PACK = 4
 K_PASS = P * PACK
 PASSES = K // K_PASS
+WIDTH = 512
 CHUNK = 256
-CHUNKS = N // CHUNK
+CHUNKS = WIDTH // CHUNK
 TILES = CHUNK // P
-HALF = 512
-HALVES = J // HALF
 RUN = 4
+LIST_ROWS = 16
+PASS_GAP = 16
 SUM_BANKS = 6
 BACK_BANKS = 2
 ROUND_BUFS = 12
 REST_BUFS = 4
-OPEN_ORDER = [(c, h) for h in range(HALVES) for c in range(CHUNKS)]
-CLOSE_ORDER = [(c, h) for h in range(HALVES) for c in range(CHUNKS)]
-ON_VECTOR = {("x",1,0),("x",1,1),("wt",2,0),("wt",2,1)}
-TABLE_AT = 2
-BIAS_AT = 1
-SHIFT = 16
-SHIFT_ON_SYNC = True
-HOLD = ["picked_0", "picked_1"]
-LOADS = "wt_0 x_0 wt_1 wx_0 wx_1 x_1 wt_2 wx_2 wt_3 wx_3"
-WIDE = {}
-FULL = 7
-LOOK = 1
-AHEAD = 6
-STEPS = "pick_0 wt_0 open_0_0 pick_1 open_0_1 x_0 wt_1 open_1_0 wx_0 close_0_0 open_1_1 wx_1 close_1_0 x_1 wt_2 close_0_1 close_1_1 wx_2 wt_3 open_2_0_0 close_2_0_0 open_2_1_0 close_2_1_0 open_2_0_1 close_2_0_1 open_2_1_1 close_2_1_1 wx_3 open_3_0_0 close_3_0_0 open_3_1_0 close_3_1_0 open_3_0_1 close_3_0_1 open_3_1_1 close_3_1_1"
-WARM = 0
+ROUNDED_BY_VECTOR = (("x", 1, 0), ("x", 1, 1), ("wt", 1, 0))
 
 
 def tile_list_tiert_silu_kernel(tc, tab_words, tab_scales, wt, x, wx, b, offs, out):
@@ -55,83 +43,92 @@ def tile_list_tiert_silu_kernel(tc, tab_words, tab_scales, wt, x, wx, b, offs, o
         sum_pool = ctx.enter_context(tc.psum_pool(name="sums", bufs=1))
         back_pool = ctx.enter_context(tc.psum_pool(name="back", bufs=BACK_BANKS))
 
-        ahead = AHEAD
-        opens = [(c, h, u) for c, h in OPEN_ORDER for u in range(TILES)]
-        closes = [(c, h, u) for c, h in CLOSE_ORDER for u in range(TILES)]
-        steps = []
-        sums_order = []
-        for s in range(len(opens) + ahead):
-            if s >= ahead:
-                sums_order.append(("close",) + closes[s - ahead])
-            if s < len(opens):
-                sums_order.append(("open",) + opens[s])
-        def needs(kind, c, h, u):
-            return [("pick", h), ("wt", c)] if kind == "open" else [("x", h), ("wx", c)]
+        def quantize(rounded, name):
+            width = rounded.shape[1] // PACK
+            codes = keep.tile([P, width], U32, name=name + "_codes", align_bytes=64)
+            scales = keep.tile([P, width], U8, name=name + "_scales", align_bytes=64)
+            nc.vector.quantize_mx(out=codes[:].bitcast(FP8X4), scales=scales[:], in_=rounded)
+            return codes, scales
 
-        for s, step in enumerate(sums_order):
-            steps.extend(needs(*step))
-            if step[0] == "close":
-                steps.append(step)
-            for later in sums_order[s + 1 : s + 1 + LOOK]:
-                steps.extend(needs(*later))
-            steps.append(step)
-        if STEPS:
-            steps = [(w.split("_")[0],) + tuple(int(z) for z in w.split("_")[1:]) for w in STEPS.split()]
-
-        offsets = keep.tile([P, J // 16], U16, name="offsets")
+        offsets = keep.tile([P, J // LIST_ROWS], U16, name="offsets")
         nc.sync.dma_start(offsets[:], offs)
+
         scale_window = keep.tile([P, T], U8, name="scale_window", align_bytes=64)
         nc.vector.memset(scale_window[:].bitcast(I32), 0)
         bias_rows = keep.tile([P, P], F32, name="bias_rows")
         nc.vector.memset(bias_rows[:], 0.0)
         moved_scales = keep.tile([P, J], U8, name="moved_scales", align_bytes=64)
         nc.vector.memset(moved_scales[:].bitcast(I32), 0)
-        word_window = keep.tile([P, T], U32, name="word_window", align_bytes=64)
 
-        def load_scales():
-            for r in range(4):
-                nc.scalar.dma_start(
-                    out=scale_window[r:P:SHIFT, :].bitcast(I32),
-                    in_=tab_scales[:, r:16:4, :].rearrange("a q t -> q a t").bitcast(I32),
-                )
+        zero = keep.tile([P, 1], F32, name="zero")
+        nc.vector.memset(zero[:], 0.0)
+        warm = keep.tile([P, 1], F32, name="warm")
+        nc.scalar.activation(out=warm[:], in_=zero[:], func=SILU)
+
+        step = keep.tile([P, 40], F32, name="step")
+        nc.vector.memset(step[:], 1.0)
+        count = keep.tile([P, 40], F32, name="count", align_bytes=64)
+        nc.vector.tensor_tensor_scan(count[:], step[:], step[:], -9.0, ALU.mult, ALU.add)
+        count_down = keep.tile([P, QUAD], F32, name="count_down", align_bytes=64)
+        nc.vector.transpose(count_down[:], count[:, 0:QUAD])
+        column = keep.tile([P, K_PASS], BF16, name="column", align_bytes=64)
+        nc.vector.scalar_tensor_tensor(
+            out=column[:].rearrange("p (u z) -> p u z", z=QUAD),
+            in0=count[:, 0:16].unsqueeze(2).to_broadcast([P, 16, QUAD]),
+            scalar=32.0,
+            in1=count[:, 8:40].unsqueeze(1).to_broadcast([P, 16, QUAD]),
+            op0=ALU.mult,
+            op1=ALU.add,
+        )
+        first_row = keep.tile([P, 1], F32, name="first_row")
+        for q in range(P // QUAD):
+            rows = slice(QUAD * q, QUAD * (q + 1))
+            nc.vector.tensor_scalar(
+                out=first_row[rows, :], in0=count_down[rows, 0:1], scalar1=4.0, scalar2=128.0 * q - 224.0, op0=ALU.mult, op1=ALU.add
+            )
+        ones = keep.tile([P, PACK, K_PASS], BF16, name="ones", align_bytes=64)
+        for t in range(PACK):
+            nc.vector.tensor_scalar(
+                out=ones[:, t, :], in0=column[:], scalar1=first_row[:], scalar2=float(t), op0=ALU.subtract, op1=ALU.is_equal
+            )
+        ident_codes, ident_scales = quantize(ones[:].rearrange("p t w -> p (t w)"), "ident")
+        unit = keep.tile([P, P], F32, name="unit")
+        nc.vector.tensor_scalar(
+            out=unit[:], in0=column[:, 0:K_PASS:PACK], scalar1=first_row[:], scalar2=0.0, op0=ALU.subtract, op1=ALU.is_equal
+        )
+
+        inputs = {"wt": wt, "wx": wx, "x": x}
+        raw = {}
+
+        def load(name, i, a):
+            raw[name, i, a] = keep.tile([P, PACK, WIDTH], F32, name="raw_%s_%d_%d" % (name, i, a), align_bytes=64)
+            rows = inputs[name][a * K_PASS : (a + 1) * K_PASS, i * WIDTH : (i + 1) * WIDTH]
+            nc.sync.dma_start(out=raw[name, i, a][:], in_=rows.rearrange("(p t) w -> p t w", t=PACK))
+
+        for r in range(4):
+            nc.sync.dma_start(
+                out=scale_window[r:P:PASS_GAP, :].bitcast(I32),
+                in_=tab_scales[:, r:16:4, :].rearrange("a q t -> q a t").bitcast(I32),
+            )
+        word_window = keep.tile([P, T], U32, name="word_window", align_bytes=64)
+        nc.sync.dma_start(out=word_window[:].bitcast(I32), in_=tab_words[0].rearrange("p t z -> p (t z)").bitcast(I32))
+        load("wt", 0, 0)
+        nc.sync.dma_start(out=bias_rows[0 : N // P, :], in_=b.rearrange("(c p) -> c p", p=P))
+        load("wt", 0, 1)
 
         picked_scales = keep.tile([P, J], U8, name="picked_scales", align_bytes=64)
-        tab_planes = [picked_scales, moved_scales]
+        nc.vector.tensor_copy(picked_scales[:], scale_window[:].indirect(offsets[:]))
+        nc.sync.dma_start(out=moved_scales[0 : P - PASS_GAP, :].bitcast(I32), in_=picked_scales[PASS_GAP:P, :].bitcast(I32))
+        tab_planes = (picked_scales, moved_scales)
 
-        def pick_scales():
-            nc.vector.tensor_copy(picked_scales[:], scale_window[:].indirect(offsets[:]))
-            nc.sync.dma_start(
-                out=moved_scales[0 : P - SHIFT, :].bitcast(I32),
-                in_=picked_scales[SHIFT:P, :].bitcast(I32),
-            )
+        for name, i in (("x", 0), ("wx", 0), ("x", 1), ("wt", 1), ("wx", 1)):
+            for a in range(PASSES):
+                load(name, i, a)
 
-        def load_table():
-            nc.sync.dma_start(out=word_window[:].bitcast(I32), in_=tab_words[0].rearrange("p t z -> p (t z)").bitcast(I32))
-
-        sources = {"wt": (wt, CHUNK), "wx": (wx, CHUNK), "x": (x, HALF)}
-        raw = {}
-        loads = [(step[0], step[1], a) for step in steps if step[0] in sources for a in range(PASSES)]
-        if LOADS:
-            loads = [(w.split("_")[0], int(w.split("_")[1]), a) for w in LOADS.split() for a in range(PASSES)]
-        for place, (name, i, a) in enumerate(loads):
-            if place == 0:
-                load_scales()
-                pick_scales()
-            if place == TABLE_AT:
-                load_table()
-            if place == BIAS_AT:
-                nc.sync.dma_start(out=bias_rows[0 : N // P, :], in_=b.rearrange("(c p) -> c p", p=P))
-            if (name, i, a) in raw:
-                continue
-            src, width = sources[name]
-            count = WIDE.get((name, i), 1)
-            rows = keep.tile([P, PACK, count * width], F32, name="raw_%s_%d_%d" % (name, i, a), align_bytes=64)
-            nc.sync.dma_start(
-                out=rows[:],
-                in_=src[a * K_PASS : (a + 1) * K_PASS, i * width : (i + count) * width].rearrange("(p t) w -> p t w", t=PACK),
-            )
-            for k in range(count):
-                raw[name, i + k, a] = rows[:, :, k * width : (k + 1) * width]
+        turned = back_pool.tile([P, PACK, P], F32, name="back")
+        nc.tensor.transpose(turned[:, 0, :], bias_rows[:], unit[:])
+        bias = keep.tile([P, N // P], F32, name="bias")
+        nc.scalar.copy(out=bias[:], in_=turned[:, 0, 0 : N // P])
 
         def woven(ap):
             return ap.rearrange("p (c i t) -> p c t i", i=RUN, t=PACK)
@@ -139,156 +136,141 @@ def tile_list_tiert_silu_kernel(tc, tab_words, tab_scales, wt, x, wx, b, offs, o
         def by_runs(ap):
             return ap.rearrange("p t (c i) -> p c t i", i=RUN)
 
-        def round_rows(raw_ap, on_vector):
-            rounded = stage.tile([P, CHUNK * PACK], BF16, name="rounded", align_bytes=64)
-            if on_vector:
-                nc.vector.tensor_copy(out=woven(rounded[:]), in_=by_runs(raw_ap))
-            else:
-                nc.scalar.copy(out=woven(rounded[:]), in_=by_runs(raw_ap))
-            return rounded
-
-        def quantize(rounded_ap, codes_ap, scales_ap):
-            nc.vector.quantize_mx(out=codes_ap.bitcast(FP8X4), scales=scales_ap, in_=rounded_ap)
-
-        def operand(width, name):
-            codes = keep.tile([P, width], U32, name=name + "_codes", align_bytes=64)
-            scales = keep.tile([P, width], U8, name=name + "_scales", align_bytes=64)
-            return codes, scales
-
-        zero = keep.tile([P, 1], F32, name="zero")
-        nc.vector.memset(zero[:], 0.0)
-        warm = keep.tile([P, 1], F32, name="warm")
-        nc.scalar.activation(out=warm[:], in_=zero[:], func=SILU)
-
-        row_gap = keep.tile([P, K_PASS], I32, name="row_gap")
-        nc.gpsimd.iota(row_gap[:], pattern=[[1, K_PASS]], base=0, channel_multiplier=-PACK)
-        ones = keep.tile([P, PACK, K_PASS], BF16, name="ones", align_bytes=64)
-        for t in range(PACK):
-            nc.vector.tensor_scalar(out=ones[:, t, :], in0=row_gap[:], scalar1=float(t), scalar2=None, op0=ALU.is_equal)
-        ident_codes, ident_scales = operand(K_PASS, "ident")
-        quantize(ones[:].rearrange("p t w -> p (t w)"), ident_codes[:], ident_scales[:])
-
-        for i in range(WARM):
-            idle = back_pool.tile([P, PACK, P], F32, name="back")
-            nc.tensor.matmul_mx(
-                out=idle[:].rearrange("p t w -> p (t w)"),
-                lhsT=ident_codes[:, 0:P].bitcast(FP8X4),
-                lhsT_scale=ident_scales[:, 0:P],
-                rhs=ident_codes[:].bitcast(FP8X4),
-                rhs_scale=ident_scales[:],
-                start=True,
-                stop=True,
-            )
-
-        unit = keep.tile([P, P], F32, name="unit")
-        nc.vector.tensor_scalar(out=unit[:], in0=row_gap[:, 0:K_PASS:PACK], scalar1=0.0, scalar2=None, op0=ALU.is_equal)
-        turned = back_pool.tile([P, PACK, P], F32, name="back")
-        nc.tensor.transpose(turned[:, 0, :], bias_rows[:], unit[:])
-        bias = keep.tile([P, N // P], F32, name="bias")
-        nc.scalar.copy(out=bias[:], in_=turned[:, 0, 0 : N // P])
-
         tab_codes = {}
 
-        def pick(h):
-            entries = offsets[:, h * HALF // 16 : (h + 1) * HALF // 16]
-            picked = keep.tile([P, HALF], U32, name="picked_%d" % h, tag=HOLD[h], align_bytes=64)
+        def pick_words(h, tenant_of):
+            picked = keep.tile([P, WIDTH], U32, name="picked_%d" % h, tag=tenant_of, align_bytes=64)
+            entries = offsets[:, h * WIDTH // LIST_ROWS : (h + 1) * WIDTH // LIST_ROWS]
             nc.vector.tensor_copy(picked[:], word_window[:].indirect(entries))
-            tab_codes[h] = keep.tile([P, PASSES, 2 * HALF], U8, name="parted_%d" % h, align_bytes=64)
+            tab_codes[h] = keep.tile([P, PASSES, 2 * WIDTH], U8, name="parted_%d" % h, align_bytes=64)
             nc.vector.tensor_copy(
                 out=tab_codes[h][:].bitcast(U16),
-                in_=picked[:].bitcast(U16).rearrange("p (s d) -> p d s", d=PASSES),
+                in_=picked[:].bitcast(U16).rearrange("p (s a) -> p a s", a=PASSES),
             )
 
-        quantized = {}
+        def rounded_chunk(name, i, a, s):
+            rounded = stage.tile([P, CHUNK * PACK], BF16, name="rounded", align_bytes=64)
+            source = by_runs(raw[name, i, a][:, :, s * CHUNK : (s + 1) * CHUNK])
+            if (name, i, a) in ROUNDED_BY_VECTOR:
+                nc.vector.tensor_copy(out=woven(rounded[:]), in_=source)
+            else:
+                nc.scalar.copy(out=woven(rounded[:]), in_=source)
+            return rounded
 
-        def make_operand(name, i):
-            width = sources[name][1]
+        weights = {}
+        tokens = {}
+
+        def make_x(h):
             for a in range(PASSES):
-                codes, scales = operand(width, "%s_%d_%d" % (name, i, a))
-                quantized[name, i, a] = codes, scales
-                for s in range(width // CHUNK):
+                codes = keep.tile([P, WIDTH], U32, name="x_%d_%d_codes" % (h, a), align_bytes=64)
+                scales = keep.tile([P, WIDTH], U8, name="x_%d_%d_scales" % (h, a), align_bytes=64)
+                tokens[h, a] = codes, scales
+                for s in range(CHUNKS):
                     cols = slice(s * CHUNK, (s + 1) * CHUNK)
-                    rounded = round_rows(raw[name, i, a][:, :, cols], (name, i, a) in ON_VECTOR or (name, i, a, s) in ON_VECTOR)
-                    quantize(rounded[:], codes[:, cols], scales[:, cols])
-
-        def make_rest(c):
-            for a in range(PASSES):
-                rest = stage.tile([P, CHUNK * PACK], BF16, name="rest", bufs=REST_BUFS, align_bytes=64)
-                codes, scales = quantized["wt", c, a]
-                for u in range(TILES):
-                    cols = slice(u * P, (u + 1) * P)
-                    back = back_pool.tile([P, PACK, P], F32, name="back")
-                    for t in range(PACK):
-                        nc.tensor.matmul_mx(
-                            out=back[:, t, :],
-                            lhsT=ident_codes[:, t * P : (t + 1) * P].bitcast(FP8X4),
-                            lhsT_scale=ident_scales[:, t * P : (t + 1) * P],
-                            rhs=codes[:, cols].bitcast(FP8X4),
-                            rhs_scale=scales[:, cols],
-                            start=True,
-                            stop=True,
-                        )
-                    nc.vector.tensor_tensor(
-                        out=woven(rest[:, u * P * PACK : (u + 1) * P * PACK]),
-                        in0=by_runs(raw["wt", c, a][:, :, cols]),
-                        in1=by_runs(back[:]),
-                        op=ALU.subtract,
+                    nc.vector.quantize_mx(
+                        out=codes[:, cols].bitcast(FP8X4), scales=scales[:, cols], in_=rounded_chunk("x", h, a, s)[:]
                     )
-                quantized["rest", c, a] = operand(CHUNK, "rest_%d_%d" % (c, a))
-                quantize(rest[:], quantized["rest", c, a][0][:], quantized["rest", c, a][1][:])
 
+        def make_wx(side):
+            for a in range(PASSES):
+                for s in range(CHUNKS):
+                    c = side * CHUNKS + s
+                    weights["wx", c, a] = quantize(rounded_chunk("wx", side, a, s)[:], "wx_%d_%d" % (c, a))
+
+        def make_tiers(side):
+            for a in range(PASSES):
+                for s in range(CHUNKS):
+                    c = side * CHUNKS + s
+                    codes, scales = quantize(rounded_chunk("wt", side, a, s)[:], "wq_%d_%d" % (c, a))
+                    weights["wq", c, a] = codes, scales
+                    rest = stage.tile([P, CHUNK * PACK], BF16, name="rest", bufs=REST_BUFS, align_bytes=64)
+                    for u in range(TILES):
+                        cols = slice(u * P, (u + 1) * P)
+                        back = back_pool.tile([P, PACK, P], F32, name="back")
+                        for t in range(PACK):
+                            nc.tensor.matmul_mx(
+                                out=back[:, t, :],
+                                lhsT=ident_codes[:, t * P : (t + 1) * P].bitcast(FP8X4),
+                                lhsT_scale=ident_scales[:, t * P : (t + 1) * P],
+                                rhs=codes[:, cols].bitcast(FP8X4),
+                                rhs_scale=scales[:, cols],
+                                start=True,
+                                stop=True,
+                            )
+                        nc.vector.tensor_tensor(
+                            out=woven(rest[:, u * P * PACK : (u + 1) * P * PACK]),
+                            in0=by_runs(raw["wt", side, a][:, :, s * CHUNK + u * P : s * CHUNK + (u + 1) * P]),
+                            in1=by_runs(back[:]),
+                            op=ALU.subtract,
+                        )
+                    weights["wr", c, a] = quantize(rest[:], "wr_%d_%d" % (c, a))
+
+        free_banks = ["sum_%d" % i for i in range(SUM_BANKS)]
         sums = {}
         results = {}
-        free_banks = ["sum_%d" % i for i in range(SUM_BANKS)]
 
-        def add_pass(acc, weights, u, rhs, rhs_scale, start, stop):
-            cols = slice(u * P, (u + 1) * P)
+        def add_pass(n, h, operand, a, rhs, rhs_scale, start, stop):
+            codes, scales = weights[operand, n // TILES, a]
+            cols = slice(n % TILES * P, (n % TILES + 1) * P)
             nc.tensor.matmul_mx(
-                out=acc[:],
-                lhsT=weights[0][:, cols].bitcast(FP8X4),
-                lhsT_scale=weights[1][:, cols],
+                out=sums[n, h][1][:],
+                lhsT=codes[:, cols].bitcast(FP8X4),
+                lhsT_scale=scales[:, cols],
                 rhs=rhs,
                 rhs_scale=rhs_scale,
                 start=start,
                 stop=stop,
             )
 
-        def open_sums(c, h, *tiles):
-            for u in tiles or range(TILES):
-                bank = free_banks.pop(0)
-                acc = sum_pool.tile([P, HALF], F32, name=bank)
-                sums[c, h, u] = bank, acc
-                for tier in ("wt", "rest"):
-                    for a in range(PASSES):
-                        rhs = tab_codes[h][:, a, :].bitcast(FP4X4)
-                        add_pass(acc, quantized[tier, c, a], u, rhs, tab_planes[a][:, h * HALF : (h + 1) * HALF], tier == "wt" and a == 0, False)
+        def open_sum(n, h):
+            bank = free_banks.pop(0)
+            sums[n, h] = bank, sum_pool.tile([P, WIDTH], F32, name=bank)
+            for a in range(PASSES):
+                for operand in ("wq", "wr"):
+                    rhs = tab_codes[h][:, a, :].bitcast(FP4X4)
+                    plane = tab_planes[a][:, h * WIDTH : (h + 1) * WIDTH]
+                    add_pass(n, h, operand, a, rhs, plane, start=(a == 0 and operand == "wq"), stop=False)
 
-        def close_sums(c, h, *tiles):
-            for u in tiles or range(TILES):
-                bank, acc = sums[c, h, u]
-                for a in range(PASSES):
-                    codes, scales = quantized["x", h, a]
-                    add_pass(acc, quantized["wx", c, a], u, codes[:].bitcast(FP8X4), scales[:], False, a == PASSES - 1)
-                free_banks.append(bank)
-                n_tile = c * TILES + u
-                if n_tile not in results:
-                    results[n_tile] = keep.tile([P, J], F32, name="result_%d" % n_tile)
-                result = results[n_tile]
-                cols = slice(h * HALF, (h + 1) * HALF)
-                nc.scalar.activation(out=result[:, cols], in_=acc[:], func=SILU, bias=bias[:, n_tile : n_tile + 1])
-                if n_tile >= FULL:
-                    nc.sync.dma_start(out=out[n_tile * P : (n_tile + 1) * P, cols], in_=result[:, cols])
-                elif h == HALVES - 1:
-                    nc.sync.dma_start(out=out[n_tile * P : (n_tile + 1) * P, :], in_=result[:])
+        def close_sum(n, h):
+            for a in range(PASSES):
+                codes, scales = tokens[h, a]
+                add_pass(n, h, "wx", a, codes[:].bitcast(FP8X4), scales[:], start=False, stop=(a == PASSES - 1))
+            bank, acc = sums[n, h]
+            free_banks.append(bank)
+            if h == 0:
+                results[n] = keep.tile([P, J], F32, name="result_%d" % n)
+            cols = slice(h * WIDTH, (h + 1) * WIDTH)
+            nc.scalar.activation(out=results[n][:, cols], in_=acc[:], func=SILU, bias=bias[:, n : n + 1])
+            if n == N // P - 1:
+                nc.sync.dma_start(out=out[n * P : (n + 1) * P, cols], in_=results[n][:, cols])
+            elif h == 1:
+                nc.sync.dma_start(out=out[n * P : (n + 1) * P, :], in_=results[n][:])
 
-        for step in steps:
-            if step[0] == "pick":
-                pick(step[1])
-            elif step[0] == "open":
-                open_sums(*step[1:])
-            elif step[0] == "close":
-                close_sums(*step[1:])
-            else:
-                make_operand(step[0], step[1])
-                if step[0] == "wt":
-                    make_rest(step[1])
+        side_tiles = WIDTH // P
+        spare = SUM_BANKS - side_tiles
+
+        pick_words(0, "picked_0")
+        make_tiers(0)
+        for n in range(side_tiles):
+            open_sum(n, 0)
+        pick_words(1, "raw_wt_0_0")
+        for n in range(spare):
+            open_sum(n, 1)
+        make_x(0)
+        make_wx(0)
+        for n in range(spare):
+            close_sum(n, 0)
+        for n in range(spare, side_tiles):
+            open_sum(n, 1)
+        for n in range(spare, side_tiles):
+            close_sum(n, 0)
+        make_x(1)
+        make_tiers(1)
+        for n in range(side_tiles):
+            close_sum(n, 1)
+
+        make_wx(1)
+        for n in range(side_tiles, N // P):
+            for h in range(J // WIDTH):
+                open_sum(n, h)
+                close_sum(n, h)

@@ -28,11 +28,13 @@ TILES = CHUNK // P
 RUN = 4
 LIST_ROWS = 16
 PASS_GAP = 16
-SUM_BANKS = 6
-BACK_BANKS = 2
 ROUND_BUFS = 12
 REST_BUFS = 4
-ROUNDED_BY_VECTOR = (("x", 1, 0), ("x", 1, 1), ("wt", 1, 0))
+LATER_LOADS = (
+    ("x", (0, 1), 0), ("wx", (0,), 0), ("x", (0, 1), 1), ("wx", (0,), 1),
+    ("wt", (1,), 0), ("wt", (1,), 1), ("wx", (1,), 0), ("wx", (1,), 1),
+)
+ROUNDED_BY_VECTOR = (("wx", 0, 0, 0), ("x", 1, 1, 0), ("x", 1, 1, 1), ("wx", 0, 1, 0), ("wt", 1, 0, 0), ("wt", 1, 0, 1), ("wx", 1, 1, 0))
 
 
 def tile_list_tiert_silu_kernel(tc, tab_words, tab_scales, wt, x, wx, b, offs, out):
@@ -40,8 +42,10 @@ def tile_list_tiert_silu_kernel(tc, tab_words, tab_scales, wt, x, wx, b, offs, o
     with ExitStack() as ctx:
         keep = ctx.enter_context(tc.tile_pool(name="keep", bufs=1))
         stage = ctx.enter_context(tc.tile_pool(name="stage", bufs=ROUND_BUFS))
-        sum_pool = ctx.enter_context(tc.psum_pool(name="sums", bufs=1))
-        back_pool = ctx.enter_context(tc.psum_pool(name="back", bufs=BACK_BANKS))
+        psum = ctx.enter_context(tc.psum_pool(name="psum", bufs=1))
+
+        def bank(i, shape):
+            return psum.tile(shape, F32, name="bank_%d" % i)
 
         def quantize(rounded, name):
             width = rounded.shape[1] // PACK
@@ -59,11 +63,6 @@ def tile_list_tiert_silu_kernel(tc, tab_words, tab_scales, wt, x, wx, b, offs, o
         nc.vector.memset(bias_rows[:], 0.0)
         moved_scales = keep.tile([P, J], U8, name="moved_scales", align_bytes=64)
         nc.vector.memset(moved_scales[:].bitcast(I32), 0)
-
-        zero = keep.tile([P, 1], F32, name="zero")
-        nc.vector.memset(zero[:], 0.0)
-        warm = keep.tile([P, 1], F32, name="warm")
-        nc.scalar.activation(out=warm[:], in_=zero[:], func=SILU)
 
         step = keep.tile([P, 40], F32, name="step")
         nc.vector.memset(step[:], 1.0)
@@ -100,32 +99,40 @@ def tile_list_tiert_silu_kernel(tc, tab_words, tab_scales, wt, x, wx, b, offs, o
         inputs = {"wt": wt, "wx": wx, "x": x}
         raw = {}
 
-        def load(name, i, a):
-            raw[name, i, a] = keep.tile([P, PACK, WIDTH], F32, name="raw_%s_%d_%d" % (name, i, a), align_bytes=64)
-            rows = inputs[name][a * K_PASS : (a + 1) * K_PASS, i * WIDTH : (i + 1) * WIDTH]
-            nc.sync.dma_start(out=raw[name, i, a][:], in_=rows.rearrange("(p t) w -> p t w", t=PACK))
+        def load(name, sides, a):
+            first, width = sides[0] * WIDTH, len(sides) * WIDTH
+            tile = keep.tile([P, PACK, width], F32, name="raw_%s_%d_%d" % (name, sides[0], a), align_bytes=64)
+            rows = inputs[name][a * K_PASS : (a + 1) * K_PASS, first : first + width]
+            nc.sync.dma_start(out=tile[:], in_=rows.rearrange("(p t) w -> p t w", t=PACK))
+            for i in sides:
+                raw[name, i, a] = tile[:, :, i * WIDTH - first : (i + 1) * WIDTH - first]
 
         for r in range(4):
-            nc.sync.dma_start(
+            nc.scalar.dma_start(
                 out=scale_window[r:P:PASS_GAP, :].bitcast(I32),
                 in_=tab_scales[:, r:16:4, :].rearrange("a q t -> q a t").bitcast(I32),
             )
         word_window = keep.tile([P, T], U32, name="word_window", align_bytes=64)
+        load("wt", (0,), 0)
         nc.sync.dma_start(out=word_window[:].bitcast(I32), in_=tab_words[0].rearrange("p t z -> p (t z)").bitcast(I32))
-        load("wt", 0, 0)
-        nc.sync.dma_start(out=bias_rows[0 : N // P, :], in_=b.rearrange("(c p) -> c p", p=P))
-        load("wt", 0, 1)
+        nc.scalar.dma_start(out=bias_rows[0 : N // P, :], in_=b.rearrange("(c p) -> c p", p=P))
+        load("wt", (0,), 1)
+
+        zero = keep.tile([P, 1], F32, name="zero")
+        nc.vector.memset(zero[:], 0.0)
+        warm = keep.tile([P, 1], F32, name="warm")
+        nc.scalar.activation(out=warm[:], in_=zero[:], func=SILU)
+
 
         picked_scales = keep.tile([P, J], U8, name="picked_scales", align_bytes=64)
         nc.vector.tensor_copy(picked_scales[:], scale_window[:].indirect(offsets[:]))
         nc.sync.dma_start(out=moved_scales[0 : P - PASS_GAP, :].bitcast(I32), in_=picked_scales[PASS_GAP:P, :].bitcast(I32))
         tab_planes = (picked_scales, moved_scales)
 
-        for name, i in (("x", 0), ("wx", 0), ("x", 1), ("wt", 1), ("wx", 1)):
-            for a in range(PASSES):
-                load(name, i, a)
+        for name, sides, a in LATER_LOADS:
+            load(name, sides, a)
 
-        turned = back_pool.tile([P, PACK, P], F32, name="back")
+        turned = bank(7, [P, PACK, P])
         nc.tensor.transpose(turned[:, 0, :], bias_rows[:], unit[:])
         bias = keep.tile([P, N // P], F32, name="bias")
         nc.scalar.copy(out=bias[:], in_=turned[:, 0, 0 : N // P])
@@ -149,9 +156,12 @@ def tile_list_tiert_silu_kernel(tc, tab_words, tab_scales, wt, x, wx, b, offs, o
             )
 
         def rounded_chunk(name, i, a, s):
-            rounded = stage.tile([P, CHUNK * PACK], BF16, name="rounded", align_bytes=64)
+            if (name, i, a, s) == ("wt", 0, 1, 1):
+                rounded = keep.tile([P, CHUNK * PACK], BF16, name="before_picked_1", align_bytes=64)
+            else:
+                rounded = stage.tile([P, CHUNK * PACK], BF16, name="rounded", align_bytes=64)
             source = by_runs(raw[name, i, a][:, :, s * CHUNK : (s + 1) * CHUNK])
-            if (name, i, a) in ROUNDED_BY_VECTOR:
+            if (name, i, a, s) in ROUNDED_BY_VECTOR:
                 nc.vector.tensor_copy(out=woven(rounded[:]), in_=source)
             else:
                 nc.scalar.copy(out=woven(rounded[:]), in_=source)
@@ -160,52 +170,61 @@ def tile_list_tiert_silu_kernel(tc, tab_words, tab_scales, wt, x, wx, b, offs, o
         weights = {}
         tokens = {}
 
-        def make_x(h):
-            for a in range(PASSES):
-                codes = keep.tile([P, WIDTH], U32, name="x_%d_%d_codes" % (h, a), align_bytes=64)
-                scales = keep.tile([P, WIDTH], U8, name="x_%d_%d_scales" % (h, a), align_bytes=64)
-                tokens[h, a] = codes, scales
-                for s in range(CHUNKS):
-                    cols = slice(s * CHUNK, (s + 1) * CHUNK)
-                    nc.vector.quantize_mx(
-                        out=codes[:, cols].bitcast(FP8X4), scales=scales[:, cols], in_=rounded_chunk("x", h, a, s)[:]
-                    )
+        def make_x(h, a):
+            codes = keep.tile([P, WIDTH], U32, name="x_%d_%d_codes" % (h, a), align_bytes=64)
+            scales = keep.tile([P, WIDTH], U8, name="x_%d_%d_scales" % (h, a), align_bytes=64)
+            tokens[h, a] = codes, scales
+            rounded = [rounded_chunk("x", h, a, s) for s in range(CHUNKS)]
+            for s in range(CHUNKS):
+                cols = slice(s * CHUNK, (s + 1) * CHUNK)
+                nc.vector.quantize_mx(out=codes[:, cols].bitcast(FP8X4), scales=scales[:, cols], in_=rounded[s][:])
 
-        def make_wx(side):
-            for a in range(PASSES):
-                for s in range(CHUNKS):
-                    c = side * CHUNKS + s
-                    weights["wx", c, a] = quantize(rounded_chunk("wx", side, a, s)[:], "wx_%d_%d" % (c, a))
+        def make_wx(side, a, chunks=range(CHUNKS)):
+            rounded = {s: rounded_chunk("wx", side, a, s) for s in chunks}
+            for s in chunks:
+                c = side * CHUNKS + s
+                weights["wx", c, a] = quantize(rounded[s][:], "wx_%d_%d" % (c, a))
 
-        def make_tiers(side):
-            for a in range(PASSES):
-                for s in range(CHUNKS):
-                    c = side * CHUNKS + s
-                    codes, scales = quantize(rounded_chunk("wt", side, a, s)[:], "wq_%d_%d" % (c, a))
-                    weights["wq", c, a] = codes, scales
-                    rest = stage.tile([P, CHUNK * PACK], BF16, name="rest", bufs=REST_BUFS, align_bytes=64)
-                    for u in range(TILES):
-                        cols = slice(u * P, (u + 1) * P)
-                        back = back_pool.tile([P, PACK, P], F32, name="back")
-                        for t in range(PACK):
-                            nc.tensor.matmul_mx(
-                                out=back[:, t, :],
-                                lhsT=ident_codes[:, t * P : (t + 1) * P].bitcast(FP8X4),
-                                lhsT_scale=ident_scales[:, t * P : (t + 1) * P],
-                                rhs=codes[:, cols].bitcast(FP8X4),
-                                rhs_scale=scales[:, cols],
-                                start=True,
-                                stop=True,
-                            )
-                        nc.vector.tensor_tensor(
-                            out=woven(rest[:, u * P * PACK : (u + 1) * P * PACK]),
-                            in0=by_runs(raw["wt", side, a][:, :, s * CHUNK + u * P : s * CHUNK + (u + 1) * P]),
-                            in1=by_runs(back[:]),
-                            op=ALU.subtract,
+        waiting = []
+
+        def quantize_waiting():
+            for c, a, rest in waiting:
+                weights["wr", c, a] = quantize(rest[:], "wr_%d_%d" % (c, a))
+            waiting.clear()
+
+        def make_wq(side, a):
+            for s in range(CHUNKS):
+                c = side * CHUNKS + s
+                weights["wq", c, a] = quantize(rounded_chunk("wt", side, a, s)[:], "wq_%d_%d" % (c, a))
+
+        def make_rest(side, a, banks, chunks=range(CHUNKS)):
+            for s in chunks:
+                c = side * CHUNKS + s
+                codes, scales = weights["wq", c, a]
+                rest = stage.tile([P, CHUNK * PACK], BF16, name="rest", bufs=REST_BUFS, align_bytes=64)
+                for u in range(TILES):
+                    cols = slice(u * P, (u + 1) * P)
+                    back = bank(banks[(s * TILES + u) % len(banks)], [P, PACK, P])
+                    for t in range(PACK):
+                        nc.tensor.matmul_mx(
+                            out=back[:, t, :],
+                            lhsT=ident_codes[:, t * P : (t + 1) * P].bitcast(FP8X4),
+                            lhsT_scale=ident_scales[:, t * P : (t + 1) * P],
+                            rhs=codes[:, cols].bitcast(FP8X4),
+                            rhs_scale=scales[:, cols],
+                            start=True,
+                            stop=True,
                         )
-                    weights["wr", c, a] = quantize(rest[:], "wr_%d_%d" % (c, a))
+                    nc.vector.tensor_tensor(
+                        out=woven(rest[:, u * P * PACK : (u + 1) * P * PACK]),
+                        in0=by_runs(raw["wt", side, a][:, :, s * CHUNK + u * P : s * CHUNK + (u + 1) * P]),
+                        in1=by_runs(back[:]),
+                        op=ALU.subtract,
+                    )
+                    if u == 0:
+                        quantize_waiting()
+                waiting.append((c, a, rest))
 
-        free_banks = ["sum_%d" % i for i in range(SUM_BANKS)]
         sums = {}
         results = {}
 
@@ -213,7 +232,7 @@ def tile_list_tiert_silu_kernel(tc, tab_words, tab_scales, wt, x, wx, b, offs, o
             codes, scales = weights[operand, n // TILES, a]
             cols = slice(n % TILES * P, (n % TILES + 1) * P)
             nc.tensor.matmul_mx(
-                out=sums[n, h][1][:],
+                out=sums[n, h][:],
                 lhsT=codes[:, cols].bitcast(FP8X4),
                 lhsT_scale=scales[:, cols],
                 rhs=rhs,
@@ -222,55 +241,85 @@ def tile_list_tiert_silu_kernel(tc, tab_words, tab_scales, wt, x, wx, b, offs, o
                 stop=stop,
             )
 
-        def open_sum(n, h):
-            bank = free_banks.pop(0)
-            sums[n, h] = bank, sum_pool.tile([P, WIDTH], F32, name=bank)
-            for a in range(PASSES):
-                for operand in ("wq", "wr"):
-                    rhs = tab_codes[h][:, a, :].bitcast(FP4X4)
-                    plane = tab_planes[a][:, h * WIDTH : (h + 1) * WIDTH]
-                    add_pass(n, h, operand, a, rhs, plane, start=(a == 0 and operand == "wq"), stop=False)
+        def open_sum(n, h, i):
+            sums[n, h] = bank(i, [P, WIDTH])
+
+        def table_passes(n, h, a):
+            for operand in ("wq", "wr"):
+                rhs = tab_codes[h][:, a, :].bitcast(FP4X4)
+                plane = tab_planes[a][:, h * WIDTH : (h + 1) * WIDTH]
+                add_pass(n, h, operand, a, rhs, plane, start=(a == 0 and operand == "wq"), stop=False)
+
+        def x_pass(n, h, a):
+            codes, scales = tokens[h, a]
+            add_pass(n, h, "wx", a, codes[:].bitcast(FP8X4), scales[:], start=False, stop=(a == PASSES - 1))
 
         def close_sum(n, h):
-            for a in range(PASSES):
-                codes, scales = tokens[h, a]
-                add_pass(n, h, "wx", a, codes[:].bitcast(FP8X4), scales[:], start=False, stop=(a == PASSES - 1))
-            bank, acc = sums[n, h]
-            free_banks.append(bank)
+            x_pass(n, h, PASSES - 1)
             if h == 0:
                 results[n] = keep.tile([P, J], F32, name="result_%d" % n)
             cols = slice(h * WIDTH, (h + 1) * WIDTH)
-            nc.scalar.activation(out=results[n][:, cols], in_=acc[:], func=SILU, bias=bias[:, n : n + 1])
+            nc.scalar.activation(out=results[n][:, cols], in_=sums[n, h][:], func=SILU, bias=bias[:, n : n + 1])
             if n == N // P - 1:
                 nc.sync.dma_start(out=out[n * P : (n + 1) * P, cols], in_=results[n][:, cols])
             elif h == 1:
                 nc.sync.dma_start(out=out[n * P : (n + 1) * P, :], in_=results[n][:])
 
-        side_tiles = WIDTH // P
-        spare = SUM_BANKS - side_tiles
+        def table_sum(n, h, i):
+            open_sum(n, h, i)
+            for a in range(PASSES):
+                table_passes(n, h, a)
 
         pick_words(0, "picked_0")
-        make_tiers(0)
-        for n in range(side_tiles):
-            open_sum(n, 0)
-        pick_words(1, "raw_wt_0_0")
-        for n in range(spare):
-            open_sum(n, 1)
-        make_x(0)
-        make_wx(0)
-        for n in range(spare):
-            close_sum(n, 0)
-        for n in range(spare, side_tiles):
-            open_sum(n, 1)
-        for n in range(spare, side_tiles):
-            close_sum(n, 0)
-        make_x(1)
-        make_tiers(1)
-        for n in range(side_tiles):
-            close_sum(n, 1)
-
-        make_wx(1)
-        for n in range(side_tiles, N // P):
-            for h in range(J // WIDTH):
-                open_sum(n, h)
+        make_wq(0, 0)
+        make_rest(0, 0, (4, 5, 6, 7))
+        make_wq(0, 1)
+        pick_words(1, "before_picked_1")
+        make_rest(0, 1, (6, 7))
+        quantize_waiting()
+        early = [(0, 0), (1, 0), (2, 0), (3, 0), (0, 1), (1, 1)]
+        for i, (n, h) in enumerate(early):
+            open_sum(n, h, i)
+        for a in range(PASSES):
+            for n, h in early:
+                table_passes(n, h, a)
+        table_sum(2, 1, 6)
+        table_sum(3, 1, 7)
+        make_x(0, 0)
+        make_wx(0, 0)
+        make_x(1, 0)
+        first = [(n, h) for h in range(2) for n in range(4)]
+        for n, h in first:
+            x_pass(n, h, 0)
+        make_x(1, 1)
+        make_x(0, 1)
+        make_wx(0, 1)
+        for n in range(4):
+            for h in range(2):
                 close_sum(n, h)
+
+        make_wq(1, 0)
+        make_rest(1, 0, (0, 4))
+        make_wq(1, 1)
+        make_rest(1, 1, (0, 4), (0,))
+        quantize_waiting()
+        make_wx(1, 0, (0,))
+        make_wx(1, 1, (0,))
+        make_rest(1, 1, (0, 4), (1,))
+        quantize_waiting()
+        make_wx(1, 0, (1,))
+        make_wx(1, 1, (1,))
+        both = [(n, h) for n in (4, 5, 6) for h in range(2)]
+        for n, h in both:
+            open_sum(n, h, n - 3 + 4 * h)
+            table_passes(n, h, 0)
+        for n in (4, 5, 6):
+            for h in range(2):
+                table_passes(n, h, 1)
+                x_pass(n, h, 0)
+            for h in range(2):
+                close_sum(n, h)
+        for h in range(2):
+            table_sum(7, h, 4 * h)
+            x_pass(7, h, 0)
+            close_sum(7, h)

@@ -17,7 +17,6 @@ SILU = mybir.ActivationFunctionType.Silu
 ALU = mybir.AluOpType
 
 P = 128
-QUAD = 32
 PACK = 4
 K_PASS = P * PACK
 PASSES = K // K_PASS
@@ -30,11 +29,8 @@ LIST_ROWS = 16
 PASS_GAP = 16
 ROUND_BUFS = 12
 REST_BUFS = 4
-LATER_LOADS = (
-    ("x", (0, 1), 0), ("wx", (0,), 0), ("x", (0, 1), 1), ("wx", (0,), 1),
-    ("wt", (1,), 0), ("wt", (1,), 1), ("wx", (1,), 0), ("wx", (1,), 1),
-)
-ROUNDED_BY_VECTOR = (("wx", 0, 0, 0), ("x", 1, 1, 0), ("x", 1, 1, 1), ("wx", 0, 1, 0), ("wt", 1, 0, 0), ("wt", 1, 0, 1), ("wx", 1, 1, 0))
+LATER_LOADS = (("x", (0,), 0), ("wx", (0,), 0), ("x", (1,), 0), ("x", (0, 1), 1), ("wx", (0,), 1), ("wt", (1,), 0), ("wt", (1,), 1), ("wx", (1,), 0), ("wx", (1,), 1))
+ROUNDED_BY_VECTOR = (("x", 1, 1, 0), ("x", 1, 1, 1), ("wx", 0, 1, 0), ("wt", 1, 0, 0), ("wt", 1, 0, 1), ("wx", 1, 1, 0))
 
 
 def tile_list_tiert_silu_kernel(tc, tab_words, tab_scales, wt, x, wx, b, offs, out):
@@ -57,44 +53,21 @@ def tile_list_tiert_silu_kernel(tc, tab_words, tab_scales, wt, x, wx, b, offs, o
         offsets = keep.tile([P, J // LIST_ROWS], U16, name="offsets")
         nc.sync.dma_start(offsets[:], offs)
 
-        scale_window = keep.tile([P, T], U8, name="scale_window", align_bytes=64)
-        nc.vector.memset(scale_window[:].bitcast(I32), 0)
         bias_rows = keep.tile([P, P], F32, name="bias_rows")
         nc.vector.memset(bias_rows[:], 0.0)
+        scale_window = keep.tile([P, T], U8, name="scale_window", align_bytes=64)
+        nc.vector.memset(scale_window[:].bitcast(I32), 0)
         moved_scales = keep.tile([P, J], U8, name="moved_scales", align_bytes=64)
         nc.vector.memset(moved_scales[:].bitcast(I32), 0)
 
-        step = keep.tile([P, 40], F32, name="step")
-        nc.vector.memset(step[:], 1.0)
-        count = keep.tile([P, 40], F32, name="count", align_bytes=64)
-        nc.vector.tensor_tensor_scan(count[:], step[:], step[:], -9.0, ALU.mult, ALU.add)
-        count_down = keep.tile([P, QUAD], F32, name="count_down", align_bytes=64)
-        nc.vector.transpose(count_down[:], count[:, 0:QUAD])
-        column = keep.tile([P, K_PASS], BF16, name="column", align_bytes=64)
-        nc.vector.scalar_tensor_tensor(
-            out=column[:].rearrange("p (u z) -> p u z", z=QUAD),
-            in0=count[:, 0:16].unsqueeze(2).to_broadcast([P, 16, QUAD]),
-            scalar=32.0,
-            in1=count[:, 8:40].unsqueeze(1).to_broadcast([P, 16, QUAD]),
-            op0=ALU.mult,
-            op1=ALU.add,
-        )
-        first_row = keep.tile([P, 1], F32, name="first_row")
-        for q in range(P // QUAD):
-            rows = slice(QUAD * q, QUAD * (q + 1))
-            nc.vector.tensor_scalar(
-                out=first_row[rows, :], in0=count_down[rows, 0:1], scalar1=4.0, scalar2=128.0 * q - 224.0, op0=ALU.mult, op1=ALU.add
-            )
+        ahead = keep.tile([P, K_PASS], BF16, name="ahead", align_bytes=64)
+        nc.gpsimd.iota(ahead[:], [[1, K_PASS]], base=0, channel_multiplier=-PACK, allow_small_or_imprecise_dtypes=True)
         ones = keep.tile([P, PACK, K_PASS], BF16, name="ones", align_bytes=64)
         for t in range(PACK):
-            nc.vector.tensor_scalar(
-                out=ones[:, t, :], in0=column[:], scalar1=first_row[:], scalar2=float(t), op0=ALU.subtract, op1=ALU.is_equal
-            )
+            nc.vector.tensor_scalar(out=ones[:, t, :], in0=ahead[:], scalar1=float(t), scalar2=None, op0=ALU.is_equal)
         ident_codes, ident_scales = quantize(ones[:].rearrange("p t w -> p (t w)"), "ident")
         unit = keep.tile([P, P], F32, name="unit")
-        nc.vector.tensor_scalar(
-            out=unit[:], in0=column[:, 0:K_PASS:PACK], scalar1=first_row[:], scalar2=0.0, op0=ALU.subtract, op1=ALU.is_equal
-        )
+        nc.vector.tensor_scalar(out=unit[:], in0=ahead[:, 0:K_PASS:PACK], scalar1=0.0, scalar2=None, op0=ALU.is_equal)
 
         inputs = {"wt": wt, "wx": wx, "x": x}
         raw = {}
@@ -107,15 +80,15 @@ def tile_list_tiert_silu_kernel(tc, tab_words, tab_scales, wt, x, wx, b, offs, o
             for i in sides:
                 raw[name, i, a] = tile[:, :, i * WIDTH - first : (i + 1) * WIDTH - first]
 
+        nc.sync.dma_start(out=bias_rows[0 : N // P, :], in_=b.rearrange("(c p) -> c p", p=P))
         for r in range(4):
-            nc.scalar.dma_start(
+            nc.sync.dma_start(
                 out=scale_window[r:P:PASS_GAP, :].bitcast(I32),
                 in_=tab_scales[:, r:16:4, :].rearrange("a q t -> q a t").bitcast(I32),
             )
         word_window = keep.tile([P, T], U32, name="word_window", align_bytes=64)
-        load("wt", (0,), 0)
         nc.sync.dma_start(out=word_window[:].bitcast(I32), in_=tab_words[0].rearrange("p t z -> p (t z)").bitcast(I32))
-        nc.scalar.dma_start(out=bias_rows[0 : N // P, :], in_=b.rearrange("(c p) -> c p", p=P))
+        load("wt", (0,), 0)
         load("wt", (0,), 1)
 
         zero = keep.tile([P, 1], F32, name="zero")
@@ -124,7 +97,7 @@ def tile_list_tiert_silu_kernel(tc, tab_words, tab_scales, wt, x, wx, b, offs, o
         nc.scalar.activation(out=warm[:], in_=zero[:], func=SILU)
 
 
-        picked_scales = keep.tile([P, J], U8, name="picked_scales", align_bytes=64)
+        picked_scales = keep.tile([P, J], U8, name="picked_scales", tag="ones", align_bytes=64)
         nc.vector.tensor_copy(picked_scales[:], scale_window[:].indirect(offsets[:]))
         nc.sync.dma_start(out=moved_scales[0 : P - PASS_GAP, :].bitcast(I32), in_=picked_scales[PASS_GAP:P, :].bitcast(I32))
         tab_planes = (picked_scales, moved_scales)
@@ -145,21 +118,20 @@ def tile_list_tiert_silu_kernel(tc, tab_words, tab_scales, wt, x, wx, b, offs, o
 
         tab_codes = {}
 
-        def pick_words(h, tenant_of):
-            picked = keep.tile([P, WIDTH], U32, name="picked_%d" % h, tag=tenant_of, align_bytes=64)
-            entries = offsets[:, h * WIDTH // LIST_ROWS : (h + 1) * WIDTH // LIST_ROWS]
-            nc.vector.tensor_copy(picked[:], word_window[:].indirect(entries))
-            tab_codes[h] = keep.tile([P, PASSES, 2 * WIDTH], U8, name="parted_%d" % h, align_bytes=64)
-            nc.vector.tensor_copy(
-                out=tab_codes[h][:].bitcast(U16),
-                in_=picked[:].bitcast(U16).rearrange("p (s a) -> p a s", a=PASSES),
-            )
+        def pick_words():
+            picked = keep.tile([P, J], U32, name="picked", tag="scale_window", align_bytes=64)
+            for h in range(J // WIDTH):
+                entries = offsets[:, h * WIDTH // LIST_ROWS : (h + 1) * WIDTH // LIST_ROWS]
+                nc.vector.tensor_copy(picked[:, h * WIDTH : (h + 1) * WIDTH], word_window[:].indirect(entries))
+            for h in range(J // WIDTH):
+                tab_codes[h] = keep.tile([P, PASSES, 2 * WIDTH], U8, name="parted_%d" % h, align_bytes=64)
+                nc.vector.tensor_copy(
+                    out=tab_codes[h][:].bitcast(U16),
+                    in_=picked[:, h * WIDTH : (h + 1) * WIDTH].bitcast(U16).rearrange("p (s a) -> p a s", a=PASSES),
+                )
 
         def rounded_chunk(name, i, a, s):
-            if (name, i, a, s) == ("wt", 0, 1, 1):
-                rounded = keep.tile([P, CHUNK * PACK], BF16, name="before_picked_1", align_bytes=64)
-            else:
-                rounded = stage.tile([P, CHUNK * PACK], BF16, name="rounded", align_bytes=64)
+            rounded = stage.tile([P, CHUNK * PACK], BF16, name="rounded", align_bytes=64)
             source = by_runs(raw[name, i, a][:, :, s * CHUNK : (s + 1) * CHUNK])
             if (name, i, a, s) in ROUNDED_BY_VECTOR:
                 nc.vector.tensor_copy(out=woven(rounded[:]), in_=source)
@@ -228,11 +200,11 @@ def tile_list_tiert_silu_kernel(tc, tab_words, tab_scales, wt, x, wx, b, offs, o
         sums = {}
         results = {}
 
-        def add_pass(n, h, operand, a, rhs, rhs_scale, start, stop):
+        def add_pass(n, first, operand, a, rhs, rhs_scale, start, stop):
             codes, scales = weights[operand, n // TILES, a]
             cols = slice(n % TILES * P, (n % TILES + 1) * P)
             nc.tensor.matmul_mx(
-                out=sums[n, h][:],
+                out=sums[n, first][:],
                 lhsT=codes[:, cols].bitcast(FP8X4),
                 lhsT_scale=scales[:, cols],
                 rhs=rhs,
@@ -241,40 +213,40 @@ def tile_list_tiert_silu_kernel(tc, tab_words, tab_scales, wt, x, wx, b, offs, o
                 stop=stop,
             )
 
-        def open_sum(n, h, i):
-            sums[n, h] = bank(i, [P, WIDTH])
+        def open_sum(n, h, i, first=0, width=WIDTH):
+            sums[n, h * WIDTH + first] = bank(i, [P, width])
 
-        def table_passes(n, h, a):
+        def table_passes(n, h, a, first=0, width=WIDTH):
             for operand in ("wq", "wr"):
-                rhs = tab_codes[h][:, a, :].bitcast(FP4X4)
-                plane = tab_planes[a][:, h * WIDTH : (h + 1) * WIDTH]
-                add_pass(n, h, operand, a, rhs, plane, start=(a == 0 and operand == "wq"), stop=False)
+                rhs = tab_codes[h][:, a, 2 * first : 2 * (first + width)].bitcast(FP4X4)
+                plane = tab_planes[a][:, h * WIDTH + first : h * WIDTH + first + width]
+                add_pass(n, h * WIDTH + first, operand, a, rhs, plane, start=(a == 0 and operand == "wq"), stop=False)
 
-        def x_pass(n, h, a):
+        def x_pass(n, h, a, first=0, width=WIDTH):
             codes, scales = tokens[h, a]
-            add_pass(n, h, "wx", a, codes[:].bitcast(FP8X4), scales[:], start=False, stop=(a == PASSES - 1))
+            cols = slice(first, first + width)
+            add_pass(n, h * WIDTH + first, "wx", a, codes[:, cols].bitcast(FP8X4), scales[:, cols], start=False, stop=(a == PASSES - 1))
 
-        def close_sum(n, h):
-            x_pass(n, h, PASSES - 1)
-            if h == 0:
+        def close_sum(n, h, first=0, width=WIDTH):
+            x_pass(n, h, PASSES - 1, first, width)
+            if n not in results:
                 results[n] = keep.tile([P, J], F32, name="result_%d" % n)
-            cols = slice(h * WIDTH, (h + 1) * WIDTH)
-            nc.scalar.activation(out=results[n][:, cols], in_=sums[n, h][:], func=SILU, bias=bias[:, n : n + 1])
+            cols = slice(h * WIDTH + first, h * WIDTH + first + width)
+            nc.scalar.activation(out=results[n][:, cols], in_=sums[n, cols.start][:], func=SILU, bias=bias[:, n : n + 1])
             if n == N // P - 1:
                 nc.sync.dma_start(out=out[n * P : (n + 1) * P, cols], in_=results[n][:, cols])
             elif h == 1:
                 nc.sync.dma_start(out=out[n * P : (n + 1) * P, :], in_=results[n][:])
 
-        def table_sum(n, h, i):
-            open_sum(n, h, i)
+        def table_sum(n, h, i, first=0, width=WIDTH):
+            open_sum(n, h, i, first, width)
             for a in range(PASSES):
-                table_passes(n, h, a)
+                table_passes(n, h, a, first, width)
 
-        pick_words(0, "picked_0")
+        pick_words()
         make_wq(0, 0)
-        make_rest(0, 0, (4, 5, 6, 7))
+        make_rest(0, 0, (0, 1, 4, 5))
         make_wq(0, 1)
-        pick_words(1, "before_picked_1")
         make_rest(0, 1, (6, 7))
         quantize_waiting()
         early = [(0, 0), (1, 0), (2, 0), (3, 0), (0, 1), (1, 1)]
@@ -319,7 +291,7 @@ def tile_list_tiert_silu_kernel(tc, tab_words, tab_scales, wt, x, wx, b, offs, o
                 x_pass(n, h, 0)
             for h in range(2):
                 close_sum(n, h)
-        for h in range(2):
-            table_sum(7, h, 4 * h)
-            x_pass(7, h, 0)
-            close_sum(7, h)
+        for h, i, first, width in ((0, 0, 0, WIDTH), (1, 4, 0, CHUNK), (1, 1, CHUNK, CHUNK)):
+            table_sum(7, h, i, first, width)
+            x_pass(7, h, 0, first, width)
+            close_sum(7, h, first, width)

@@ -25,6 +25,7 @@ CHUNK = 256
 CHUNKS = WIDTH // CHUNK
 TILES = CHUNK // P
 RUN = 4
+DMA_ALIGN = 256
 LIST_ROWS = 16
 PASS_GAP = 16
 ROUND_BUFS = 12
@@ -74,7 +75,7 @@ def tile_list_tiert_silu_kernel(tc, tab_words, tab_scales, wt, x, wx, b, offs, o
 
         def load(name, sides, a):
             first, width = sides[0] * WIDTH, len(sides) * WIDTH
-            tile = keep.tile([P, PACK, width], F32, name="raw_%s_%d_%d" % (name, sides[0], a), align_bytes=64)
+            tile = keep.tile([P, PACK, width], F32, name="raw_%s_%d_%d" % (name, sides[0], a), align_bytes=DMA_ALIGN)
             rows = inputs[name][a * K_PASS : (a + 1) * K_PASS, first : first + width]
             nc.sync.dma_start(out=tile[:], in_=rows.rearrange("(p t) w -> p t w", t=PACK))
             for i in sides:
@@ -86,7 +87,7 @@ def tile_list_tiert_silu_kernel(tc, tab_words, tab_scales, wt, x, wx, b, offs, o
                 out=scale_window[r:P:PASS_GAP, :].bitcast(I32),
                 in_=tab_scales[:, r:16:4, :].rearrange("a q t -> q a t").bitcast(I32),
             )
-        word_window = keep.tile([P, T], U32, name="word_window", align_bytes=64)
+        word_window = keep.tile([P, T], U32, name="word_window", align_bytes=DMA_ALIGN)
         nc.sync.dma_start(out=word_window[:].bitcast(I32), in_=tab_words[0].rearrange("p t z -> p (t z)").bitcast(I32))
         load("wt", (0,), 0)
         load("wt", (0,), 1)
@@ -230,7 +231,7 @@ def tile_list_tiert_silu_kernel(tc, tab_words, tab_scales, wt, x, wx, b, offs, o
         def close_sum(n, h, first=0, width=WIDTH):
             x_pass(n, h, PASSES - 1, first, width)
             if n not in results:
-                results[n] = keep.tile([P, J], F32, name="result_%d" % n)
+                results[n] = keep.tile([P, J], F32, name="result_%d" % n, align_bytes=DMA_ALIGN)
             cols = slice(h * WIDTH + first, h * WIDTH + first + width)
             nc.scalar.activation(out=results[n][:, cols], in_=sums[n, cols.start][:], func=SILU, bias=bias[:, n : n + 1])
             if n == N // P - 1:

@@ -28,10 +28,9 @@ RUN = 4
 DMA_ALIGN = 256
 LIST_ROWS = 16
 PASS_GAP = 16
-ROUND_BUFS = 12
+ROUND_BUFS = 10
+HEAD_TILES = 9
 REST_BUFS = 4
-LATER_LOADS = (("x", (0,), 0), ("wx", (0,), 0), ("x", (1,), 0), ("x", (0, 1), 1), ("wx", (0,), 1), ("wt", (1,), 0), ("wt", (1,), 1), ("wx", (1,), 0), ("wx", (1,), 1))
-ROUNDED_BY_VECTOR = (("x", 1, 1, 0), ("x", 1, 1, 1), ("wx", 0, 1, 0), ("wt", 1, 0, 0), ("wt", 1, 0, 1), ("wx", 1, 1, 0))
 
 
 def tile_list_tiert_silu_kernel(tc, tab_words, tab_scales, wt, x, wx, b, offs, out):
@@ -44,9 +43,15 @@ def tile_list_tiert_silu_kernel(tc, tab_words, tab_scales, wt, x, wx, b, offs, o
         def bank(i, shape):
             return psum.tile(shape, F32, name="bank_%d" % i)
 
+        def in_turn(shape, dtype, name):
+            return keep.tile(shape, dtype, name=name, tag="head", bufs=HEAD_TILES, align_bytes=64)
+
         def quantize(rounded, name):
             width = rounded.shape[1] // PACK
-            codes = keep.tile([P, width], U32, name=name + "_codes", align_bytes=64)
+            if name in ("ident", "wq_0_0", "wq_1_0"):
+                codes = in_turn([P, width], U32, name + "_codes")
+            else:
+                codes = keep.tile([P, width], U32, name=name + "_codes", align_bytes=64)
             scales = keep.tile([P, width], U8, name=name + "_scales", align_bytes=64)
             nc.vector.quantize_mx(out=codes[:].bitcast(FP8X4), scales=scales[:], in_=rounded)
             return codes, scales
@@ -81,35 +86,43 @@ def tile_list_tiert_silu_kernel(tc, tab_words, tab_scales, wt, x, wx, b, offs, o
             for i in sides:
                 raw[name, i, a] = tile[:, :, i * WIDTH - first : (i + 1) * WIDTH - first]
 
-        nc.sync.dma_start(out=bias_rows[0 : N // P, :], in_=b.rearrange("(c p) -> c p", p=P))
-        for r in range(4):
-            nc.sync.dma_start(
-                out=scale_window[r:P:PASS_GAP, :].bitcast(I32),
-                in_=tab_scales[:, r:16:4, :].rearrange("a q t -> q a t").bitcast(I32),
-            )
+        def load_bias():
+            nc.sync.dma_start(out=bias_rows[0 : N // P, :], in_=b.rearrange("(c p) -> c p", p=P))
+
+        def load_scales():
+            for r in range(4):
+                nc.sync.dma_start(
+                    out=scale_window[r:P:PASS_GAP, :].bitcast(I32),
+                    in_=tab_scales[:, r:16:4, :].rearrange("a q t -> q a t").bitcast(I32),
+                )
+
         word_window = keep.tile([P, T], U32, name="word_window", align_bytes=DMA_ALIGN)
-        nc.sync.dma_start(out=word_window[:].bitcast(I32), in_=tab_words[0].rearrange("p t z -> p (t z)").bitcast(I32))
-        load("wt", (0,), 0)
-        load("wt", (0,), 1)
 
-        zero = keep.tile([P, 1], F32, name="zero")
-        nc.vector.memset(zero[:], 0.0)
-        warm = keep.tile([P, 1], F32, name="warm")
-        nc.scalar.activation(out=warm[:], in_=zero[:], func=SILU)
+        def load_words():
+            nc.sync.dma_start(out=word_window[:].bitcast(I32), in_=tab_words[0].rearrange("p t z -> p (t z)").bitcast(I32))
 
+        def warm_up():
+            zero = keep.tile([P, 1], F32, name="zero")
+            nc.vector.memset(zero[:], 0.0)
+            warm = keep.tile([P, 1], F32, name="warm")
+            nc.scalar.activation(out=warm[:], in_=zero[:], func=SILU)
 
-        picked_scales = keep.tile([P, J], U8, name="picked_scales", tag="ones", align_bytes=64)
-        nc.vector.tensor_copy(picked_scales[:], scale_window[:].indirect(offsets[:]))
-        nc.sync.dma_start(out=moved_scales[0 : P - PASS_GAP, :].bitcast(I32), in_=picked_scales[PASS_GAP:P, :].bitcast(I32))
-        tab_planes = (picked_scales, moved_scales)
+        tab_planes = {}
 
-        for name, sides, a in LATER_LOADS:
-            load(name, sides, a)
+        def pick_scales():
+            tab_planes[0] = in_turn([P, J], U8, "picked_scales")
+            nc.vector.tensor_copy(tab_planes[0][:], scale_window[:].indirect(offsets[:]))
 
-        turned = bank(7, [P, PACK, P])
-        nc.tensor.transpose(turned[:, 0, :], bias_rows[:], unit[:])
+        def move_scales():
+            nc.sync.dma_start(out=moved_scales[0 : P - PASS_GAP, :].bitcast(I32), in_=tab_planes[0][PASS_GAP:P, :].bitcast(I32))
+            tab_planes[1] = moved_scales
+
         bias = keep.tile([P, N // P], F32, name="bias")
-        nc.scalar.copy(out=bias[:], in_=turned[:, 0, 0 : N // P])
+
+        def turn_bias(i):
+            turned = bank(i, [P, PACK, P])
+            nc.tensor.transpose(turned[:, 0, :], bias_rows[:], unit[:])
+            nc.scalar.copy(out=bias[:], in_=turned[:, 0, 0 : N // P])
 
         def woven(ap):
             return ap.rearrange("p (c i t) -> p c t i", i=RUN, t=PACK)
@@ -117,91 +130,98 @@ def tile_list_tiert_silu_kernel(tc, tab_words, tab_scales, wt, x, wx, b, offs, o
         def by_runs(ap):
             return ap.rearrange("p t (c i) -> p c t i", i=RUN)
 
+        picked = {}
         tab_codes = {}
 
-        def pick_words():
-            picked = keep.tile([P, J], U32, name="picked", tag="scale_window", align_bytes=64)
-            for h in range(J // WIDTH):
-                entries = offsets[:, h * WIDTH // LIST_ROWS : (h + 1) * WIDTH // LIST_ROWS]
-                nc.vector.tensor_copy(picked[:, h * WIDTH : (h + 1) * WIDTH], word_window[:].indirect(entries))
-            for h in range(J // WIDTH):
-                tab_codes[h] = keep.tile([P, PASSES, 2 * WIDTH], U8, name="parted_%d" % h, align_bytes=64)
-                nc.vector.tensor_copy(
-                    out=tab_codes[h][:].bitcast(U16),
-                    in_=picked[:, h * WIDTH : (h + 1) * WIDTH].bitcast(U16).rearrange("p (s a) -> p a s", a=PASSES),
-                )
+        def pick_words(h):
+            picked[h] = in_turn([P, WIDTH], U32, "picked_%d" % h)[:]
+            entries = offsets[:, h * WIDTH // LIST_ROWS : (h + 1) * WIDTH // LIST_ROWS]
+            nc.vector.tensor_copy(picked[h], word_window[:].indirect(entries))
 
-        def rounded_chunk(name, i, a, s):
-            rounded = stage.tile([P, CHUNK * PACK], BF16, name="rounded", align_bytes=64)
-            source = by_runs(raw[name, i, a][:, :, s * CHUNK : (s + 1) * CHUNK])
-            if (name, i, a, s) in ROUNDED_BY_VECTOR:
-                nc.vector.tensor_copy(out=woven(rounded[:]), in_=source)
+        def part_words(h):
+            tab_codes[h] = in_turn([P, PASSES, 2 * WIDTH], U8, "parted_%d" % h)
+            nc.vector.tensor_copy(out=tab_codes[h][:].bitcast(U16), in_=picked[h].bitcast(U16).rearrange("p (s a) -> p a s", a=PASSES))
+
+        rounded = {}
+
+        def round_chunk(name, i, a, s, engine):
+            if not rounded:
+                tile = in_turn([P, CHUNK * PACK], BF16, "first_rounded")
             else:
-                nc.scalar.copy(out=woven(rounded[:]), in_=source)
-            return rounded
+                tile = stage.tile([P, CHUNK * PACK], BF16, name="rounded", align_bytes=64)
+            source = by_runs(raw[name, i, a][:, :, s * CHUNK : (s + 1) * CHUNK])
+            if engine == "V":
+                nc.vector.tensor_copy(out=woven(tile[:]), in_=source)
+            else:
+                nc.scalar.copy(out=woven(tile[:]), in_=source)
+            rounded[name, i, a, s] = tile
 
         weights = {}
         tokens = {}
 
-        def make_x(h, a):
-            codes = keep.tile([P, WIDTH], U32, name="x_%d_%d_codes" % (h, a), align_bytes=64)
-            scales = keep.tile([P, WIDTH], U8, name="x_%d_%d_scales" % (h, a), align_bytes=64)
-            tokens[h, a] = codes, scales
-            rounded = [rounded_chunk("x", h, a, s) for s in range(CHUNKS)]
-            for s in range(CHUNKS):
+        def quantize_chunk(name, i, a, s):
+            if name == "x":
+                if (i, a) not in tokens:
+                    codes = keep.tile([P, WIDTH], U32, name="x_%d_%d_codes" % (i, a), align_bytes=64)
+                    scales = keep.tile([P, WIDTH], U8, name="x_%d_%d_scales" % (i, a), align_bytes=64)
+                    tokens[i, a] = codes, scales
+                codes, scales = tokens[i, a]
                 cols = slice(s * CHUNK, (s + 1) * CHUNK)
-                nc.vector.quantize_mx(out=codes[:, cols].bitcast(FP8X4), scales=scales[:, cols], in_=rounded[s][:])
+                nc.vector.quantize_mx(out=codes[:, cols].bitcast(FP8X4), scales=scales[:, cols], in_=rounded[name, i, a, s][:])
+            else:
+                operand = "wq" if name == "wt" else name
+                c = i * CHUNKS + s
+                weights[operand, c, a] = quantize(rounded[name, i, a, s][:], "%s_%d_%d" % (operand, c, a))
 
-        def make_wx(side, a, chunks=range(CHUNKS)):
-            rounded = {s: rounded_chunk("wx", side, a, s) for s in chunks}
-            for s in chunks:
-                c = side * CHUNKS + s
-                weights["wx", c, a] = quantize(rounded[s][:], "wx_%d_%d" % (c, a))
-
-        waiting = []
-
-        def quantize_waiting():
-            for c, a, rest in waiting:
-                weights["wr", c, a] = quantize(rest[:], "wr_%d_%d" % (c, a))
-            waiting.clear()
-
-        def make_wq(side, a):
+        def make(name, i, a, engines):
             for s in range(CHUNKS):
-                c = side * CHUNKS + s
-                weights["wq", c, a] = quantize(rounded_chunk("wt", side, a, s)[:], "wq_%d_%d" % (c, a))
+                round_chunk(name, i, a, s, engines[s])
+            for s in range(CHUNKS):
+                quantize_chunk(name, i, a, s)
 
-        def make_rest(side, a, banks, chunks=range(CHUNKS)):
-            for s in chunks:
-                c = side * CHUNKS + s
-                codes, scales = weights["wq", c, a]
-                rest = stage.tile([P, CHUNK * PACK], BF16, name="rest", bufs=REST_BUFS, align_bytes=64)
-                for u in range(TILES):
-                    cols = slice(u * P, (u + 1) * P)
-                    back = bank(banks[(s * TILES + u) % len(banks)], [P, PACK, P])
-                    for t in range(PACK):
-                        nc.tensor.matmul_mx(
-                            out=back[:, t, :],
-                            lhsT=ident_codes[:, t * P : (t + 1) * P].bitcast(FP8X4),
-                            lhsT_scale=ident_scales[:, t * P : (t + 1) * P],
-                            rhs=codes[:, cols].bitcast(FP8X4),
-                            rhs_scale=scales[:, cols],
-                            start=True,
-                            stop=True,
-                        )
-                    nc.vector.tensor_tensor(
-                        out=woven(rest[:, u * P * PACK : (u + 1) * P * PACK]),
-                        in0=by_runs(raw["wt", side, a][:, :, s * CHUNK + u * P : s * CHUNK + (u + 1) * P]),
-                        in1=by_runs(back[:]),
-                        op=ALU.subtract,
-                    )
-                    if u == 0:
-                        quantize_waiting()
-                waiting.append((c, a, rest))
+        rests = {}
+
+        def subtract(c, a, u, i):
+            codes, scales = weights["wq", c, a]
+            if u == 0:
+                rests[c, a] = stage.tile([P, CHUNK * PACK], BF16, name="rest", bufs=REST_BUFS, align_bytes=64)
+            cols = slice(u * P, (u + 1) * P)
+            back = bank(i, [P, PACK, P])
+            for t in range(PACK):
+                nc.tensor.matmul_mx(
+                    out=back[:, t, :],
+                    lhsT=ident_codes[:, t * P : (t + 1) * P].bitcast(FP8X4),
+                    lhsT_scale=ident_scales[:, t * P : (t + 1) * P],
+                    rhs=codes[:, cols].bitcast(FP8X4),
+                    rhs_scale=scales[:, cols],
+                    start=True,
+                    stop=True,
+                )
+            first = c % CHUNKS * CHUNK + u * P
+            nc.vector.tensor_tensor(
+                out=woven(rests[c, a][:, u * P * PACK : (u + 1) * P * PACK]),
+                in0=by_runs(raw["wt", c // CHUNKS, a][:, :, first : first + P]),
+                in1=by_runs(back[:]),
+                op=ALU.subtract,
+            )
+
+        def quantize_rest(c, a):
+            weights["wr", c, a] = quantize(rests[c, a][:], "wr_%d_%d" % (c, a))
+
+        def tier(side, a, banks):
+            c = side * CHUNKS
+            subtract(c, a, 0, banks[0])
+            subtract(c, a, 1, banks[1 % len(banks)])
+            subtract(c + 1, a, 0, banks[2 % len(banks)])
+            quantize_rest(c, a)
+            subtract(c + 1, a, 1, banks[3 % len(banks)])
+            quantize_rest(c + 1, a)
 
         sums = {}
+        done = {}
         results = {}
 
-        def add_pass(n, first, operand, a, rhs, rhs_scale, start, stop):
+        def add_pass(n, first, operand, a, rhs, rhs_scale):
             codes, scales = weights[operand, n // TILES, a]
             cols = slice(n % TILES * P, (n % TILES + 1) * P)
             nc.tensor.matmul_mx(
@@ -210,89 +230,193 @@ def tile_list_tiert_silu_kernel(tc, tab_words, tab_scales, wt, x, wx, b, offs, o
                 lhsT_scale=scales[:, cols],
                 rhs=rhs,
                 rhs_scale=rhs_scale,
-                start=start,
-                stop=stop,
+                start=done[n, first] == 0,
+                stop=done[n, first] == 3 * PASSES - 1,
             )
+            done[n, first] += 1
 
         def open_sum(n, h, i, first=0, width=WIDTH):
             sums[n, h * WIDTH + first] = bank(i, [P, width])
+            done[n, h * WIDTH + first] = 0
+
+        def table_pass(n, h, a, operand, first=0, width=WIDTH):
+            rhs = tab_codes[h][:, a, 2 * first : 2 * (first + width)].bitcast(FP4X4)
+            plane = tab_planes[a][:, h * WIDTH + first : h * WIDTH + first + width]
+            add_pass(n, h * WIDTH + first, operand, a, rhs, plane)
 
         def table_passes(n, h, a, first=0, width=WIDTH):
             for operand in ("wq", "wr"):
-                rhs = tab_codes[h][:, a, 2 * first : 2 * (first + width)].bitcast(FP4X4)
-                plane = tab_planes[a][:, h * WIDTH + first : h * WIDTH + first + width]
-                add_pass(n, h * WIDTH + first, operand, a, rhs, plane, start=(a == 0 and operand == "wq"), stop=False)
+                table_pass(n, h, a, operand, first, width)
 
         def x_pass(n, h, a, first=0, width=WIDTH):
             codes, scales = tokens[h, a]
             cols = slice(first, first + width)
-            add_pass(n, h * WIDTH + first, "wx", a, codes[:, cols].bitcast(FP8X4), scales[:, cols], start=False, stop=(a == PASSES - 1))
+            add_pass(n, h * WIDTH + first, "wx", a, codes[:, cols].bitcast(FP8X4), scales[:, cols])
 
-        def close_sum(n, h, first=0, width=WIDTH):
-            x_pass(n, h, PASSES - 1, first, width)
+        def finish(n, h, first=0, width=WIDTH):
             if n not in results:
                 results[n] = keep.tile([P, J], F32, name="result_%d" % n, align_bytes=DMA_ALIGN)
             cols = slice(h * WIDTH + first, h * WIDTH + first + width)
             nc.scalar.activation(out=results[n][:, cols], in_=sums[n, cols.start][:], func=SILU, bias=bias[:, n : n + 1])
-            if n == N // P - 1:
-                nc.sync.dma_start(out=out[n * P : (n + 1) * P, cols], in_=results[n][:, cols])
-            elif h == 1:
-                nc.sync.dma_start(out=out[n * P : (n + 1) * P, :], in_=results[n][:])
 
-        def table_sum(n, h, i, first=0, width=WIDTH):
-            open_sum(n, h, i, first, width)
-            for a in range(PASSES):
-                table_passes(n, h, a, first, width)
+        def store(n, first=0, width=J):
+            cols = slice(first, first + width)
+            nc.sync.dma_start(out=out[n * P : (n + 1) * P, cols], in_=results[n][:, cols])
 
-        pick_words()
-        make_wq(0, 0)
-        make_rest(0, 0, (0, 1, 4, 5))
-        make_wq(0, 1)
-        make_rest(0, 1, (6, 7))
-        quantize_waiting()
-        early = [(0, 0), (1, 0), (2, 0), (3, 0), (0, 1), (1, 1)]
-        for i, (n, h) in enumerate(early):
-            open_sum(n, h, i)
-        for a in range(PASSES):
-            for n, h in early:
-                table_passes(n, h, a)
-        table_sum(2, 1, 6)
-        table_sum(3, 1, 7)
-        make_x(0, 0)
-        make_wx(0, 0)
-        make_x(1, 0)
-        first = [(n, h) for h in range(2) for n in range(4)]
-        for n, h in first:
-            x_pass(n, h, 0)
-        make_x(1, 1)
-        make_x(0, 1)
-        make_wx(0, 1)
+        load_bias()
+        load_scales()
+        load_words()
+        load("wt", (0,), 0)
+        load("wt", (0,), 1)
+        warm_up()
+        pick_scales()
+        move_scales()
+
+        def r(name, i, a, s, e):
+            round_chunk(name, i, a, s, e)
+        def q(name, i, a, s):
+            quantize_chunk(name, i, a, s)
+        def t(n, h, a, op):
+            table_pass(n, h, a, op)
+        for name, i, a in (("wt", 1, 0), ("x", 0, 0), ("wx", 0, 0), ("x", 0, 1), ("wx", 0, 1), ("wt", 1, 1), ("x", 1, 0), ("x", 1, 1), ("wx", 1, 0), ("wx", 1, 1)):
+            load(name, (i,), a)
+        turn_bias(7)
+        pick_words(0)
+        pick_words(1)
+        r("wt", 0, 0, 0, "V")
+        r("wt", 0, 0, 1, "A")
+        for name, i, a in (("wt", 0, 1), ("wt", 1, 0), ("x", 0, 0), ("wx", 0, 0), ("x", 0, 1)):
+            for s in range(2):
+                r(name, i, a, s, "A")
+        r("wx", 0, 1, 0, "V")
+        r("wx", 0, 1, 1, "A")
+        part_words(0)
+        q("wt", 0, 0, 0)
+        q("wt", 0, 0, 1)
+        part_words(1)
+        subtract(0, 0, 0, 4)
+        subtract(0, 0, 1, 5)
+        q("wt", 0, 1, 0)
+        subtract(1, 0, 0, 6)
+        quantize_rest(0, 0)
+        subtract(1, 0, 1, 7)
         for n in range(4):
-            for h in range(2):
-                close_sum(n, h)
-
-        make_wq(1, 0)
-        make_rest(1, 0, (0, 4))
-        make_wq(1, 1)
-        make_rest(1, 1, (0, 4), (0,))
-        quantize_waiting()
-        make_wx(1, 0, (0,))
-        make_wx(1, 1, (0,))
-        make_rest(1, 1, (0, 4), (1,))
-        quantize_waiting()
-        make_wx(1, 0, (1,))
-        make_wx(1, 1, (1,))
-        both = [(n, h) for n in (4, 5, 6) for h in range(2)]
-        for n, h in both:
-            open_sum(n, h, n - 3 + 4 * h)
-            table_passes(n, h, 0)
-        for n in (4, 5, 6):
-            for h in range(2):
-                table_passes(n, h, 1)
-                x_pass(n, h, 0)
-            for h in range(2):
-                close_sum(n, h)
-        for h, i, first, width in ((0, 0, 0, WIDTH), (1, 4, 0, CHUNK), (1, 1, CHUNK, CHUNK)):
-            table_sum(7, h, i, first, width)
-            x_pass(7, h, 0, first, width)
-            close_sum(7, h, first, width)
+            open_sum(n, 0, n)
+            t(n, 0, 0, "wq")
+        q("wt", 0, 1, 1)
+        subtract(0, 1, 0, 4)
+        quantize_rest(1, 0)
+        subtract(0, 1, 1, 5)
+        t(0, 0, 0, "wr")
+        t(1, 0, 0, "wr")
+        q("wt", 1, 0, 0)
+        subtract(1, 1, 0, 6)
+        quantize_rest(0, 1)
+        subtract(1, 1, 1, 7)
+        t(2, 0, 0, "wr")
+        t(3, 0, 0, "wr")
+        for n in range(4):
+            t(n, 0, 1, "wq")
+        q("wt", 1, 0, 1)
+        subtract(2, 0, 0, 6)
+        quantize_rest(1, 1)
+        open_sum(0, 1, 4)
+        table_passes(0, 1, 0)
+        subtract(2, 0, 1, 7)
+        t(0, 0, 1, "wr")
+        t(1, 0, 1, "wr")
+        q("x", 0, 0, 0)
+        subtract(3, 0, 0, 6)
+        quantize_rest(2, 0)
+        t(2, 0, 1, "wr")
+        t(3, 0, 1, "wr")
+        subtract(3, 0, 1, 7)
+        table_passes(0, 1, 1)
+        open_sum(1, 1, 5)
+        for a in range(2):
+            table_passes(1, 1, a)
+        q("x", 0, 0, 1)
+        q("wx", 0, 0, 0)
+        q("wx", 0, 0, 1)
+        quantize_rest(3, 0)
+        q("x", 0, 1, 0)
+        q("x", 0, 1, 1)
+        open_sum(2, 1, 6)
+        for a in range(2):
+            table_passes(2, 1, a)
+        for n in range(4):
+            x_pass(n, 0, 0)
+        open_sum(3, 1, 7)
+        table_passes(3, 1, 0)
+        q("wx", 0, 1, 0)
+        q("wx", 0, 1, 1)
+        r("wt", 1, 1, 0, "V")
+        r("wt", 1, 1, 1, "V")
+        for n in range(4):
+            x_pass(n, 0, 1)
+            finish(n, 0)
+            store(n, 0, WIDTH)
+        table_passes(3, 1, 1)
+        q("wt", 1, 1, 0)
+        q("wt", 1, 1, 1)
+        r("x", 1, 0, 0, "A")
+        r("x", 1, 0, 1, "A")
+        r("x", 1, 1, 0, "A")
+        subtract(2, 1, 0, 1)
+        subtract(2, 1, 1, 2)
+        open_sum(4, 0, 0)
+        table_passes(4, 0, 0)
+        subtract(3, 1, 0, 1)
+        quantize_rest(2, 1)
+        open_sum(5, 0, 3)
+        table_passes(5, 0, 0)
+        subtract(3, 1, 1, 2)
+        q("x", 1, 0, 0)
+        q("x", 1, 0, 1)
+        r("x", 1, 1, 1, "V")
+        quantize_rest(3, 1)
+        table_passes(4, 0, 1)
+        table_passes(5, 0, 1)
+        open_sum(6, 0, 1)
+        table_passes(6, 0, 0)
+        for n in range(4):
+            x_pass(n, 1, 0)
+        q("x", 1, 1, 0)
+        q("x", 1, 1, 1)
+        r("wx", 1, 0, 0, "A")
+        r("wx", 1, 0, 1, "V")
+        for n in range(4):
+            x_pass(n, 1, 1)
+            finish(n, 1)
+            store(n, WIDTH, WIDTH)
+        q("wx", 1, 0, 0)
+        q("wx", 1, 0, 1)
+        r("wx", 1, 1, 0, "V")
+        r("wx", 1, 1, 1, "V")
+        q("wx", 1, 1, 0)
+        q("wx", 1, 1, 1)
+        table_passes(6, 0, 1)
+        open_sum(7, 0, 2)
+        for a in range(2):
+            table_passes(7, 0, a)
+        for n in range(4, 8):
+            for a in range(2):
+                x_pass(n, 0, a)
+            finish(n, 0)
+            store(n, 0, WIDTH)
+        for n in range(4, 7):
+            open_sum(n, 1, n)
+            for a in range(2):
+                table_passes(n, 1, a)
+            for a in range(2):
+                x_pass(n, 1, a)
+            finish(n, 1)
+            store(n, WIDTH, WIDTH)
+        for i, first in ((7, 0), (0, CHUNK)):
+            open_sum(7, 1, i, first, CHUNK)
+            for a in range(PASSES):
+                table_passes(7, 1, a, first, CHUNK)
+            for a in range(PASSES):
+                x_pass(7, 1, a, first, CHUNK)
+            finish(7, 1, first, CHUNK)
+            store(7, WIDTH + first, CHUNK)

@@ -28,36 +28,43 @@ RUN = 4
 DMA_ALIGN = 256
 LIST_ROWS = 16
 PASS_GAP = 16
-ROUND_BUFS = 10
-HEAD_TILES = 9
-REST_BUFS = 4
+VECTOR_TILES = 49
+SCALAR_SLOTS = 16
 
 
 def tile_list_tiert_silu_kernel(tc, tab_words, tab_scales, wt, x, wx, b, offs, out):
     nc = tc.nc
     with ExitStack() as ctx:
         keep = ctx.enter_context(tc.tile_pool(name="keep", bufs=1))
-        stage = ctx.enter_context(tc.tile_pool(name="stage", bufs=ROUND_BUFS))
         psum = ctx.enter_context(tc.psum_pool(name="psum", bufs=1))
 
         def bank(i, shape):
             return psum.tile(shape, F32, name="bank_%d" % i)
 
-        def in_turn(shape, dtype, name):
-            return keep.tile(shape, dtype, name=name, tag="head", bufs=HEAD_TILES, align_bytes=64)
+        def vector_tile(shape, dtype, name):
+            return keep.tile(shape, dtype, name=name, tag="vector_turn", bufs=VECTOR_TILES, align_bytes=64)
+
+        def scalar_tile(shape, dtype, name):
+            return keep.tile(shape, dtype, name=name, tag="scalar_turn", bufs=SCALAR_SLOTS, align_bytes=DMA_ALIGN)
 
         def quantize(rounded, name):
             width = rounded.shape[1] // PACK
-            if name in ("ident", "wq_0_0", "wq_1_0"):
-                codes = in_turn([P, width], U32, name + "_codes")
+            if width == CHUNK:
+                both = vector_tile([P, (PACK + 1) * width], U8, name + "_codes")
+                codes, scales = both[:, 0 : PACK * width].bitcast(U32), both[:, PACK * width :]
             else:
-                codes = keep.tile([P, width], U32, name=name + "_codes", align_bytes=64)
-            scales = keep.tile([P, width], U8, name=name + "_scales", align_bytes=64)
-            nc.vector.quantize_mx(out=codes[:].bitcast(FP8X4), scales=scales[:], in_=rounded)
+                codes = vector_tile([P, width], U32, name + "_codes")[:]
+                scales = keep.tile([P, width], U8, name=name + "_scales", align_bytes=64)[:]
+            nc.vector.quantize_mx(out=codes.bitcast(FP8X4), scales=scales, in_=rounded)
             return codes, scales
 
         offsets = keep.tile([P, J // LIST_ROWS], U16, name="offsets")
         nc.sync.dma_start(offsets[:], offs)
+
+        zero = keep.tile([P, 1], F32, name="zero")
+        nc.vector.memset(zero[:], 0.0)
+        warm = keep.tile([P, 1], F32, name="warm")
+        nc.scalar.activation(out=warm[:], in_=zero[:], func=SILU)
 
         bias_rows = keep.tile([P, P], F32, name="bias_rows")
         nc.vector.memset(bias_rows[:], 0.0)
@@ -68,12 +75,12 @@ def tile_list_tiert_silu_kernel(tc, tab_words, tab_scales, wt, x, wx, b, offs, o
 
         ahead = keep.tile([P, K_PASS], BF16, name="ahead", align_bytes=64)
         nc.gpsimd.iota(ahead[:], [[1, K_PASS]], base=0, channel_multiplier=-PACK, allow_small_or_imprecise_dtypes=True)
-        ones = keep.tile([P, PACK, K_PASS], BF16, name="ones", align_bytes=64)
+        ones = keep.tile([P, PACK, K_PASS], BF16, name="ones", tag="raw_wx_1_1", align_bytes=DMA_ALIGN)
         for t in range(PACK):
             nc.vector.tensor_scalar(out=ones[:, t, :], in0=ahead[:], scalar1=float(t), scalar2=None, op0=ALU.is_equal)
-        ident_codes, ident_scales = quantize(ones[:].rearrange("p t w -> p (t w)"), "ident")
         unit = keep.tile([P, P], F32, name="unit")
         nc.vector.tensor_scalar(out=unit[:], in0=ahead[:, 0:K_PASS:PACK], scalar1=0.0, scalar2=None, op0=ALU.is_equal)
+        ident_codes, ident_scales = quantize(ones[:].rearrange("p t w -> p (t w)"), "ident")
 
         inputs = {"wt": wt, "wx": wx, "x": x}
         raw = {}
@@ -96,21 +103,15 @@ def tile_list_tiert_silu_kernel(tc, tab_words, tab_scales, wt, x, wx, b, offs, o
                     in_=tab_scales[:, r:16:4, :].rearrange("a q t -> q a t").bitcast(I32),
                 )
 
-        word_window = keep.tile([P, T], U32, name="word_window", align_bytes=DMA_ALIGN)
+        word_window = keep.tile([P, T], U32, name="word_window", tag="raw_wx_1_0", align_bytes=DMA_ALIGN)
 
         def load_words():
             nc.sync.dma_start(out=word_window[:].bitcast(I32), in_=tab_words[0].rearrange("p t z -> p (t z)").bitcast(I32))
 
-        def warm_up():
-            zero = keep.tile([P, 1], F32, name="zero")
-            nc.vector.memset(zero[:], 0.0)
-            warm = keep.tile([P, 1], F32, name="warm")
-            nc.scalar.activation(out=warm[:], in_=zero[:], func=SILU)
-
         tab_planes = {}
 
         def pick_scales():
-            tab_planes[0] = in_turn([P, J], U8, "picked_scales")
+            tab_planes[0] = vector_tile([P, J], U8, "picked_scales")
             nc.vector.tensor_copy(tab_planes[0][:], scale_window[:].indirect(offsets[:]))
 
         def move_scales():
@@ -133,22 +134,21 @@ def tile_list_tiert_silu_kernel(tc, tab_words, tab_scales, wt, x, wx, b, offs, o
         picked = {}
         tab_codes = {}
 
-        def pick_words(h):
-            picked[h] = in_turn([P, WIDTH], U32, "picked_%d" % h)[:]
-            entries = offsets[:, h * WIDTH // LIST_ROWS : (h + 1) * WIDTH // LIST_ROWS]
-            nc.vector.tensor_copy(picked[h], word_window[:].indirect(entries))
+        def pick_words(h, first=0, width=WIDTH):
+            if first == 0:
+                picked[h] = vector_tile([P, WIDTH], U32, "picked_%d" % h)[:]
+            start = h * WIDTH + first
+            entries = offsets[:, start // LIST_ROWS : (start + width) // LIST_ROWS]
+            nc.vector.tensor_copy(picked[h][:, first : first + width], word_window[:].indirect(entries))
 
         def part_words(h):
-            tab_codes[h] = in_turn([P, PASSES, 2 * WIDTH], U8, "parted_%d" % h)
+            tab_codes[h] = vector_tile([P, PASSES, 2 * WIDTH], U8, "parted_%d" % h)
             nc.vector.tensor_copy(out=tab_codes[h][:].bitcast(U16), in_=picked[h].bitcast(U16).rearrange("p (s a) -> p a s", a=PASSES))
 
         rounded = {}
 
         def round_chunk(name, i, a, s, engine):
-            if not rounded:
-                tile = in_turn([P, CHUNK * PACK], BF16, "first_rounded")
-            else:
-                tile = stage.tile([P, CHUNK * PACK], BF16, name="rounded", align_bytes=64)
+            tile = (vector_tile if engine == "V" else scalar_tile)([P, CHUNK * PACK], BF16, "rounded")
             source = by_runs(raw[name, i, a][:, :, s * CHUNK : (s + 1) * CHUNK])
             if engine == "V":
                 nc.vector.tensor_copy(out=woven(tile[:]), in_=source)
@@ -162,7 +162,7 @@ def tile_list_tiert_silu_kernel(tc, tab_words, tab_scales, wt, x, wx, b, offs, o
         def quantize_chunk(name, i, a, s):
             if name == "x":
                 if (i, a) not in tokens:
-                    codes = keep.tile([P, WIDTH], U32, name="x_%d_%d_codes" % (i, a), align_bytes=64)
+                    codes = vector_tile([P, WIDTH], U32, "x_%d_%d_codes" % (i, a))
                     scales = keep.tile([P, WIDTH], U8, name="x_%d_%d_scales" % (i, a), align_bytes=64)
                     tokens[i, a] = codes, scales
                 codes, scales = tokens[i, a]
@@ -173,23 +173,16 @@ def tile_list_tiert_silu_kernel(tc, tab_words, tab_scales, wt, x, wx, b, offs, o
                 c = i * CHUNKS + s
                 weights[operand, c, a] = quantize(rounded[name, i, a, s][:], "%s_%d_%d" % (operand, c, a))
 
-        def make(name, i, a, engines):
-            for s in range(CHUNKS):
-                round_chunk(name, i, a, s, engines[s])
-            for s in range(CHUNKS):
-                quantize_chunk(name, i, a, s)
-
+        backs = {}
         rests = {}
 
-        def subtract(c, a, u, i):
+        def bring_back(c, a, u, i):
             codes, scales = weights["wq", c, a]
-            if u == 0:
-                rests[c, a] = stage.tile([P, CHUNK * PACK], BF16, name="rest", bufs=REST_BUFS, align_bytes=64)
             cols = slice(u * P, (u + 1) * P)
-            back = bank(i, [P, PACK, P])
+            backs[c, a, u] = bank(i, [P, PACK, P])
             for t in range(PACK):
                 nc.tensor.matmul_mx(
-                    out=back[:, t, :],
+                    out=backs[c, a, u][:, t, :],
                     lhsT=ident_codes[:, t * P : (t + 1) * P].bitcast(FP8X4),
                     lhsT_scale=ident_scales[:, t * P : (t + 1) * P],
                     rhs=codes[:, cols].bitcast(FP8X4),
@@ -197,25 +190,20 @@ def tile_list_tiert_silu_kernel(tc, tab_words, tab_scales, wt, x, wx, b, offs, o
                     start=True,
                     stop=True,
                 )
+
+        def subtract(c, a, u):
+            if u == 0:
+                rests[c, a] = vector_tile([P, CHUNK * PACK], BF16, "rest")
             first = c % CHUNKS * CHUNK + u * P
             nc.vector.tensor_tensor(
                 out=woven(rests[c, a][:, u * P * PACK : (u + 1) * P * PACK]),
                 in0=by_runs(raw["wt", c // CHUNKS, a][:, :, first : first + P]),
-                in1=by_runs(back[:]),
+                in1=by_runs(backs[c, a, u][:]),
                 op=ALU.subtract,
             )
 
         def quantize_rest(c, a):
             weights["wr", c, a] = quantize(rests[c, a][:], "wr_%d_%d" % (c, a))
-
-        def tier(side, a, banks):
-            c = side * CHUNKS
-            subtract(c, a, 0, banks[0])
-            subtract(c, a, 1, banks[1 % len(banks)])
-            subtract(c + 1, a, 0, banks[2 % len(banks)])
-            quantize_rest(c, a)
-            subtract(c + 1, a, 1, banks[3 % len(banks)])
-            quantize_rest(c + 1, a)
 
         sums = {}
         done = {}
@@ -254,169 +242,274 @@ def tile_list_tiert_silu_kernel(tc, tab_words, tab_scales, wt, x, wx, b, offs, o
             add_pass(n, h * WIDTH + first, "wx", a, codes[:, cols].bitcast(FP8X4), scales[:, cols])
 
         def finish(n, h, first=0, width=WIDTH):
-            if n not in results:
-                results[n] = keep.tile([P, J], F32, name="result_%d" % n, align_bytes=DMA_ALIGN)
-            cols = slice(h * WIDTH + first, h * WIDTH + first + width)
-            nc.scalar.activation(out=results[n][:, cols], in_=sums[n, cols.start][:], func=SILU, bias=bias[:, n : n + 1])
+            start = h * WIDTH + first
+            results[n, start] = scalar_tile([P, width], F32, "result_%d" % n)
+            nc.scalar.activation(out=results[n, start][:], in_=sums[n, start][:], func=SILU, bias=bias[:, n : n + 1])
 
-        def store(n, first=0, width=J):
-            cols = slice(first, first + width)
-            nc.sync.dma_start(out=out[n * P : (n + 1) * P, cols], in_=results[n][:, cols])
+        def store(n, first, width):
+            nc.sync.dma_start(out=out[n * P : (n + 1) * P, first : first + width], in_=results[n, first][:])
 
         load_bias()
         load_scales()
         load_words()
         load("wt", (0,), 0)
         load("wt", (0,), 1)
-        warm_up()
         pick_scales()
+        load("wt", (1,), 0)
         move_scales()
-
-        def r(name, i, a, s, e):
-            round_chunk(name, i, a, s, e)
-        def q(name, i, a, s):
-            quantize_chunk(name, i, a, s)
-        def t(n, h, a, op):
-            table_pass(n, h, a, op)
-        for name, i, a in (("wt", 1, 0), ("x", 0, 0), ("wx", 0, 0), ("x", 0, 1), ("wx", 0, 1), ("wt", 1, 1), ("x", 1, 0), ("x", 1, 1), ("wx", 1, 0), ("wx", 1, 1)):
-            load(name, (i,), a)
+        load("x", (0,), 0)
+        load("wx", (0,), 0)
+        load("x", (0,), 1)
+        load("wx", (0,), 1)
+        load("wt", (1,), 1)
+        load("x", (1,), 0)
+        load("x", (1,), 1)
+        load("wx", (1,), 0)
+        load("wx", (1,), 1)
         turn_bias(7)
         pick_words(0)
-        pick_words(1)
-        r("wt", 0, 0, 0, "V")
-        r("wt", 0, 0, 1, "A")
-        for name, i, a in (("wt", 0, 1), ("wt", 1, 0), ("x", 0, 0), ("wx", 0, 0), ("x", 0, 1)):
-            for s in range(2):
-                r(name, i, a, s, "A")
-        r("wx", 0, 1, 0, "V")
-        r("wx", 0, 1, 1, "A")
+        pick_words(1, 0, 256)
+        round_chunk("wt", 0, 0, 0, "V")
         part_words(0)
-        q("wt", 0, 0, 0)
-        q("wt", 0, 0, 1)
+        quantize_chunk("wt", 0, 0, 0)
+        pick_words(1, 256, 256)
+        round_chunk("wt", 0, 0, 1, "A")
+        round_chunk("wt", 0, 1, 0, "A")
+        round_chunk("wt", 0, 1, 1, "A")
+        round_chunk("wt", 1, 0, 0, "A")
+        round_chunk("wt", 1, 0, 1, "A")
+        round_chunk("x", 0, 0, 0, "A")
+        round_chunk("x", 0, 0, 1, "A")
+        round_chunk("wx", 0, 0, 0, "A")
+        round_chunk("wx", 0, 0, 1, "A")
+        round_chunk("x", 0, 1, 0, "A")
+        round_chunk("x", 0, 1, 1, "A")
+        round_chunk("wx", 0, 1, 1, "A")
+        round_chunk("wt", 1, 1, 1, "A")
+        bring_back(0, 0, 0, 4)
+        bring_back(0, 0, 1, 5)
+        quantize_chunk("wt", 0, 0, 1)
         part_words(1)
-        subtract(0, 0, 0, 4)
-        subtract(0, 0, 1, 5)
-        q("wt", 0, 1, 0)
-        subtract(1, 0, 0, 6)
+        subtract(0, 0, 0)
+        subtract(0, 0, 1)
+        quantize_chunk("wt", 0, 1, 0)
+        bring_back(1, 0, 0, 6)
+        bring_back(1, 0, 1, 7)
+        open_sum(0, 0, 0, 0, 512)
+        table_pass(0, 0, 0, "wq", 0, 512)
+        open_sum(1, 0, 1, 0, 512)
+        table_pass(1, 0, 0, "wq", 0, 512)
+        open_sum(2, 0, 2, 0, 512)
+        table_pass(2, 0, 0, "wq", 0, 512)
+        open_sum(3, 0, 3, 0, 512)
+        table_pass(3, 0, 0, "wq", 0, 512)
+        bring_back(0, 1, 0, 4)
+        bring_back(0, 1, 1, 5)
+        subtract(1, 0, 0)
         quantize_rest(0, 0)
-        subtract(1, 0, 1, 7)
-        for n in range(4):
-            open_sum(n, 0, n)
-            t(n, 0, 0, "wq")
-        q("wt", 0, 1, 1)
-        subtract(0, 1, 0, 4)
+        subtract(1, 0, 1)
+        quantize_chunk("wt", 0, 1, 1)
+        subtract(0, 1, 0)
         quantize_rest(1, 0)
-        subtract(0, 1, 1, 5)
-        t(0, 0, 0, "wr")
-        t(1, 0, 0, "wr")
-        q("wt", 1, 0, 0)
-        subtract(1, 1, 0, 6)
+        subtract(0, 1, 1)
+        quantize_chunk("wt", 1, 0, 0)
+        table_pass(0, 0, 0, "wr", 0, 512)
+        table_pass(1, 0, 0, "wr", 0, 512)
+        bring_back(1, 1, 0, 6)
+        bring_back(1, 1, 1, 7)
+        table_pass(2, 0, 0, "wr", 0, 512)
+        table_pass(3, 0, 0, "wr", 0, 512)
+        table_pass(0, 0, 1, "wq", 0, 512)
+        table_pass(1, 0, 1, "wq", 0, 512)
+        table_pass(2, 0, 1, "wq", 0, 512)
+        table_pass(3, 0, 1, "wq", 0, 512)
+        bring_back(2, 0, 0, 5)
+        subtract(1, 1, 0)
         quantize_rest(0, 1)
-        subtract(1, 1, 1, 7)
-        t(2, 0, 0, "wr")
-        t(3, 0, 0, "wr")
-        for n in range(4):
-            t(n, 0, 1, "wq")
-        q("wt", 1, 0, 1)
-        subtract(2, 0, 0, 6)
+        subtract(1, 1, 1)
+        quantize_chunk("wt", 1, 0, 1)
+        subtract(2, 0, 0)
         quantize_rest(1, 1)
-        open_sum(0, 1, 4)
-        table_passes(0, 1, 0)
-        subtract(2, 0, 1, 7)
-        t(0, 0, 1, "wr")
-        t(1, 0, 1, "wr")
-        q("x", 0, 0, 0)
-        subtract(3, 0, 0, 6)
+        bring_back(2, 0, 1, 6)
+        table_pass(0, 0, 1, "wr", 0, 512)
+        table_pass(1, 0, 1, "wr", 0, 512)
+        bring_back(3, 0, 0, 7)
+        table_pass(2, 0, 1, "wr", 0, 512)
+        table_pass(3, 0, 1, "wr", 0, 512)
+        open_sum(0, 1, 4, 0, 512)
+        table_pass(0, 1, 0, "wq", 0, 512)
+        table_pass(0, 1, 0, "wr", 0, 512)
+        table_pass(0, 1, 1, "wq", 0, 512)
+        table_pass(0, 1, 1, "wr", 0, 512)
+        subtract(2, 0, 1)
+        quantize_chunk("x", 0, 0, 0)
+        quantize_chunk("x", 0, 0, 1)
+        quantize_chunk("wx", 0, 0, 0)
+        quantize_chunk("wx", 0, 0, 1)
+        subtract(3, 0, 0)
+        round_chunk("wx", 0, 1, 0, "V")
+        quantize_chunk("x", 0, 1, 0)
+        quantize_chunk("x", 0, 1, 1)
+        quantize_chunk("wx", 0, 1, 0)
+        quantize_chunk("wx", 0, 1, 1)
+        bring_back(3, 0, 1, 6)
+        open_sum(1, 1, 5, 0, 512)
+        table_pass(1, 1, 0, "wq", 0, 512)
+        table_pass(1, 1, 0, "wr", 0, 512)
+        table_pass(1, 1, 1, "wq", 0, 512)
+        table_pass(1, 1, 1, "wr", 0, 512)
+        x_pass(0, 0, 0, 0, 512)
+        x_pass(1, 0, 0, 0, 512)
+        x_pass(2, 0, 0, 0, 512)
+        x_pass(3, 0, 0, 0, 512)
+        x_pass(0, 0, 1, 0, 512)
+        x_pass(1, 0, 1, 0, 512)
+        x_pass(2, 0, 1, 0, 512)
+        x_pass(3, 0, 1, 0, 512)
+        open_sum(2, 1, 7, 0, 512)
+        table_pass(2, 1, 0, "wq", 0, 512)
+        table_pass(2, 1, 0, "wr", 0, 512)
+        table_pass(2, 1, 1, "wq", 0, 512)
+        table_pass(2, 1, 1, "wr", 0, 512)
+        subtract(3, 0, 1)
+        round_chunk("wt", 1, 1, 0, "V")
         quantize_rest(2, 0)
-        t(2, 0, 1, "wr")
-        t(3, 0, 1, "wr")
-        subtract(3, 0, 1, 7)
-        table_passes(0, 1, 1)
-        open_sum(1, 1, 5)
-        for a in range(2):
-            table_passes(1, 1, a)
-        q("x", 0, 0, 1)
-        q("wx", 0, 0, 0)
-        q("wx", 0, 0, 1)
+        quantize_chunk("wt", 1, 1, 0)
+        quantize_chunk("wt", 1, 1, 1)
         quantize_rest(3, 0)
-        q("x", 0, 1, 0)
-        q("x", 0, 1, 1)
-        open_sum(2, 1, 6)
-        for a in range(2):
-            table_passes(2, 1, a)
-        for n in range(4):
-            x_pass(n, 0, 0)
-        open_sum(3, 1, 7)
-        table_passes(3, 1, 0)
-        q("wx", 0, 1, 0)
-        q("wx", 0, 1, 1)
-        r("wt", 1, 1, 0, "V")
-        r("wt", 1, 1, 1, "V")
-        for n in range(4):
-            x_pass(n, 0, 1)
-            finish(n, 0)
-            store(n, 0, WIDTH)
-        table_passes(3, 1, 1)
-        q("wt", 1, 1, 0)
-        q("wt", 1, 1, 1)
-        r("x", 1, 0, 0, "A")
-        r("x", 1, 0, 1, "A")
-        r("x", 1, 1, 0, "A")
-        subtract(2, 1, 0, 1)
-        subtract(2, 1, 1, 2)
-        open_sum(4, 0, 0)
-        table_passes(4, 0, 0)
-        subtract(3, 1, 0, 1)
+        finish(0, 0, 0, 512)
+        store(0, 0, 512)
+        finish(1, 0, 0, 512)
+        store(1, 0, 512)
+        finish(2, 0, 0, 512)
+        store(2, 0, 512)
+        finish(3, 0, 0, 512)
+        store(3, 0, 512)
+        round_chunk("x", 1, 0, 0, "A")
+        round_chunk("x", 1, 0, 1, "A")
+        round_chunk("x", 1, 1, 0, "A")
+        round_chunk("wx", 1, 0, 1, "A")
+        bring_back(2, 1, 0, 0)
+        bring_back(2, 1, 1, 1)
+        open_sum(3, 1, 6, 0, 512)
+        table_pass(3, 1, 0, "wq", 0, 512)
+        table_pass(3, 1, 0, "wr", 0, 512)
+        table_pass(3, 1, 1, "wq", 0, 512)
+        table_pass(3, 1, 1, "wr", 0, 512)
+        subtract(2, 1, 0)
+        subtract(2, 1, 1)
         quantize_rest(2, 1)
-        open_sum(5, 0, 3)
-        table_passes(5, 0, 0)
-        subtract(3, 1, 1, 2)
-        q("x", 1, 0, 0)
-        q("x", 1, 0, 1)
-        r("x", 1, 1, 1, "V")
+        bring_back(3, 1, 0, 0)
+        bring_back(3, 1, 1, 1)
+        open_sum(4, 0, 2, 0, 512)
+        table_pass(4, 0, 0, "wq", 0, 512)
+        table_pass(4, 0, 0, "wr", 0, 512)
+        open_sum(5, 0, 3, 0, 512)
+        table_pass(5, 0, 0, "wq", 0, 512)
+        table_pass(5, 0, 0, "wr", 0, 512)
+        table_pass(4, 0, 1, "wq", 0, 512)
+        table_pass(5, 0, 1, "wq", 0, 512)
+        table_pass(4, 0, 1, "wr", 0, 512)
+        table_pass(5, 0, 1, "wr", 0, 512)
+        subtract(3, 1, 0)
+        quantize_chunk("x", 1, 0, 0)
+        subtract(3, 1, 1)
+        quantize_chunk("x", 1, 0, 1)
+        round_chunk("x", 1, 1, 1, "V")
         quantize_rest(3, 1)
-        table_passes(4, 0, 1)
-        table_passes(5, 0, 1)
-        open_sum(6, 0, 1)
-        table_passes(6, 0, 0)
-        for n in range(4):
-            x_pass(n, 1, 0)
-        q("x", 1, 1, 0)
-        q("x", 1, 1, 1)
-        r("wx", 1, 0, 0, "A")
-        r("wx", 1, 0, 1, "V")
-        for n in range(4):
-            x_pass(n, 1, 1)
-            finish(n, 1)
-            store(n, WIDTH, WIDTH)
-        q("wx", 1, 0, 0)
-        q("wx", 1, 0, 1)
-        r("wx", 1, 1, 0, "V")
-        r("wx", 1, 1, 1, "V")
-        q("wx", 1, 1, 0)
-        q("wx", 1, 1, 1)
-        table_passes(6, 0, 1)
-        open_sum(7, 0, 2)
-        for a in range(2):
-            table_passes(7, 0, a)
-        for n in range(4, 8):
-            for a in range(2):
-                x_pass(n, 0, a)
-            finish(n, 0)
-            store(n, 0, WIDTH)
-        for n in range(4, 7):
-            open_sum(n, 1, n)
-            for a in range(2):
-                table_passes(n, 1, a)
-            for a in range(2):
-                x_pass(n, 1, a)
-            finish(n, 1)
-            store(n, WIDTH, WIDTH)
-        for i, first in ((7, 0), (0, CHUNK)):
-            open_sum(7, 1, i, first, CHUNK)
-            for a in range(PASSES):
-                table_passes(7, 1, a, first, CHUNK)
-            for a in range(PASSES):
-                x_pass(7, 1, a, first, CHUNK)
-            finish(7, 1, first, CHUNK)
-            store(7, WIDTH + first, CHUNK)
+        quantize_chunk("x", 1, 1, 0)
+        quantize_chunk("x", 1, 1, 1)
+        round_chunk("wx", 1, 0, 0, "V")
+        quantize_chunk("wx", 1, 0, 1)
+        quantize_chunk("wx", 1, 0, 0)
+        round_chunk("wx", 1, 1, 0, "V")
+        round_chunk("wx", 1, 1, 1, "V")
+        quantize_chunk("wx", 1, 1, 0)
+        quantize_chunk("wx", 1, 1, 1)
+        x_pass(0, 1, 0, 0, 512)
+        x_pass(1, 1, 0, 0, 512)
+        x_pass(2, 1, 0, 0, 512)
+        x_pass(3, 1, 0, 0, 512)
+        x_pass(0, 1, 1, 0, 512)
+        x_pass(1, 1, 1, 0, 512)
+        x_pass(2, 1, 1, 0, 512)
+        x_pass(3, 1, 1, 0, 512)
+        open_sum(6, 0, 0, 0, 512)
+        table_pass(6, 0, 0, "wq", 0, 512)
+        table_pass(6, 0, 0, "wr", 0, 512)
+        table_pass(6, 0, 1, "wq", 0, 512)
+        table_pass(6, 0, 1, "wr", 0, 512)
+        open_sum(7, 0, 1, 0, 512)
+        table_pass(7, 0, 0, "wq", 0, 512)
+        table_pass(7, 0, 0, "wr", 0, 512)
+        table_pass(7, 0, 1, "wq", 0, 512)
+        table_pass(7, 0, 1, "wr", 0, 512)
+        x_pass(4, 0, 0, 0, 512)
+        x_pass(5, 0, 0, 0, 512)
+        x_pass(6, 0, 0, 0, 512)
+        x_pass(7, 0, 0, 0, 512)
+        x_pass(4, 0, 1, 0, 512)
+        x_pass(5, 0, 1, 0, 512)
+        x_pass(6, 0, 1, 0, 512)
+        x_pass(7, 0, 1, 0, 512)
+        finish(0, 1, 0, 512)
+        store(0, 512, 512)
+        finish(1, 1, 0, 512)
+        store(1, 512, 512)
+        finish(2, 1, 0, 512)
+        store(2, 512, 512)
+        finish(3, 1, 0, 512)
+        store(3, 512, 512)
+        finish(4, 0, 0, 512)
+        store(4, 0, 512)
+        finish(5, 0, 0, 512)
+        store(5, 0, 512)
+        finish(6, 0, 0, 512)
+        store(6, 0, 512)
+        finish(7, 0, 0, 512)
+        store(7, 0, 512)
+        open_sum(4, 1, 4, 0, 512)
+        table_pass(4, 1, 0, "wq", 0, 512)
+        table_pass(4, 1, 0, "wr", 0, 512)
+        table_pass(4, 1, 1, "wq", 0, 512)
+        table_pass(4, 1, 1, "wr", 0, 512)
+        x_pass(4, 1, 0, 0, 512)
+        x_pass(4, 1, 1, 0, 512)
+        open_sum(5, 1, 5, 0, 512)
+        table_pass(5, 1, 0, "wq", 0, 512)
+        table_pass(5, 1, 0, "wr", 0, 512)
+        table_pass(5, 1, 1, "wq", 0, 512)
+        table_pass(5, 1, 1, "wr", 0, 512)
+        x_pass(5, 1, 0, 0, 512)
+        x_pass(5, 1, 1, 0, 512)
+        open_sum(6, 1, 7, 0, 512)
+        table_pass(6, 1, 0, "wq", 0, 512)
+        table_pass(6, 1, 0, "wr", 0, 512)
+        table_pass(6, 1, 1, "wq", 0, 512)
+        table_pass(6, 1, 1, "wr", 0, 512)
+        x_pass(6, 1, 0, 0, 512)
+        x_pass(6, 1, 1, 0, 512)
+        open_sum(7, 1, 6, 0, 256)
+        table_pass(7, 1, 0, "wq", 0, 256)
+        table_pass(7, 1, 0, "wr", 0, 256)
+        table_pass(7, 1, 1, "wq", 0, 256)
+        table_pass(7, 1, 1, "wr", 0, 256)
+        x_pass(7, 1, 0, 0, 256)
+        x_pass(7, 1, 1, 0, 256)
+        open_sum(7, 1, 2, 256, 256)
+        table_pass(7, 1, 0, "wq", 256, 256)
+        table_pass(7, 1, 0, "wr", 256, 256)
+        table_pass(7, 1, 1, "wq", 256, 256)
+        table_pass(7, 1, 1, "wr", 256, 256)
+        x_pass(7, 1, 0, 256, 256)
+        x_pass(7, 1, 1, 256, 256)
+        finish(4, 1, 0, 512)
+        store(4, 512, 512)
+        finish(5, 1, 0, 512)
+        store(5, 512, 512)
+        finish(6, 1, 0, 512)
+        store(6, 512, 512)
+        finish(7, 1, 0, 256)
+        store(7, 512, 256)
+        finish(7, 1, 256, 256)
+        store(7, 768, 256)

@@ -28,7 +28,7 @@ RUN = 4
 DMA_ALIGN = 256
 LIST_ROWS = 16
 PASS_GAP = 16
-VECTOR_TILES = 49
+VECTOR_TILES = 42
 SCALAR_SLOTS = 16
 
 
@@ -39,7 +39,7 @@ def tile_list_tiert_silu_kernel(tc, tab_words, tab_scales, wt, x, wx, b, offs, o
         psum = ctx.enter_context(tc.psum_pool(name="psum", bufs=1))
 
         def bank(i, shape):
-            return psum.tile(shape, F32, name="bank_%d" % i)
+            return psum.tile(shape, F32, name="bank_%d" % i, tag="bank", bufs=8)
 
         def vector_tile(shape, dtype, name):
             return keep.tile(shape, dtype, name=name, tag="vector_turn", bufs=VECTOR_TILES, align_bytes=64)
@@ -49,7 +49,7 @@ def tile_list_tiert_silu_kernel(tc, tab_words, tab_scales, wt, x, wx, b, offs, o
 
         def quantize(rounded, name):
             width = rounded.shape[1] // PACK
-            if width == CHUNK:
+            if width < WIDTH:
                 both = vector_tile([P, (PACK + 1) * width], U8, name + "_codes")
                 codes, scales = both[:, 0 : PACK * width].bitcast(U32), both[:, PACK * width :]
             else:
@@ -75,7 +75,7 @@ def tile_list_tiert_silu_kernel(tc, tab_words, tab_scales, wt, x, wx, b, offs, o
 
         ahead = keep.tile([P, K_PASS], BF16, name="ahead", align_bytes=64)
         nc.gpsimd.iota(ahead[:], [[1, K_PASS]], base=0, channel_multiplier=-PACK, allow_small_or_imprecise_dtypes=True)
-        ones = keep.tile([P, PACK, K_PASS], BF16, name="ones", tag="raw_wx_1_1", align_bytes=DMA_ALIGN)
+        ones = keep.tile([P, PACK, K_PASS], BF16, name="ones", tag="raw_wx_4_1", align_bytes=DMA_ALIGN)
         for t in range(PACK):
             nc.vector.tensor_scalar(out=ones[:, t, :], in0=ahead[:], scalar1=float(t), scalar2=None, op0=ALU.is_equal)
         unit = keep.tile([P, P], F32, name="unit")
@@ -85,13 +85,16 @@ def tile_list_tiert_silu_kernel(tc, tab_words, tab_scales, wt, x, wx, b, offs, o
         inputs = {"wt": wt, "wx": wx, "x": x}
         raw = {}
 
-        def load(name, sides, a):
-            first, width = sides[0] * WIDTH, len(sides) * WIDTH
-            tile = keep.tile([P, PACK, width], F32, name="raw_%s_%d_%d" % (name, sides[0], a), align_bytes=DMA_ALIGN)
-            rows = inputs[name][a * K_PASS : (a + 1) * K_PASS, first : first + width]
+        def load(name, a, first, count):
+            tile = keep.tile([P, PACK, count * P], F32, name="raw_%s_%d_%d" % (name, first, a), align_bytes=DMA_ALIGN)
+            rows = inputs[name][a * K_PASS : (a + 1) * K_PASS, first * P : (first + count) * P]
             nc.sync.dma_start(out=tile[:], in_=rows.rearrange("(p t) w -> p t w", t=PACK))
-            for i in sides:
-                raw[name, i, a] = tile[:, :, i * WIDTH - first : (i + 1) * WIDTH - first]
+            for g in range(count):
+                raw[name, a, first + g] = tile, g
+
+        def raw_columns(name, a, first, count):
+            tile, g = raw[name, a, first]
+            return tile[:, :, g * P : (g + count) * P]
 
         def load_bias():
             nc.sync.dma_start(out=bias_rows[0 : N // P, :], in_=b.rearrange("(c p) -> c p", p=P))
@@ -103,7 +106,7 @@ def tile_list_tiert_silu_kernel(tc, tab_words, tab_scales, wt, x, wx, b, offs, o
                     in_=tab_scales[:, r:16:4, :].rearrange("a q t -> q a t").bitcast(I32),
                 )
 
-        word_window = keep.tile([P, T], U32, name="word_window", tag="raw_wx_1_0", align_bytes=DMA_ALIGN)
+        word_window = keep.tile([P, T], U32, name="word_window", tag="raw_wx_4_0", align_bytes=DMA_ALIGN)
 
         def load_words():
             nc.sync.dma_start(out=word_window[:].bitcast(I32), in_=tab_words[0].rearrange("p t z -> p (t z)").bitcast(I32))
@@ -147,75 +150,75 @@ def tile_list_tiert_silu_kernel(tc, tab_words, tab_scales, wt, x, wx, b, offs, o
 
         rounded = {}
 
-        def round_chunk(name, i, a, s, engine):
-            tile = (vector_tile if engine == "V" else scalar_tile)([P, CHUNK * PACK], BF16, "rounded")
-            source = by_runs(raw[name, i, a][:, :, s * CHUNK : (s + 1) * CHUNK])
+        def round_columns(name, a, first, count, engine):
+            tile = (vector_tile if engine == "V" else scalar_tile)([P, count * P * PACK], BF16, "rounded")
+            source = by_runs(raw_columns(name, a, first, count))
             if engine == "V":
                 nc.vector.tensor_copy(out=woven(tile[:]), in_=source)
             else:
                 nc.scalar.copy(out=woven(tile[:]), in_=source)
-            rounded[name, i, a, s] = tile
+            for g in range(count):
+                rounded[name, a, first + g] = tile, g
 
         weights = {}
         tokens = {}
 
-        def quantize_chunk(name, i, a, s):
+        def quantize_columns(name, a, first, count):
+            tile, g = rounded[name, a, first]
+            source = tile[:, g * P * PACK : (g + count) * P * PACK]
             if name == "x":
-                if (i, a) not in tokens:
-                    codes = vector_tile([P, WIDTH], U32, "x_%d_%d_codes" % (i, a))
-                    scales = keep.tile([P, WIDTH], U8, name="x_%d_%d_scales" % (i, a), align_bytes=64)
-                    tokens[i, a] = codes, scales
-                codes, scales = tokens[i, a]
-                cols = slice(s * CHUNK, (s + 1) * CHUNK)
-                nc.vector.quantize_mx(out=codes[:, cols].bitcast(FP8X4), scales=scales[:, cols], in_=rounded[name, i, a, s][:])
+                h, start = divmod(first * P, WIDTH)
+                if (h, a) not in tokens:
+                    codes = vector_tile([P, WIDTH], U32, "x_%d_%d_codes" % (h, a))
+                    scales = keep.tile([P, WIDTH], U8, name="x_%d_%d_scales" % (h, a), align_bytes=64)
+                    tokens[h, a] = codes, scales
+                codes, scales = tokens[h, a]
+                cols = slice(start, start + count * P)
+                nc.vector.quantize_mx(out=codes[:, cols].bitcast(FP8X4), scales=scales[:, cols], in_=source)
             else:
-                operand = "wq" if name == "wt" else name
-                c = i * CHUNKS + s
-                weights[operand, c, a] = quantize(rounded[name, i, a, s][:], "%s_%d_%d" % (operand, c, a))
+                codes, scales = quantize(source, "%s_%d_%d" % (name, first, a))
+                for g in range(count):
+                    weights[name, first + g, a] = codes[:, g * P : (g + 1) * P], scales[:, g * P : (g + 1) * P]
 
         backs = {}
-        rests = {}
 
-        def bring_back(c, a, u, i):
-            codes, scales = weights["wq", c, a]
-            cols = slice(u * P, (u + 1) * P)
-            backs[c, a, u] = bank(i, [P, PACK, P])
+        def bring_back(n, a, i):
+            codes, scales = weights["wt", n, a]
+            backs[n, a] = bank(i, [P, PACK, P])
             for t in range(PACK):
                 nc.tensor.matmul_mx(
-                    out=backs[c, a, u][:, t, :],
+                    out=backs[n, a][:, t, :],
                     lhsT=ident_codes[:, t * P : (t + 1) * P].bitcast(FP8X4),
                     lhsT_scale=ident_scales[:, t * P : (t + 1) * P],
-                    rhs=codes[:, cols].bitcast(FP8X4),
-                    rhs_scale=scales[:, cols],
+                    rhs=codes.bitcast(FP8X4),
+                    rhs_scale=scales,
                     start=True,
                     stop=True,
                 )
 
-        def subtract(c, a, u):
-            if u == 0:
-                rests[c, a] = vector_tile([P, CHUNK * PACK], BF16, "rest")
-            first = c % CHUNKS * CHUNK + u * P
+        def subtract(n, a, count):
+            if count:
+                tile = vector_tile([P, count * P * PACK], BF16, "rest")
+                for g in range(count):
+                    rounded["wr", a, n + g] = tile, g
+            tile, g = rounded["wr", a, n]
             nc.vector.tensor_tensor(
-                out=woven(rests[c, a][:, u * P * PACK : (u + 1) * P * PACK]),
-                in0=by_runs(raw["wt", c // CHUNKS, a][:, :, first : first + P]),
-                in1=by_runs(backs[c, a, u][:]),
+                out=woven(tile[:, g * P * PACK : (g + 1) * P * PACK]),
+                in0=by_runs(raw_columns("wt", a, n, 1)),
+                in1=by_runs(backs[n, a][:]),
                 op=ALU.subtract,
             )
-
-        def quantize_rest(c, a):
-            weights["wr", c, a] = quantize(rests[c, a][:], "wr_%d_%d" % (c, a))
 
         sums = {}
         done = {}
         results = {}
 
         def add_pass(n, first, operand, a, rhs, rhs_scale):
-            codes, scales = weights[operand, n // TILES, a]
-            cols = slice(n % TILES * P, (n % TILES + 1) * P)
+            codes, scales = weights[operand, n, a]
             nc.tensor.matmul_mx(
                 out=sums[n, first][:],
-                lhsT=codes[:, cols].bitcast(FP8X4),
-                lhsT_scale=scales[:, cols],
+                lhsT=codes.bitcast(FP8X4),
+                lhsT_scale=scales,
                 rhs=rhs,
                 rhs_scale=rhs_scale,
                 start=done[n, first] == 0,
@@ -233,7 +236,7 @@ def tile_list_tiert_silu_kernel(tc, tab_words, tab_scales, wt, x, wx, b, offs, o
             add_pass(n, h * WIDTH + first, operand, a, rhs, plane)
 
         def table_passes(n, h, a, first=0, width=WIDTH):
-            for operand in ("wq", "wr"):
+            for operand in ("wt", "wr"):
                 table_pass(n, h, a, operand, first, width)
 
         def x_pass(n, h, a, first=0, width=WIDTH):
@@ -252,111 +255,109 @@ def tile_list_tiert_silu_kernel(tc, tab_words, tab_scales, wt, x, wx, b, offs, o
         load_bias()
         load_scales()
         load_words()
-        load("wt", (0,), 0)
-        load("wt", (0,), 1)
+        load("wt", 0, 0, 4)
+        load("wt", 1, 0, 4)
         pick_scales()
-        load("wt", (1,), 0)
+        load("wt", 0, 4, 4)
         move_scales()
-        load("x", (0,), 0)
-        load("wx", (0,), 0)
-        load("x", (0,), 1)
-        load("wx", (0,), 1)
-        load("wt", (1,), 1)
-        load("x", (1,), 0)
-        load("x", (1,), 1)
-        load("wx", (1,), 0)
-        load("wx", (1,), 1)
+        load("x", 0, 0, 4)
+        load("wx", 0, 0, 4)
+        load("x", 1, 0, 4)
+        load("wx", 1, 0, 4)
+        load("wt", 1, 4, 4)
+        load("x", 0, 4, 4)
+        load("x", 1, 4, 4)
+        load("wx", 0, 4, 4)
+        load("wx", 1, 4, 4)
         turn_bias(7)
         pick_words(0)
-        pick_words(1, 0, 256)
-        round_chunk("wt", 0, 0, 0, "V")
+        pick_words(1)
+        round_columns("wt", 0, 0, 2, "V")
         part_words(0)
-        quantize_chunk("wt", 0, 0, 0)
-        pick_words(1, 256, 256)
-        round_chunk("wt", 0, 0, 1, "A")
-        round_chunk("wt", 0, 1, 0, "A")
-        round_chunk("wt", 0, 1, 1, "A")
-        round_chunk("wt", 1, 0, 0, "A")
-        round_chunk("wt", 1, 0, 1, "A")
-        round_chunk("x", 0, 0, 0, "A")
-        round_chunk("x", 0, 0, 1, "A")
-        round_chunk("wx", 0, 0, 0, "A")
-        round_chunk("wx", 0, 0, 1, "A")
-        round_chunk("x", 0, 1, 0, "A")
-        round_chunk("x", 0, 1, 1, "A")
-        round_chunk("wx", 0, 1, 1, "A")
-        round_chunk("wt", 1, 1, 1, "A")
-        bring_back(0, 0, 0, 4)
-        bring_back(0, 0, 1, 5)
-        quantize_chunk("wt", 0, 0, 1)
+        quantize_columns("wt", 0, 0, 2)
+        round_columns("wt", 0, 2, 2, "A")
+        round_columns("wt", 1, 0, 2, "A")
+        round_columns("wt", 1, 2, 2, "A")
+        round_columns("wt", 0, 4, 2, "A")
+        round_columns("wt", 0, 6, 2, "A")
+        round_columns("x", 0, 0, 2, "A")
+        round_columns("x", 0, 2, 2, "A")
+        round_columns("wx", 0, 0, 2, "A")
+        round_columns("wx", 0, 2, 2, "A")
+        round_columns("x", 1, 0, 2, "A")
+        round_columns("wx", 1, 2, 2, "A")
+        bring_back(0, 0, 4)
+        bring_back(1, 0, 5)
+        quantize_columns("wt", 0, 2, 2)
         part_words(1)
-        subtract(0, 0, 0)
-        subtract(0, 0, 1)
-        quantize_chunk("wt", 0, 1, 0)
-        bring_back(1, 0, 0, 6)
-        bring_back(1, 0, 1, 7)
-        open_sum(0, 0, 0, 0, 512)
-        table_pass(0, 0, 0, "wq", 0, 512)
-        open_sum(1, 0, 1, 0, 512)
-        table_pass(1, 0, 0, "wq", 0, 512)
-        open_sum(2, 0, 2, 0, 512)
-        table_pass(2, 0, 0, "wq", 0, 512)
-        open_sum(3, 0, 3, 0, 512)
-        table_pass(3, 0, 0, "wq", 0, 512)
-        bring_back(0, 1, 0, 4)
-        bring_back(0, 1, 1, 5)
+        subtract(0, 0, 2)
         subtract(1, 0, 0)
-        quantize_rest(0, 0)
-        subtract(1, 0, 1)
-        quantize_chunk("wt", 0, 1, 1)
-        subtract(0, 1, 0)
-        quantize_rest(1, 0)
-        subtract(0, 1, 1)
-        quantize_chunk("wt", 1, 0, 0)
+        quantize_columns("wt", 1, 0, 2)
+        bring_back(2, 0, 6)
+        bring_back(3, 0, 7)
+        open_sum(0, 0, 0, 0, 512)
+        table_pass(0, 0, 0, "wt", 0, 512)
+        open_sum(1, 0, 1, 0, 512)
+        table_pass(1, 0, 0, "wt", 0, 512)
+        open_sum(2, 0, 2, 0, 512)
+        table_pass(2, 0, 0, "wt", 0, 512)
+        open_sum(3, 0, 3, 0, 512)
+        table_pass(3, 0, 0, "wt", 0, 512)
+        bring_back(0, 1, 4)
+        bring_back(1, 1, 5)
+        subtract(2, 0, 2)
+        quantize_columns("wr", 0, 0, 2)
+        subtract(3, 0, 0)
+        quantize_columns("wt", 1, 2, 2)
+        subtract(0, 1, 2)
+        quantize_columns("wr", 0, 2, 2)
+        subtract(1, 1, 0)
+        quantize_columns("wt", 0, 4, 2)
         table_pass(0, 0, 0, "wr", 0, 512)
         table_pass(1, 0, 0, "wr", 0, 512)
-        bring_back(1, 1, 0, 6)
-        bring_back(1, 1, 1, 7)
+        bring_back(2, 1, 6)
+        bring_back(3, 1, 7)
+        table_pass(0, 0, 1, "wt", 0, 512)
+        table_pass(1, 0, 1, "wt", 0, 512)
         table_pass(2, 0, 0, "wr", 0, 512)
         table_pass(3, 0, 0, "wr", 0, 512)
-        table_pass(0, 0, 1, "wq", 0, 512)
-        table_pass(1, 0, 1, "wq", 0, 512)
-        table_pass(2, 0, 1, "wq", 0, 512)
-        table_pass(3, 0, 1, "wq", 0, 512)
-        bring_back(2, 0, 0, 5)
-        subtract(1, 1, 0)
-        quantize_rest(0, 1)
-        subtract(1, 1, 1)
-        quantize_chunk("wt", 1, 0, 1)
-        subtract(2, 0, 0)
-        quantize_rest(1, 1)
-        bring_back(2, 0, 1, 6)
+        open_sum(0, 1, 4, 0, 512)
+        table_pass(0, 1, 0, "wt", 0, 512)
+        table_pass(2, 0, 1, "wt", 0, 512)
+        table_pass(3, 0, 1, "wt", 0, 512)
+        bring_back(4, 0, 5)
+        subtract(2, 1, 2)
+        quantize_columns("wr", 1, 0, 2)
+        subtract(3, 1, 0)
+        quantize_columns("wt", 0, 6, 2)
+        subtract(4, 0, 2)
+        quantize_columns("wr", 1, 2, 2)
+        bring_back(5, 0, 6)
         table_pass(0, 0, 1, "wr", 0, 512)
         table_pass(1, 0, 1, "wr", 0, 512)
-        bring_back(3, 0, 0, 7)
+        table_pass(0, 1, 0, "wr", 0, 512)
+        bring_back(6, 0, 7)
+        table_pass(0, 1, 1, "wt", 0, 512)
+        table_pass(0, 1, 1, "wr", 0, 512)
         table_pass(2, 0, 1, "wr", 0, 512)
         table_pass(3, 0, 1, "wr", 0, 512)
-        open_sum(0, 1, 4, 0, 512)
-        table_pass(0, 1, 0, "wq", 0, 512)
-        table_pass(0, 1, 0, "wr", 0, 512)
-        table_pass(0, 1, 1, "wq", 0, 512)
-        table_pass(0, 1, 1, "wr", 0, 512)
-        subtract(2, 0, 1)
-        quantize_chunk("x", 0, 0, 0)
-        quantize_chunk("x", 0, 0, 1)
-        quantize_chunk("wx", 0, 0, 0)
-        quantize_chunk("wx", 0, 0, 1)
-        subtract(3, 0, 0)
-        round_chunk("wx", 0, 1, 0, "V")
-        quantize_chunk("x", 0, 1, 0)
-        quantize_chunk("x", 0, 1, 1)
-        quantize_chunk("wx", 0, 1, 0)
-        quantize_chunk("wx", 0, 1, 1)
-        bring_back(3, 0, 1, 6)
         open_sum(1, 1, 5, 0, 512)
-        table_pass(1, 1, 0, "wq", 0, 512)
+        table_pass(1, 1, 0, "wt", 0, 512)
+        subtract(5, 0, 0)
+        quantize_columns("x", 0, 0, 2)
+        quantize_columns("x", 0, 2, 2)
+        subtract(6, 0, 1)
+        round_columns("x", 1, 2, 2, "V")
+        quantize_columns("wx", 0, 0, 2)
+        quantize_columns("wx", 0, 2, 2)
+        round_columns("wx", 1, 0, 2, "V")
+        quantize_columns("x", 1, 2, 2)
+        quantize_columns("x", 1, 0, 2)
+        quantize_columns("wx", 1, 0, 2)
+        quantize_columns("wx", 1, 2, 2)
+        bring_back(7, 0, 6)
         table_pass(1, 1, 0, "wr", 0, 512)
-        table_pass(1, 1, 1, "wq", 0, 512)
+        table_pass(1, 1, 1, "wt", 0, 512)
         table_pass(1, 1, 1, "wr", 0, 512)
         x_pass(0, 0, 0, 0, 512)
         x_pass(1, 0, 0, 0, 512)
@@ -367,16 +368,18 @@ def tile_list_tiert_silu_kernel(tc, tab_words, tab_scales, wt, x, wx, b, offs, o
         x_pass(2, 0, 1, 0, 512)
         x_pass(3, 0, 1, 0, 512)
         open_sum(2, 1, 7, 0, 512)
-        table_pass(2, 1, 0, "wq", 0, 512)
+        table_pass(2, 1, 0, "wt", 0, 512)
         table_pass(2, 1, 0, "wr", 0, 512)
-        table_pass(2, 1, 1, "wq", 0, 512)
+        table_pass(2, 1, 1, "wt", 0, 512)
         table_pass(2, 1, 1, "wr", 0, 512)
-        subtract(3, 0, 1)
-        round_chunk("wt", 1, 1, 0, "V")
-        quantize_rest(2, 0)
-        quantize_chunk("wt", 1, 1, 0)
-        quantize_chunk("wt", 1, 1, 1)
-        quantize_rest(3, 0)
+        subtract(7, 0, 1)
+        round_columns("wt", 1, 4, 2, "V")
+        quantize_columns("wr", 0, 4, 2)
+        quantize_columns("wt", 1, 4, 2)
+        round_columns("wt", 1, 6, 2, "V")
+        quantize_columns("wr", 0, 6, 1)
+        quantize_columns("wt", 1, 6, 2)
+        quantize_columns("wr", 0, 7, 1)
         finish(0, 0, 0, 512)
         store(0, 0, 512)
         finish(1, 0, 0, 512)
@@ -385,47 +388,47 @@ def tile_list_tiert_silu_kernel(tc, tab_words, tab_scales, wt, x, wx, b, offs, o
         store(2, 0, 512)
         finish(3, 0, 0, 512)
         store(3, 0, 512)
-        round_chunk("x", 1, 0, 0, "A")
-        round_chunk("x", 1, 0, 1, "A")
-        round_chunk("x", 1, 1, 0, "A")
-        round_chunk("wx", 1, 0, 1, "A")
-        bring_back(2, 1, 0, 0)
-        bring_back(2, 1, 1, 1)
+        round_columns("x", 0, 4, 2, "A")
+        round_columns("x", 0, 6, 2, "A")
+        round_columns("x", 1, 4, 2, "A")
+        round_columns("wx", 0, 6, 2, "A")
         open_sum(3, 1, 6, 0, 512)
-        table_pass(3, 1, 0, "wq", 0, 512)
+        table_pass(3, 1, 0, "wt", 0, 512)
         table_pass(3, 1, 0, "wr", 0, 512)
-        table_pass(3, 1, 1, "wq", 0, 512)
+        table_pass(3, 1, 1, "wt", 0, 512)
         table_pass(3, 1, 1, "wr", 0, 512)
-        subtract(2, 1, 0)
-        subtract(2, 1, 1)
-        quantize_rest(2, 1)
-        bring_back(3, 1, 0, 0)
-        bring_back(3, 1, 1, 1)
+        bring_back(4, 1, 0)
+        bring_back(5, 1, 1)
         open_sum(4, 0, 2, 0, 512)
-        table_pass(4, 0, 0, "wq", 0, 512)
+        table_pass(4, 0, 0, "wt", 0, 512)
         table_pass(4, 0, 0, "wr", 0, 512)
         open_sum(5, 0, 3, 0, 512)
-        table_pass(5, 0, 0, "wq", 0, 512)
+        table_pass(5, 0, 0, "wt", 0, 512)
         table_pass(5, 0, 0, "wr", 0, 512)
-        table_pass(4, 0, 1, "wq", 0, 512)
-        table_pass(5, 0, 1, "wq", 0, 512)
+        subtract(4, 1, 2)
+        subtract(5, 1, 0)
+        quantize_columns("wr", 1, 4, 2)
+        bring_back(6, 1, 0)
+        bring_back(7, 1, 1)
+        table_pass(4, 0, 1, "wt", 0, 512)
+        table_pass(5, 0, 1, "wt", 0, 512)
         table_pass(4, 0, 1, "wr", 0, 512)
         table_pass(5, 0, 1, "wr", 0, 512)
-        subtract(3, 1, 0)
-        quantize_chunk("x", 1, 0, 0)
-        subtract(3, 1, 1)
-        quantize_chunk("x", 1, 0, 1)
-        round_chunk("x", 1, 1, 1, "V")
-        quantize_rest(3, 1)
-        quantize_chunk("x", 1, 1, 0)
-        quantize_chunk("x", 1, 1, 1)
-        round_chunk("wx", 1, 0, 0, "V")
-        quantize_chunk("wx", 1, 0, 1)
-        quantize_chunk("wx", 1, 0, 0)
-        round_chunk("wx", 1, 1, 0, "V")
-        round_chunk("wx", 1, 1, 1, "V")
-        quantize_chunk("wx", 1, 1, 0)
-        quantize_chunk("wx", 1, 1, 1)
+        subtract(6, 1, 2)
+        quantize_columns("x", 0, 4, 2)
+        subtract(7, 1, 0)
+        quantize_columns("x", 0, 6, 2)
+        round_columns("x", 1, 6, 2, "V")
+        quantize_columns("wr", 1, 6, 2)
+        quantize_columns("x", 1, 4, 2)
+        quantize_columns("x", 1, 6, 2)
+        round_columns("wx", 0, 4, 2, "V")
+        quantize_columns("wx", 0, 6, 2)
+        quantize_columns("wx", 0, 4, 2)
+        round_columns("wx", 1, 4, 2, "V")
+        round_columns("wx", 1, 6, 2, "V")
+        quantize_columns("wx", 1, 4, 2)
+        quantize_columns("wx", 1, 6, 2)
         x_pass(0, 1, 0, 0, 512)
         x_pass(1, 1, 0, 0, 512)
         x_pass(2, 1, 0, 0, 512)
@@ -435,14 +438,14 @@ def tile_list_tiert_silu_kernel(tc, tab_words, tab_scales, wt, x, wx, b, offs, o
         x_pass(2, 1, 1, 0, 512)
         x_pass(3, 1, 1, 0, 512)
         open_sum(6, 0, 0, 0, 512)
-        table_pass(6, 0, 0, "wq", 0, 512)
+        table_pass(6, 0, 0, "wt", 0, 512)
         table_pass(6, 0, 0, "wr", 0, 512)
-        table_pass(6, 0, 1, "wq", 0, 512)
+        table_pass(6, 0, 1, "wt", 0, 512)
         table_pass(6, 0, 1, "wr", 0, 512)
         open_sum(7, 0, 1, 0, 512)
-        table_pass(7, 0, 0, "wq", 0, 512)
+        table_pass(7, 0, 0, "wt", 0, 512)
         table_pass(7, 0, 0, "wr", 0, 512)
-        table_pass(7, 0, 1, "wq", 0, 512)
+        table_pass(7, 0, 1, "wt", 0, 512)
         table_pass(7, 0, 1, "wr", 0, 512)
         x_pass(4, 0, 0, 0, 512)
         x_pass(5, 0, 0, 0, 512)
@@ -469,40 +472,47 @@ def tile_list_tiert_silu_kernel(tc, tab_words, tab_scales, wt, x, wx, b, offs, o
         finish(7, 0, 0, 512)
         store(7, 0, 512)
         open_sum(4, 1, 4, 0, 512)
-        table_pass(4, 1, 0, "wq", 0, 512)
+        table_pass(4, 1, 0, "wt", 0, 512)
         table_pass(4, 1, 0, "wr", 0, 512)
-        table_pass(4, 1, 1, "wq", 0, 512)
+        table_pass(4, 1, 1, "wt", 0, 512)
         table_pass(4, 1, 1, "wr", 0, 512)
         x_pass(4, 1, 0, 0, 512)
         x_pass(4, 1, 1, 0, 512)
         open_sum(5, 1, 5, 0, 512)
-        table_pass(5, 1, 0, "wq", 0, 512)
+        table_pass(5, 1, 0, "wt", 0, 512)
         table_pass(5, 1, 0, "wr", 0, 512)
-        table_pass(5, 1, 1, "wq", 0, 512)
+        table_pass(5, 1, 1, "wt", 0, 512)
         table_pass(5, 1, 1, "wr", 0, 512)
         x_pass(5, 1, 0, 0, 512)
         x_pass(5, 1, 1, 0, 512)
         open_sum(6, 1, 7, 0, 512)
-        table_pass(6, 1, 0, "wq", 0, 512)
+        table_pass(6, 1, 0, "wt", 0, 512)
         table_pass(6, 1, 0, "wr", 0, 512)
-        table_pass(6, 1, 1, "wq", 0, 512)
+        table_pass(6, 1, 1, "wt", 0, 512)
         table_pass(6, 1, 1, "wr", 0, 512)
         x_pass(6, 1, 0, 0, 512)
         x_pass(6, 1, 1, 0, 512)
         open_sum(7, 1, 6, 0, 256)
-        table_pass(7, 1, 0, "wq", 0, 256)
+        table_pass(7, 1, 0, "wt", 0, 256)
         table_pass(7, 1, 0, "wr", 0, 256)
-        table_pass(7, 1, 1, "wq", 0, 256)
+        table_pass(7, 1, 1, "wt", 0, 256)
         table_pass(7, 1, 1, "wr", 0, 256)
         x_pass(7, 1, 0, 0, 256)
         x_pass(7, 1, 1, 0, 256)
-        open_sum(7, 1, 2, 256, 256)
-        table_pass(7, 1, 0, "wq", 256, 256)
-        table_pass(7, 1, 0, "wr", 256, 256)
-        table_pass(7, 1, 1, "wq", 256, 256)
-        table_pass(7, 1, 1, "wr", 256, 256)
-        x_pass(7, 1, 0, 256, 256)
-        x_pass(7, 1, 1, 256, 256)
+        open_sum(7, 1, 2, 256, 128)
+        table_pass(7, 1, 0, "wt", 256, 128)
+        table_pass(7, 1, 0, "wr", 256, 128)
+        table_pass(7, 1, 1, "wt", 256, 128)
+        table_pass(7, 1, 1, "wr", 256, 128)
+        x_pass(7, 1, 0, 256, 128)
+        x_pass(7, 1, 1, 256, 128)
+        open_sum(7, 1, 3, 384, 128)
+        table_pass(7, 1, 0, "wt", 384, 128)
+        table_pass(7, 1, 0, "wr", 384, 128)
+        table_pass(7, 1, 1, "wt", 384, 128)
+        table_pass(7, 1, 1, "wr", 384, 128)
+        x_pass(7, 1, 0, 384, 128)
+        x_pass(7, 1, 1, 384, 128)
         finish(4, 1, 0, 512)
         store(4, 512, 512)
         finish(5, 1, 0, 512)
@@ -511,5 +521,7 @@ def tile_list_tiert_silu_kernel(tc, tab_words, tab_scales, wt, x, wx, b, offs, o
         store(6, 512, 512)
         finish(7, 1, 0, 256)
         store(7, 512, 256)
-        finish(7, 1, 256, 256)
-        store(7, 768, 256)
+        finish(7, 1, 256, 128)
+        store(7, 768, 128)
+        finish(7, 1, 384, 128)
+        store(7, 896, 128)

@@ -28,8 +28,8 @@ RUN = 4
 DMA_ALIGN = 256
 LIST_ROWS = 16
 PASS_GAP = 16
-VECTOR_TILES = 42
-SCALAR_SLOTS = 16
+VECTOR_TILES = 43
+SCALAR_SLOTS = 17
 
 
 def tile_list_tiert_silu_kernel(tc, tab_words, tab_scales, wt, x, wx, b, offs, out):
@@ -78,9 +78,10 @@ def tile_list_tiert_silu_kernel(tc, tab_words, tab_scales, wt, x, wx, b, offs, o
         ones = keep.tile([P, PACK, K_PASS], BF16, name="ones", tag="raw_wx_4_1", align_bytes=DMA_ALIGN)
         for t in range(PACK):
             nc.vector.tensor_scalar(out=ones[:, t, :], in0=ahead[:], scalar1=float(t), scalar2=None, op0=ALU.is_equal)
-        unit = keep.tile([P, P], F32, name="unit")
-        nc.vector.tensor_scalar(out=unit[:], in0=ahead[:, 0:K_PASS:PACK], scalar1=0.0, scalar2=None, op0=ALU.is_equal)
-        ident_codes, ident_scales = quantize(ones[:].rearrange("p t w -> p (t w)"), "ident")
+        ident = []
+
+        def quantize_identity():
+            ident.extend(quantize(ones[:].rearrange("p t w -> p (t w)"), "ident"))
 
         inputs = {"wt": wt, "wx": wx, "x": x}
         raw = {}
@@ -118,15 +119,23 @@ def tile_list_tiert_silu_kernel(tc, tab_words, tab_scales, wt, x, wx, b, offs, o
             nc.vector.tensor_copy(tab_planes[0][:], scale_window[:].indirect(offsets[:]))
 
         def move_scales():
-            nc.sync.dma_start(out=moved_scales[0 : P - PASS_GAP, :].bitcast(I32), in_=tab_planes[0][PASS_GAP:P, :].bitcast(I32))
+            for r in range(4):
+                nc.sync.dma_start(out=moved_scales[r:P:32, :].bitcast(I32), in_=tab_planes[0][PASS_GAP + r : P : 32, :].bitcast(I32))
             tab_planes[1] = moved_scales
 
-        bias = keep.tile([P, N // P], F32, name="bias")
+        bias = []
 
         def turn_bias(i):
+            unit = vector_tile([P, P], F32, "unit")
+            nc.vector.tensor_scalar(out=unit[:], in0=ahead[:, 0:K_PASS:PACK], scalar1=0.0, scalar2=None, op0=ALU.is_equal)
             turned = bank(i, [P, PACK, P])
             nc.tensor.transpose(turned[:, 0, :], bias_rows[:], unit[:])
-            nc.scalar.copy(out=bias[:], in_=turned[:, 0, 0 : N // P])
+            bias.append(turned)
+
+        def keep_bias():
+            turned = bias.pop()
+            bias.append(scalar_tile([P, N // P], F32, "bias"))
+            nc.scalar.copy(out=bias[0][:], in_=turned[:, 0, 0 : N // P])
 
         def woven(ap):
             return ap.rearrange("p (c i t) -> p c t i", i=RUN, t=PACK)
@@ -184,6 +193,7 @@ def tile_list_tiert_silu_kernel(tc, tab_words, tab_scales, wt, x, wx, b, offs, o
 
         def bring_back(n, a, i):
             codes, scales = weights["wt", n, a]
+            ident_codes, ident_scales = ident
             backs[n, a] = bank(i, [P, PACK, P])
             for t in range(PACK):
                 nc.tensor.matmul_mx(
@@ -192,6 +202,20 @@ def tile_list_tiert_silu_kernel(tc, tab_words, tab_scales, wt, x, wx, b, offs, o
                     lhsT_scale=ident_scales[:, t * P : (t + 1) * P],
                     rhs=codes.bitcast(FP8X4),
                     rhs_scale=scales,
+                    start=True,
+                    stop=True,
+                )
+
+        def warm_tensor(i, count):
+            ident_codes, ident_scales = ident
+            unread = bank(i, [P, WIDTH])
+            for _ in range(count):
+                nc.tensor.matmul_mx(
+                    out=unread[:],
+                    lhsT=ident_codes[:, 0:P].bitcast(FP8X4),
+                    lhsT_scale=ident_scales[:, 0:P],
+                    rhs=ident_codes.bitcast(FP8X4),
+                    rhs_scale=ident_scales,
                     start=True,
                     stop=True,
                 )
@@ -247,11 +271,12 @@ def tile_list_tiert_silu_kernel(tc, tab_words, tab_scales, wt, x, wx, b, offs, o
         def finish(n, h, first=0, width=WIDTH):
             start = h * WIDTH + first
             results[n, start] = scalar_tile([P, width], F32, "result_%d" % n)
-            nc.scalar.activation(out=results[n, start][:], in_=sums[n, start][:], func=SILU, bias=bias[:, n : n + 1])
+            nc.scalar.activation(out=results[n, start][:], in_=sums[n, start][:], func=SILU, bias=bias[0][:, n : n + 1])
 
         def store(n, first, width):
             nc.sync.dma_start(out=out[n * P : (n + 1) * P, first : first + width], in_=results[n, first][:])
 
+        quantize_identity()
         load_bias()
         load_scales()
         load_words()
@@ -269,13 +294,14 @@ def tile_list_tiert_silu_kernel(tc, tab_words, tab_scales, wt, x, wx, b, offs, o
         load("x", 1, 4, 4)
         load("wx", 0, 4, 4)
         load("wx", 1, 4, 4)
-        turn_bias(7)
         pick_words(0)
+        turn_bias(7)
         pick_words(1)
         round_columns("wt", 0, 0, 2, "V")
         part_words(0)
         quantize_columns("wt", 0, 0, 2)
         round_columns("wt", 0, 2, 2, "A")
+        keep_bias()
         round_columns("wt", 1, 0, 2, "A")
         round_columns("wt", 1, 2, 2, "A")
         round_columns("wt", 0, 4, 2, "A")
@@ -286,6 +312,7 @@ def tile_list_tiert_silu_kernel(tc, tab_words, tab_scales, wt, x, wx, b, offs, o
         round_columns("wx", 0, 2, 2, "A")
         round_columns("x", 1, 0, 2, "A")
         round_columns("wx", 1, 2, 2, "A")
+        warm_tensor(3, 3)
         bring_back(0, 0, 4)
         bring_back(1, 0, 5)
         quantize_columns("wt", 0, 2, 2)
@@ -354,7 +381,6 @@ def tile_list_tiert_silu_kernel(tc, tab_words, tab_scales, wt, x, wx, b, offs, o
         quantize_columns("x", 1, 2, 2)
         quantize_columns("x", 1, 0, 2)
         quantize_columns("wx", 1, 0, 2)
-        quantize_columns("wx", 1, 2, 2)
         bring_back(7, 0, 6)
         table_pass(1, 1, 0, "wr", 0, 512)
         table_pass(1, 1, 1, "wt", 0, 512)
@@ -365,14 +391,8 @@ def tile_list_tiert_silu_kernel(tc, tab_words, tab_scales, wt, x, wx, b, offs, o
         x_pass(3, 0, 0, 0, 512)
         x_pass(0, 0, 1, 0, 512)
         x_pass(1, 0, 1, 0, 512)
-        x_pass(2, 0, 1, 0, 512)
-        x_pass(3, 0, 1, 0, 512)
-        open_sum(2, 1, 7, 0, 512)
-        table_pass(2, 1, 0, "wt", 0, 512)
-        table_pass(2, 1, 0, "wr", 0, 512)
-        table_pass(2, 1, 1, "wt", 0, 512)
-        table_pass(2, 1, 1, "wr", 0, 512)
         subtract(7, 0, 1)
+        quantize_columns("wx", 1, 2, 2)
         round_columns("wt", 1, 4, 2, "V")
         quantize_columns("wr", 0, 4, 2)
         quantize_columns("wt", 1, 4, 2)
@@ -384,6 +404,23 @@ def tile_list_tiert_silu_kernel(tc, tab_words, tab_scales, wt, x, wx, b, offs, o
         store(0, 0, 512)
         finish(1, 0, 0, 512)
         store(1, 0, 512)
+        x_pass(2, 0, 1, 0, 512)
+        x_pass(3, 0, 1, 0, 512)
+        open_sum(2, 1, 7, 0, 512)
+        table_pass(2, 1, 0, "wt", 0, 512)
+        table_pass(2, 1, 0, "wr", 0, 512)
+        table_pass(2, 1, 1, "wt", 0, 512)
+        table_pass(2, 1, 1, "wr", 0, 512)
+        open_sum(3, 1, 6, 0, 512)
+        table_pass(3, 1, 0, "wt", 0, 512)
+        table_pass(3, 1, 0, "wr", 0, 512)
+        table_pass(3, 1, 1, "wt", 0, 512)
+        table_pass(3, 1, 1, "wr", 0, 512)
+        bring_back(4, 1, 0)
+        bring_back(5, 1, 1)
+        subtract(4, 1, 2)
+        subtract(5, 1, 0)
+        quantize_columns("wr", 1, 4, 2)
         finish(2, 0, 0, 512)
         store(2, 0, 512)
         finish(3, 0, 0, 512)
@@ -392,22 +429,12 @@ def tile_list_tiert_silu_kernel(tc, tab_words, tab_scales, wt, x, wx, b, offs, o
         round_columns("x", 0, 6, 2, "A")
         round_columns("x", 1, 4, 2, "A")
         round_columns("wx", 0, 6, 2, "A")
-        open_sum(3, 1, 6, 0, 512)
-        table_pass(3, 1, 0, "wt", 0, 512)
-        table_pass(3, 1, 0, "wr", 0, 512)
-        table_pass(3, 1, 1, "wt", 0, 512)
-        table_pass(3, 1, 1, "wr", 0, 512)
-        bring_back(4, 1, 0)
-        bring_back(5, 1, 1)
         open_sum(4, 0, 2, 0, 512)
         table_pass(4, 0, 0, "wt", 0, 512)
         table_pass(4, 0, 0, "wr", 0, 512)
         open_sum(5, 0, 3, 0, 512)
         table_pass(5, 0, 0, "wt", 0, 512)
         table_pass(5, 0, 0, "wr", 0, 512)
-        subtract(4, 1, 2)
-        subtract(5, 1, 0)
-        quantize_columns("wr", 1, 4, 2)
         bring_back(6, 1, 0)
         bring_back(7, 1, 1)
         table_pass(4, 0, 1, "wt", 0, 512)

@@ -21,15 +21,16 @@ PACK = 4
 K_PASS = P * PACK
 PASSES = K // K_PASS
 WIDTH = 512
-CHUNK = 256
-CHUNKS = WIDTH // CHUNK
-TILES = CHUNK // P
+GROUPS = WIDTH // P
+PAIR = 2
 RUN = 4
 DMA_ALIGN = 256
 LIST_ROWS = 16
 PASS_GAP = 16
-VECTOR_TILES = 43
+BANKS = 8
+VECTOR_SLOTS = 42
 SCALAR_SLOTS = 17
+BACK_AHEAD = 3
 
 
 def tile_list_tiert_silu_kernel(tc, tab_words, tab_scales, wt, x, wx, b, offs, out):
@@ -38,11 +39,11 @@ def tile_list_tiert_silu_kernel(tc, tab_words, tab_scales, wt, x, wx, b, offs, o
         keep = ctx.enter_context(tc.tile_pool(name="keep", bufs=1))
         psum = ctx.enter_context(tc.psum_pool(name="psum", bufs=1))
 
-        def bank(i, shape):
-            return psum.tile(shape, F32, name="bank_%d" % i, tag="bank", bufs=8)
+        def bank(shape):
+            return psum.tile(shape, F32, name="bank", tag="bank", bufs=BANKS)
 
         def vector_tile(shape, dtype, name):
-            return keep.tile(shape, dtype, name=name, tag="vector_turn", bufs=VECTOR_TILES, align_bytes=64)
+            return keep.tile(shape, dtype, name=name, tag="vector_turn", bufs=VECTOR_SLOTS, align_bytes=64)
 
         def scalar_tile(shape, dtype, name):
             return keep.tile(shape, dtype, name=name, tag="scalar_turn", bufs=SCALAR_SLOTS, align_bytes=DMA_ALIGN)
@@ -78,24 +79,22 @@ def tile_list_tiert_silu_kernel(tc, tab_words, tab_scales, wt, x, wx, b, offs, o
         ones = keep.tile([P, PACK, K_PASS], BF16, name="ones", tag="raw_wx_4_1", align_bytes=DMA_ALIGN)
         for t in range(PACK):
             nc.vector.tensor_scalar(out=ones[:, t, :], in0=ahead[:], scalar1=float(t), scalar2=None, op0=ALU.is_equal)
-        ident = []
-
-        def quantize_identity():
-            ident.extend(quantize(ones[:].rearrange("p t w -> p (t w)"), "ident"))
+        unit = keep.tile([P, P], F32, name="unit")
+        nc.vector.tensor_scalar(out=unit[:], in0=ahead[:, 0:K_PASS:PACK], scalar1=0.0, scalar2=None, op0=ALU.is_equal)
+        ident_codes, ident_scales = quantize(ones[:].rearrange("p t w -> p (t w)"), "ident")
 
         inputs = {"wt": wt, "wx": wx, "x": x}
         raw = {}
 
-        def load(name, a, first, count):
-            tile = keep.tile([P, PACK, count * P], F32, name="raw_%s_%d_%d" % (name, first, a), align_bytes=DMA_ALIGN)
-            rows = inputs[name][a * K_PASS : (a + 1) * K_PASS, first * P : (first + count) * P]
+        def load(name, a, side):
+            tile = keep.tile([P, PACK, WIDTH], F32, name="raw_%s_%d_%d" % (name, side * GROUPS, a), align_bytes=DMA_ALIGN)
+            rows = inputs[name][a * K_PASS : (a + 1) * K_PASS, side * WIDTH : (side + 1) * WIDTH]
             nc.sync.dma_start(out=tile[:], in_=rows.rearrange("(p t) w -> p t w", t=PACK))
-            for g in range(count):
-                raw[name, a, first + g] = tile, g
+            raw[name, a, side] = tile
 
         def raw_columns(name, a, first, count):
-            tile, g = raw[name, a, first]
-            return tile[:, :, g * P : (g + count) * P]
+            side, g = divmod(first, GROUPS)
+            return raw[name, a, side][:, :, g * P : (g + count) * P]
 
         def load_bias():
             nc.sync.dma_start(out=bias_rows[0 : N // P, :], in_=b.rearrange("(c p) -> c p", p=P))
@@ -123,19 +122,12 @@ def tile_list_tiert_silu_kernel(tc, tab_words, tab_scales, wt, x, wx, b, offs, o
                 nc.sync.dma_start(out=moved_scales[r:P:32, :].bitcast(I32), in_=tab_planes[0][PASS_GAP + r : P : 32, :].bitcast(I32))
             tab_planes[1] = moved_scales
 
-        bias = []
-
-        def turn_bias(i):
-            unit = vector_tile([P, P], F32, "unit")
-            nc.vector.tensor_scalar(out=unit[:], in0=ahead[:, 0:K_PASS:PACK], scalar1=0.0, scalar2=None, op0=ALU.is_equal)
-            turned = bank(i, [P, PACK, P])
+        def turn_bias():
+            turned = bank([P, PACK, P])
             nc.tensor.transpose(turned[:, 0, :], bias_rows[:], unit[:])
-            bias.append(turned)
-
-        def keep_bias():
-            turned = bias.pop()
-            bias.append(scalar_tile([P, N // P], F32, "bias"))
-            nc.scalar.copy(out=bias[0][:], in_=turned[:, 0, 0 : N // P])
+            kept = scalar_tile([P, N // P], F32, "bias")
+            nc.scalar.copy(out=kept[:], in_=turned[:, 0, 0 : N // P])
+            return kept
 
         def woven(ap):
             return ap.rearrange("p (c i t) -> p c t i", i=RUN, t=PACK)
@@ -146,12 +138,10 @@ def tile_list_tiert_silu_kernel(tc, tab_words, tab_scales, wt, x, wx, b, offs, o
         picked = {}
         tab_codes = {}
 
-        def pick_words(h, first=0, width=WIDTH):
-            if first == 0:
-                picked[h] = vector_tile([P, WIDTH], U32, "picked_%d" % h)[:]
-            start = h * WIDTH + first
-            entries = offsets[:, start // LIST_ROWS : (start + width) // LIST_ROWS]
-            nc.vector.tensor_copy(picked[h][:, first : first + width], word_window[:].indirect(entries))
+        def pick_words(h):
+            picked[h] = vector_tile([P, WIDTH], U32, "picked_%d" % h)[:]
+            entries = offsets[:, h * WIDTH // LIST_ROWS : (h + 1) * WIDTH // LIST_ROWS]
+            nc.vector.tensor_copy(picked[h], word_window[:].indirect(entries))
 
         def part_words(h):
             tab_codes[h] = vector_tile([P, PASSES, 2 * WIDTH], U8, "parted_%d" % h)
@@ -159,22 +149,21 @@ def tile_list_tiert_silu_kernel(tc, tab_words, tab_scales, wt, x, wx, b, offs, o
 
         rounded = {}
 
-        def round_columns(name, a, first, count, engine):
-            tile = (vector_tile if engine == "V" else scalar_tile)([P, count * P * PACK], BF16, "rounded")
-            source = by_runs(raw_columns(name, a, first, count))
-            if engine == "V":
+        def round_chunk(name, a, first, on_vector=False):
+            tile = (vector_tile if on_vector else scalar_tile)([P, PAIR * P * PACK], BF16, "rounded")
+            source = by_runs(raw_columns(name, a, first, PAIR))
+            if on_vector:
                 nc.vector.tensor_copy(out=woven(tile[:]), in_=source)
             else:
                 nc.scalar.copy(out=woven(tile[:]), in_=source)
-            for g in range(count):
-                rounded[name, a, first + g] = tile, g
+            rounded[name, a, first] = tile
 
         weights = {}
         tokens = {}
 
-        def quantize_columns(name, a, first, count):
-            tile, g = rounded[name, a, first]
-            source = tile[:, g * P * PACK : (g + count) * P * PACK]
+        def quantize_chunk(name, a, first):
+            source = rounded[name, a, first][:]
+            count = source.shape[1] // (P * PACK)
             if name == "x":
                 h, start = divmod(first * P, WIDTH)
                 if (h, a) not in tokens:
@@ -191,10 +180,9 @@ def tile_list_tiert_silu_kernel(tc, tab_words, tab_scales, wt, x, wx, b, offs, o
 
         backs = {}
 
-        def bring_back(n, a, i):
+        def bring_back(n, a):
             codes, scales = weights["wt", n, a]
-            ident_codes, ident_scales = ident
-            backs[n, a] = bank(i, [P, PACK, P])
+            backs[n, a] = bank([P, PACK, P])
             for t in range(PACK):
                 nc.tensor.matmul_mx(
                     out=backs[n, a][:, t, :],
@@ -206,26 +194,11 @@ def tile_list_tiert_silu_kernel(tc, tab_words, tab_scales, wt, x, wx, b, offs, o
                     stop=True,
                 )
 
-        def warm_tensor(i, count):
-            ident_codes, ident_scales = ident
-            unread = bank(i, [P, WIDTH])
-            for _ in range(count):
-                nc.tensor.matmul_mx(
-                    out=unread[:],
-                    lhsT=ident_codes[:, 0:P].bitcast(FP8X4),
-                    lhsT_scale=ident_scales[:, 0:P],
-                    rhs=ident_codes.bitcast(FP8X4),
-                    rhs_scale=ident_scales,
-                    start=True,
-                    stop=True,
-                )
-
-        def subtract(n, a, count):
-            if count:
-                tile = vector_tile([P, count * P * PACK], BF16, "rest")
-                for g in range(count):
-                    rounded["wr", a, n + g] = tile, g
-            tile, g = rounded["wr", a, n]
+        def subtract(n, a, alone=False):
+            first, count = (n, 1) if alone else (n - n % PAIR, PAIR)
+            if n == first:
+                rounded["wr", a, first] = vector_tile([P, count * P * PACK], BF16, "rest")
+            tile, g = rounded["wr", a, first], n - first
             nc.vector.tensor_tensor(
                 out=woven(tile[:, g * P * PACK : (g + 1) * P * PACK]),
                 in0=by_runs(raw_columns("wt", a, n, 1)),
@@ -235,7 +208,6 @@ def tile_list_tiert_silu_kernel(tc, tab_words, tab_scales, wt, x, wx, b, offs, o
 
         sums = {}
         done = {}
-        results = {}
 
         def add_pass(n, first, operand, a, rhs, rhs_scale):
             codes, scales = weights[operand, n, a]
@@ -250,8 +222,8 @@ def tile_list_tiert_silu_kernel(tc, tab_words, tab_scales, wt, x, wx, b, offs, o
             )
             done[n, first] += 1
 
-        def open_sum(n, h, i, first=0, width=WIDTH):
-            sums[n, h * WIDTH + first] = bank(i, [P, width])
+        def open_sum(n, h, first=0, width=WIDTH):
+            sums[n, h * WIDTH + first] = bank([P, width])
             done[n, h * WIDTH + first] = 0
 
         def table_pass(n, h, a, operand, first=0, width=WIDTH):
@@ -259,9 +231,10 @@ def tile_list_tiert_silu_kernel(tc, tab_words, tab_scales, wt, x, wx, b, offs, o
             plane = tab_planes[a][:, h * WIDTH + first : h * WIDTH + first + width]
             add_pass(n, h * WIDTH + first, operand, a, rhs, plane)
 
-        def table_passes(n, h, a, first=0, width=WIDTH):
-            for operand in ("wt", "wr"):
-                table_pass(n, h, a, operand, first, width)
+        def table_passes(n, h, first=0, width=WIDTH):
+            for a in range(PASSES):
+                for operand in ("wt", "wr"):
+                    table_pass(n, h, a, operand, first, width)
 
         def x_pass(n, h, a, first=0, width=WIDTH):
             codes, scales = tokens[h, a]
@@ -270,285 +243,167 @@ def tile_list_tiert_silu_kernel(tc, tab_words, tab_scales, wt, x, wx, b, offs, o
 
         def finish(n, h, first=0, width=WIDTH):
             start = h * WIDTH + first
-            results[n, start] = scalar_tile([P, width], F32, "result_%d" % n)
-            nc.scalar.activation(out=results[n, start][:], in_=sums[n, start][:], func=SILU, bias=bias[0][:, n : n + 1])
+            result = scalar_tile([P, width], F32, "result_%d" % n)
+            nc.scalar.activation(out=result[:], in_=sums[n, start][:], func=SILU, bias=bias[:, n : n + 1])
+            nc.sync.dma_start(out=out[n * P : (n + 1) * P, start : start + width], in_=result[:])
 
-        def store(n, first, width):
-            nc.sync.dma_start(out=out[n * P : (n + 1) * P, first : first + width], in_=results[n, first][:])
-
-        quantize_identity()
         load_bias()
         load_scales()
         load_words()
-        load("wt", 0, 0, 4)
-        load("wt", 1, 0, 4)
+        for a in range(PASSES):
+            load("wt", a, 0)
         pick_scales()
-        load("wt", 0, 4, 4)
+        load("wt", 0, 1)
         move_scales()
-        load("x", 0, 0, 4)
-        load("wx", 0, 0, 4)
-        load("x", 1, 0, 4)
-        load("wx", 1, 0, 4)
-        load("wt", 1, 4, 4)
-        load("x", 0, 4, 4)
-        load("x", 1, 4, 4)
-        load("wx", 0, 4, 4)
-        load("wx", 1, 4, 4)
+        for a in range(PASSES):
+            load("x", a, 0)
+            load("wx", a, 0)
+        load("wt", 1, 1)
+        for name in ("x", "wx"):
+            for a in range(PASSES):
+                load(name, a, 1)
+
+        bias = turn_bias()
         pick_words(0)
-        turn_bias(7)
         pick_words(1)
-        round_columns("wt", 0, 0, 2, "V")
+        round_chunk("wt", 0, 0, on_vector=True)
         part_words(0)
-        quantize_columns("wt", 0, 0, 2)
-        round_columns("wt", 0, 2, 2, "A")
-        keep_bias()
-        round_columns("wt", 1, 0, 2, "A")
-        round_columns("wt", 1, 2, 2, "A")
-        round_columns("wt", 0, 4, 2, "A")
-        round_columns("wt", 0, 6, 2, "A")
-        round_columns("x", 0, 0, 2, "A")
-        round_columns("x", 0, 2, 2, "A")
-        round_columns("wx", 0, 0, 2, "A")
-        round_columns("wx", 0, 2, 2, "A")
-        round_columns("x", 1, 0, 2, "A")
-        round_columns("wx", 1, 2, 2, "A")
-        warm_tensor(3, 3)
-        bring_back(0, 0, 4)
-        bring_back(1, 0, 5)
-        quantize_columns("wt", 0, 2, 2)
+        quantize_chunk("wt", 0, 0)
+        round_chunk("wt", 0, PAIR)
+
+        early = [(a, side * GROUPS + first) for a, side in ((0, 0), (1, 0), (0, 1)) for first in (0, PAIR)]
+        for a, first in early[2:]:
+            round_chunk("wt", a, first)
+        for name in ("x", "wx"):
+            for first in (0, PAIR):
+                round_chunk(name, 0, first)
+        round_chunk("x", 1, 0)
+        round_chunk("wx", 1, PAIR)
+
+        def bring_back_chunk(a, first):
+            for n in (first, first + 1):
+                bring_back(n, a)
+
+        def first_half_passes(operand, a, first):
+            if first < GROUPS:
+                for n in (first, first + 1):
+                    table_pass(n, 0, a, operand)
+
+        bring_back_chunk(*early[0])
+        quantize_chunk("wt", *early[1])
         part_words(1)
-        subtract(0, 0, 2)
-        subtract(1, 0, 0)
-        quantize_columns("wt", 1, 0, 2)
-        bring_back(2, 0, 6)
-        bring_back(3, 0, 7)
-        open_sum(0, 0, 0, 0, 512)
-        table_pass(0, 0, 0, "wt", 0, 512)
-        open_sum(1, 0, 1, 0, 512)
-        table_pass(1, 0, 0, "wt", 0, 512)
-        open_sum(2, 0, 2, 0, 512)
-        table_pass(2, 0, 0, "wt", 0, 512)
-        open_sum(3, 0, 3, 0, 512)
-        table_pass(3, 0, 0, "wt", 0, 512)
-        bring_back(0, 1, 4)
-        bring_back(1, 1, 5)
-        subtract(2, 0, 2)
-        quantize_columns("wr", 0, 0, 2)
-        subtract(3, 0, 0)
-        quantize_columns("wt", 1, 2, 2)
-        subtract(0, 1, 2)
-        quantize_columns("wr", 0, 2, 2)
-        subtract(1, 1, 0)
-        quantize_columns("wt", 0, 4, 2)
-        table_pass(0, 0, 0, "wr", 0, 512)
-        table_pass(1, 0, 0, "wr", 0, 512)
-        bring_back(2, 1, 6)
-        bring_back(3, 1, 7)
-        table_pass(0, 0, 1, "wt", 0, 512)
-        table_pass(1, 0, 1, "wt", 0, 512)
-        table_pass(2, 0, 0, "wr", 0, 512)
-        table_pass(3, 0, 0, "wr", 0, 512)
-        open_sum(0, 1, 4, 0, 512)
-        table_pass(0, 1, 0, "wt", 0, 512)
-        table_pass(2, 0, 1, "wt", 0, 512)
-        table_pass(3, 0, 1, "wt", 0, 512)
-        bring_back(4, 0, 5)
-        subtract(2, 1, 2)
-        quantize_columns("wr", 1, 0, 2)
-        subtract(3, 1, 0)
-        quantize_columns("wt", 0, 6, 2)
-        subtract(4, 0, 2)
-        quantize_columns("wr", 1, 2, 2)
-        bring_back(5, 0, 6)
-        table_pass(0, 0, 1, "wr", 0, 512)
-        table_pass(1, 0, 1, "wr", 0, 512)
-        table_pass(0, 1, 0, "wr", 0, 512)
-        bring_back(6, 0, 7)
-        table_pass(0, 1, 1, "wt", 0, 512)
-        table_pass(0, 1, 1, "wr", 0, 512)
-        table_pass(2, 0, 1, "wr", 0, 512)
-        table_pass(3, 0, 1, "wr", 0, 512)
-        open_sum(1, 1, 5, 0, 512)
-        table_pass(1, 1, 0, "wt", 0, 512)
-        subtract(5, 0, 0)
-        quantize_columns("x", 0, 0, 2)
-        quantize_columns("x", 0, 2, 2)
-        subtract(6, 0, 1)
-        round_columns("x", 1, 2, 2, "V")
-        quantize_columns("wx", 0, 0, 2)
-        quantize_columns("wx", 0, 2, 2)
-        round_columns("wx", 1, 0, 2, "V")
-        quantize_columns("x", 1, 2, 2)
-        quantize_columns("x", 1, 0, 2)
-        quantize_columns("wx", 1, 0, 2)
-        bring_back(7, 0, 6)
-        table_pass(1, 1, 0, "wr", 0, 512)
-        table_pass(1, 1, 1, "wt", 0, 512)
-        table_pass(1, 1, 1, "wr", 0, 512)
-        x_pass(0, 0, 0, 0, 512)
-        x_pass(1, 0, 0, 0, 512)
-        x_pass(2, 0, 0, 0, 512)
-        x_pass(3, 0, 0, 0, 512)
-        x_pass(0, 0, 1, 0, 512)
-        x_pass(1, 0, 1, 0, 512)
-        subtract(7, 0, 1)
-        quantize_columns("wx", 1, 2, 2)
-        round_columns("wt", 1, 4, 2, "V")
-        quantize_columns("wr", 0, 4, 2)
-        quantize_columns("wt", 1, 4, 2)
-        round_columns("wt", 1, 6, 2, "V")
-        quantize_columns("wr", 0, 6, 1)
-        quantize_columns("wt", 1, 6, 2)
-        quantize_columns("wr", 0, 7, 1)
-        finish(0, 0, 0, 512)
-        store(0, 0, 512)
-        finish(1, 0, 0, 512)
-        store(1, 0, 512)
-        x_pass(2, 0, 1, 0, 512)
-        x_pass(3, 0, 1, 0, 512)
-        open_sum(2, 1, 7, 0, 512)
-        table_pass(2, 1, 0, "wt", 0, 512)
-        table_pass(2, 1, 0, "wr", 0, 512)
-        table_pass(2, 1, 1, "wt", 0, 512)
-        table_pass(2, 1, 1, "wr", 0, 512)
-        open_sum(3, 1, 6, 0, 512)
-        table_pass(3, 1, 0, "wt", 0, 512)
-        table_pass(3, 1, 0, "wr", 0, 512)
-        table_pass(3, 1, 1, "wt", 0, 512)
-        table_pass(3, 1, 1, "wr", 0, 512)
-        bring_back(4, 1, 0)
-        bring_back(5, 1, 1)
-        subtract(4, 1, 2)
-        subtract(5, 1, 0)
-        quantize_columns("wr", 1, 4, 2)
-        finish(2, 0, 0, 512)
-        store(2, 0, 512)
-        finish(3, 0, 0, 512)
-        store(3, 0, 512)
-        round_columns("x", 0, 4, 2, "A")
-        round_columns("x", 0, 6, 2, "A")
-        round_columns("x", 1, 4, 2, "A")
-        round_columns("wx", 0, 6, 2, "A")
-        open_sum(4, 0, 2, 0, 512)
-        table_pass(4, 0, 0, "wt", 0, 512)
-        table_pass(4, 0, 0, "wr", 0, 512)
-        open_sum(5, 0, 3, 0, 512)
-        table_pass(5, 0, 0, "wt", 0, 512)
-        table_pass(5, 0, 0, "wr", 0, 512)
-        bring_back(6, 1, 0)
-        bring_back(7, 1, 1)
-        table_pass(4, 0, 1, "wt", 0, 512)
-        table_pass(5, 0, 1, "wt", 0, 512)
-        table_pass(4, 0, 1, "wr", 0, 512)
-        table_pass(5, 0, 1, "wr", 0, 512)
-        subtract(6, 1, 2)
-        quantize_columns("x", 0, 4, 2)
-        subtract(7, 1, 0)
-        quantize_columns("x", 0, 6, 2)
-        round_columns("x", 1, 6, 2, "V")
-        quantize_columns("wr", 1, 6, 2)
-        quantize_columns("x", 1, 4, 2)
-        quantize_columns("x", 1, 6, 2)
-        round_columns("wx", 0, 4, 2, "V")
-        quantize_columns("wx", 0, 6, 2)
-        quantize_columns("wx", 0, 4, 2)
-        round_columns("wx", 1, 4, 2, "V")
-        round_columns("wx", 1, 6, 2, "V")
-        quantize_columns("wx", 1, 4, 2)
-        quantize_columns("wx", 1, 6, 2)
-        x_pass(0, 1, 0, 0, 512)
-        x_pass(1, 1, 0, 0, 512)
-        x_pass(2, 1, 0, 0, 512)
-        x_pass(3, 1, 0, 0, 512)
-        x_pass(0, 1, 1, 0, 512)
-        x_pass(1, 1, 1, 0, 512)
-        x_pass(2, 1, 1, 0, 512)
-        x_pass(3, 1, 1, 0, 512)
-        open_sum(6, 0, 0, 0, 512)
-        table_pass(6, 0, 0, "wt", 0, 512)
-        table_pass(6, 0, 0, "wr", 0, 512)
-        table_pass(6, 0, 1, "wt", 0, 512)
-        table_pass(6, 0, 1, "wr", 0, 512)
-        open_sum(7, 0, 1, 0, 512)
-        table_pass(7, 0, 0, "wt", 0, 512)
-        table_pass(7, 0, 0, "wr", 0, 512)
-        table_pass(7, 0, 1, "wt", 0, 512)
-        table_pass(7, 0, 1, "wr", 0, 512)
-        x_pass(4, 0, 0, 0, 512)
-        x_pass(5, 0, 0, 0, 512)
-        x_pass(6, 0, 0, 0, 512)
-        x_pass(7, 0, 0, 0, 512)
-        x_pass(4, 0, 1, 0, 512)
-        x_pass(5, 0, 1, 0, 512)
-        x_pass(6, 0, 1, 0, 512)
-        x_pass(7, 0, 1, 0, 512)
-        finish(0, 1, 0, 512)
-        store(0, 512, 512)
-        finish(1, 1, 0, 512)
-        store(1, 512, 512)
-        finish(2, 1, 0, 512)
-        store(2, 512, 512)
-        finish(3, 1, 0, 512)
-        store(3, 512, 512)
-        finish(4, 0, 0, 512)
-        store(4, 0, 512)
-        finish(5, 0, 0, 512)
-        store(5, 0, 512)
-        finish(6, 0, 0, 512)
-        store(6, 0, 512)
-        finish(7, 0, 0, 512)
-        store(7, 0, 512)
-        open_sum(4, 1, 4, 0, 512)
-        table_pass(4, 1, 0, "wt", 0, 512)
-        table_pass(4, 1, 0, "wr", 0, 512)
-        table_pass(4, 1, 1, "wt", 0, 512)
-        table_pass(4, 1, 1, "wr", 0, 512)
-        x_pass(4, 1, 0, 0, 512)
-        x_pass(4, 1, 1, 0, 512)
-        open_sum(5, 1, 5, 0, 512)
-        table_pass(5, 1, 0, "wt", 0, 512)
-        table_pass(5, 1, 0, "wr", 0, 512)
-        table_pass(5, 1, 1, "wt", 0, 512)
-        table_pass(5, 1, 1, "wr", 0, 512)
-        x_pass(5, 1, 0, 0, 512)
-        x_pass(5, 1, 1, 0, 512)
-        open_sum(6, 1, 7, 0, 512)
-        table_pass(6, 1, 0, "wt", 0, 512)
-        table_pass(6, 1, 0, "wr", 0, 512)
-        table_pass(6, 1, 1, "wt", 0, 512)
-        table_pass(6, 1, 1, "wr", 0, 512)
-        x_pass(6, 1, 0, 0, 512)
-        x_pass(6, 1, 1, 0, 512)
-        open_sum(7, 1, 6, 0, 256)
-        table_pass(7, 1, 0, "wt", 0, 256)
-        table_pass(7, 1, 0, "wr", 0, 256)
-        table_pass(7, 1, 1, "wt", 0, 256)
-        table_pass(7, 1, 1, "wr", 0, 256)
-        x_pass(7, 1, 0, 0, 256)
-        x_pass(7, 1, 1, 0, 256)
-        open_sum(7, 1, 2, 256, 128)
-        table_pass(7, 1, 0, "wt", 256, 128)
-        table_pass(7, 1, 0, "wr", 256, 128)
-        table_pass(7, 1, 1, "wt", 256, 128)
-        table_pass(7, 1, 1, "wr", 256, 128)
-        x_pass(7, 1, 0, 256, 128)
-        x_pass(7, 1, 1, 256, 128)
-        open_sum(7, 1, 3, 384, 128)
-        table_pass(7, 1, 0, "wt", 384, 128)
-        table_pass(7, 1, 0, "wr", 384, 128)
-        table_pass(7, 1, 1, "wt", 384, 128)
-        table_pass(7, 1, 1, "wr", 384, 128)
-        x_pass(7, 1, 0, 384, 128)
-        x_pass(7, 1, 1, 384, 128)
-        finish(4, 1, 0, 512)
-        store(4, 512, 512)
-        finish(5, 1, 0, 512)
-        store(5, 512, 512)
-        finish(6, 1, 0, 512)
-        store(6, 512, 512)
-        finish(7, 1, 0, 256)
-        store(7, 512, 256)
-        finish(7, 1, 256, 128)
-        store(7, 768, 128)
-        finish(7, 1, 384, 128)
-        store(7, 896, 128)
+        bring_back_chunk(*early[1])
+        for n in range(GROUPS):
+            open_sum(n, 0)
+            table_pass(n, 0, 0, "wt")
+
+        tiles = [(n, a) for a, first in early for n in (first, first + 1)]
+        brought, opened = 2 * PAIR, 0
+        waiting = []
+        for i, (a, first) in enumerate(early[:-1]):
+            at_hand = set(weights)
+            subtract(first, a)
+            if i > 0:
+                quantize_chunk("wr", *early[i - 1])
+            subtract(first + 1, a)
+            if i + 2 < len(early):
+                quantize_chunk("wt", *early[i + 2])
+            for spent in (PAIR * i, PAIR * i + 1):
+                if brought < len(tiles) and (tiles[brought][0] < GROUPS or brought - spent <= BACK_AHEAD):
+                    bring_back(*tiles[brought])
+                    brought += 1
+                else:
+                    open_sum(opened, 1)
+                    table_pass(opened, 1, 0, "wt")
+                    waiting += [("wr", opened, 0), ("wt", opened, 1), ("wr", opened, 1)]
+                    opened += 1
+            for operand, n, a_pass in [key for key in waiting if key in at_hand]:
+                table_pass(n, 1, a_pass, operand)
+                waiting.remove((operand, n, a_pass))
+            if i > 0:
+                first_half_passes("wr", *early[i - 1])
+                first_half_passes("wt", *early[i + 1])
+
+        a, first = early[-1]
+        for chunk in (0, PAIR):
+            quantize_chunk("x", 0, chunk)
+        subtract(first, a, alone=True)
+        round_chunk("x", 1, PAIR, on_vector=True)
+        for chunk in (0, PAIR):
+            quantize_chunk("wx", 0, chunk)
+        round_chunk("wx", 1, 0, on_vector=True)
+        for chunk in (PAIR, 0):
+            quantize_chunk("x", 1, chunk)
+        quantize_chunk("wx", 1, 0)
+        subtract(first + 1, a, alone=True)
+        quantize_chunk("wx", 1, PAIR)
+        for a_x in range(PASSES):
+            for n in range(GROUPS):
+                x_pass(n, 0, a_x)
+        for n in range(opened, GROUPS):
+            open_sum(n, 1)
+            table_passes(n, 1)
+        for n in range(GROUPS):
+            finish(n, 0)
+
+        late = [(1, GROUPS), (1, GROUPS + PAIR)]
+        round_chunk("wt", *late[0], on_vector=True)
+        quantize_chunk("wr", *early[-2])
+        quantize_chunk("wt", *late[0])
+        round_chunk("wt", *late[1], on_vector=True)
+        quantize_chunk("wr", a, first)
+        quantize_chunk("wt", *late[1])
+        quantize_chunk("wr", a, first + 1)
+        for name, a_late, chunk in (("x", 0, GROUPS), ("x", 0, GROUPS + PAIR), ("x", 1, GROUPS), ("wx", 0, GROUPS + PAIR)):
+            round_chunk(name, a_late, chunk)
+
+        pair = range(GROUPS, GROUPS + PAIR)
+        bring_back_chunk(*late[0])
+        for n in pair:
+            open_sum(n, 0)
+            for operand in ("wt", "wr"):
+                table_pass(n, 0, 0, operand)
+        for n in pair:
+            subtract(n, 1)
+        quantize_chunk("wr", *late[0])
+        bring_back_chunk(*late[1])
+        for operand in ("wt", "wr"):
+            for n in pair:
+                table_pass(n, 0, 1, operand)
+        for chunk in range(PAIR):
+            subtract(GROUPS + PAIR + chunk, 1)
+            quantize_chunk("x", 0, GROUPS + chunk * PAIR)
+
+        round_chunk("x", 1, GROUPS + PAIR, on_vector=True)
+        quantize_chunk("wr", *late[1])
+        for chunk in (GROUPS, GROUPS + PAIR):
+            quantize_chunk("x", 1, chunk)
+        round_chunk("wx", 0, GROUPS, on_vector=True)
+        for chunk in (GROUPS + PAIR, GROUPS):
+            quantize_chunk("wx", 0, chunk)
+        for chunk in (GROUPS, GROUPS + PAIR):
+            round_chunk("wx", 1, chunk, on_vector=True)
+        for chunk in (GROUPS, GROUPS + PAIR):
+            quantize_chunk("wx", 1, chunk)
+        for a_x in range(PASSES):
+            for n in range(GROUPS):
+                x_pass(n, 1, a_x)
+        for n in range(GROUPS + PAIR, N // P):
+            open_sum(n, 0)
+            table_passes(n, 0)
+        for n in range(GROUPS):
+            finish(n, 1)
+
+        for a_x in range(PASSES):
+            for n in range(GROUPS, N // P):
+                x_pass(n, 0, a_x)
+        for n in range(GROUPS, N // P):
+            finish(n, 0)
+        pieces = [(n, 0, WIDTH) for n in range(GROUPS, N // P - 1)]
+        pieces += [(N // P - 1, 0, 2 * P), (N // P - 1, 2 * P, P), (N // P - 1, 3 * P, P)]
+        for n, start, width in pieces:
+            open_sum(n, 1, start, width)
+            table_passes(n, 1, start, width)
+            for a_x in range(PASSES):
+                x_pass(n, 1, a_x, start, width)
+            finish(n, 1, start, width)

@@ -13,7 +13,7 @@ U16 = mybir.dt.uint16
 U8 = mybir.dt.uint8
 FP8X4 = mybir.dt.float8_e4m3fn_x4
 FP4X4 = mybir.dt.float4_e2m1fn_x4
-SILU = mybir.ActivationFunctionType.Silu
+ACT = mybir.ActivationFunctionType
 ALU = mybir.AluOpType
 
 P = 128
@@ -21,16 +21,16 @@ PACK = 4
 K_PASS = P * PACK
 PASSES = K // K_PASS
 WIDTH = 512
-GROUPS = WIDTH // P
+TILES = N // P
+SIDE = TILES // 2
 PAIR = 2
 RUN = 4
 DMA_ALIGN = 256
 LIST_ROWS = 16
 PASS_GAP = 16
 BANKS = 8
-VECTOR_SLOTS = 42
+VECTOR_SLOTS = 45
 SCALAR_SLOTS = 17
-BACK_AHEAD = 3
 
 
 def tile_list_tiert_silu_kernel(tc, tab_words, tab_scales, wt, x, wx, b, offs, out):
@@ -47,6 +47,9 @@ def tile_list_tiert_silu_kernel(tc, tab_words, tab_scales, wt, x, wx, b, offs, o
 
         def scalar_tile(shape, dtype, name):
             return keep.tile(shape, dtype, name=name, tag="scalar_turn", bufs=SCALAR_SLOTS, align_bytes=DMA_ALIGN)
+
+        def load_tile(shape, dtype, name, place):
+            return keep.tile(shape, dtype, name=name, tag=place, align_bytes=DMA_ALIGN)
 
         def quantize(rounded, name):
             width = rounded.shape[1] // PACK
@@ -65,7 +68,7 @@ def tile_list_tiert_silu_kernel(tc, tab_words, tab_scales, wt, x, wx, b, offs, o
         zero = keep.tile([P, 1], F32, name="zero")
         nc.vector.memset(zero[:], 0.0)
         warm = keep.tile([P, 1], F32, name="warm")
-        nc.scalar.activation(out=warm[:], in_=zero[:], func=SILU)
+        nc.scalar.activation(out=warm[:], in_=zero[:], func=ACT.Silu)
 
         bias_rows = keep.tile([P, P], F32, name="bias_rows")
         nc.vector.memset(bias_rows[:], 0.0)
@@ -76,28 +79,33 @@ def tile_list_tiert_silu_kernel(tc, tab_words, tab_scales, wt, x, wx, b, offs, o
 
         ahead = keep.tile([P, K_PASS], BF16, name="ahead", align_bytes=64)
         nc.gpsimd.iota(ahead[:], [[1, K_PASS]], base=0, channel_multiplier=-PACK, allow_small_or_imprecise_dtypes=True)
-        ones = keep.tile([P, PACK, K_PASS], BF16, name="ones", tag="raw_wx_4_1", align_bytes=DMA_ALIGN)
+        ones = load_tile([P, PACK, K_PASS], BF16, "ones", "place_ones")
         for t in range(PACK):
             nc.vector.tensor_scalar(out=ones[:, t, :], in0=ahead[:], scalar1=float(t), scalar2=None, op0=ALU.is_equal)
-        unit = keep.tile([P, P], F32, name="unit")
+        unit = vector_tile([P, P], F32, "unit")
         nc.vector.tensor_scalar(out=unit[:], in0=ahead[:, 0:K_PASS:PACK], scalar1=0.0, scalar2=None, op0=ALU.is_equal)
-        ident_codes, ident_scales = quantize(ones[:].rearrange("p t w -> p (t w)"), "ident")
+        ident = {}
+
+        def quantize_identity():
+            ident["codes"], ident["scales"] = quantize(ones[:].rearrange("p t w -> p (t w)"), "ident")
 
         inputs = {"wt": wt, "wx": wx, "x": x}
         raw = {}
 
-        def load(name, a, side):
-            tile = keep.tile([P, PACK, WIDTH], F32, name="raw_%s_%d_%d" % (name, side * GROUPS, a), align_bytes=DMA_ALIGN)
-            rows = inputs[name][a * K_PASS : (a + 1) * K_PASS, side * WIDTH : (side + 1) * WIDTH]
+        def load(name, a, first, count, place=None):
+            label = "raw_%s_%d_%d" % (name, first, a)
+            tile = load_tile([P, PACK, count * P], F32, label, place or label)
+            rows = inputs[name][a * K_PASS : (a + 1) * K_PASS, first * P : (first + count) * P]
             nc.sync.dma_start(out=tile[:], in_=rows.rearrange("(p t) w -> p t w", t=PACK))
-            raw[name, a, side] = tile
+            for g in range(count):
+                raw[name, a, first + g] = tile, g
 
         def raw_columns(name, a, first, count):
-            side, g = divmod(first, GROUPS)
-            return raw[name, a, side][:, :, g * P : (g + count) * P]
+            tile, g = raw[name, a, first]
+            return tile[:, :, g * P : (g + count) * P]
 
         def load_bias():
-            nc.sync.dma_start(out=bias_rows[0 : N // P, :], in_=b.rearrange("(c p) -> c p", p=P))
+            nc.sync.dma_start(out=bias_rows[0:TILES, :], in_=b.rearrange("(c p) -> c p", p=P))
 
         def load_scales():
             for r in range(4):
@@ -106,7 +114,7 @@ def tile_list_tiert_silu_kernel(tc, tab_words, tab_scales, wt, x, wx, b, offs, o
                     in_=tab_scales[:, r:16:4, :].rearrange("a q t -> q a t").bitcast(I32),
                 )
 
-        word_window = keep.tile([P, T], U32, name="word_window", tag="raw_wx_4_0", align_bytes=DMA_ALIGN)
+        word_window = load_tile([P, T], U32, "word_window", "place_words")
 
         def load_words():
             nc.sync.dma_start(out=word_window[:].bitcast(I32), in_=tab_words[0].rearrange("p t z -> p (t z)").bitcast(I32))
@@ -122,12 +130,13 @@ def tile_list_tiert_silu_kernel(tc, tab_words, tab_scales, wt, x, wx, b, offs, o
                 nc.sync.dma_start(out=moved_scales[r:P:32, :].bitcast(I32), in_=tab_planes[0][PASS_GAP + r : P : 32, :].bitcast(I32))
             tab_planes[1] = moved_scales
 
+        bias = {}
+
         def turn_bias():
             turned = bank([P, PACK, P])
             nc.tensor.transpose(turned[:, 0, :], bias_rows[:], unit[:])
-            kept = scalar_tile([P, N // P], F32, "bias")
-            nc.scalar.copy(out=kept[:], in_=turned[:, 0, 0 : N // P])
-            return kept
+            bias[0] = scalar_tile([P, TILES], F32, "bias")
+            nc.scalar.copy(out=bias[0][:], in_=turned[:, 0, 0:TILES])
 
         def woven(ap):
             return ap.rearrange("p (c i t) -> p c t i", i=RUN, t=PACK)
@@ -149,12 +158,13 @@ def tile_list_tiert_silu_kernel(tc, tab_words, tab_scales, wt, x, wx, b, offs, o
 
         rounded = {}
 
-        def round_chunk(name, a, first, on_vector=False):
-            tile = (vector_tile if on_vector else scalar_tile)([P, PAIR * P * PACK], BF16, "rounded")
-            source = by_runs(raw_columns(name, a, first, PAIR))
-            if on_vector:
+        def round_chunk(name, a, first, on="scalar", count=PAIR):
+            source = by_runs(raw_columns(name, a, first, count))
+            if on == "vector":
+                tile = vector_tile([P, count * P * PACK], BF16, "rounded")
                 nc.vector.tensor_copy(out=woven(tile[:]), in_=source)
             else:
+                tile = scalar_tile([P, count * P * PACK], BF16, "rounded")
                 nc.scalar.copy(out=woven(tile[:]), in_=source)
             rounded[name, a, first] = tile
 
@@ -186,8 +196,8 @@ def tile_list_tiert_silu_kernel(tc, tab_words, tab_scales, wt, x, wx, b, offs, o
             for t in range(PACK):
                 nc.tensor.matmul_mx(
                     out=backs[n, a][:, t, :],
-                    lhsT=ident_codes[:, t * P : (t + 1) * P].bitcast(FP8X4),
-                    lhsT_scale=ident_scales[:, t * P : (t + 1) * P],
+                    lhsT=ident["codes"][:, t * P : (t + 1) * P].bitcast(FP8X4),
+                    lhsT_scale=ident["scales"][:, t * P : (t + 1) * P],
                     rhs=codes.bitcast(FP8X4),
                     rhs_scale=scales,
                     start=True,
@@ -231,8 +241,8 @@ def tile_list_tiert_silu_kernel(tc, tab_words, tab_scales, wt, x, wx, b, offs, o
             plane = tab_planes[a][:, h * WIDTH + first : h * WIDTH + first + width]
             add_pass(n, h * WIDTH + first, operand, a, rhs, plane)
 
-        def table_passes(n, h, first=0, width=WIDTH):
-            for a in range(PASSES):
+        def table_passes(n, h, first=0, width=WIDTH, passes=range(PASSES)):
+            for a in passes:
                 for operand in ("wt", "wr"):
                     table_pass(n, h, a, operand, first, width)
 
@@ -241,169 +251,117 @@ def tile_list_tiert_silu_kernel(tc, tab_words, tab_scales, wt, x, wx, b, offs, o
             cols = slice(first, first + width)
             add_pass(n, h * WIDTH + first, "wx", a, codes[:, cols].bitcast(FP8X4), scales[:, cols])
 
+        results = {}
+
         def finish(n, h, first=0, width=WIDTH):
             start = h * WIDTH + first
-            result = scalar_tile([P, width], F32, "result_%d" % n)
-            nc.scalar.activation(out=result[:], in_=sums[n, start][:], func=SILU, bias=bias[:, n : n + 1])
-            nc.sync.dma_start(out=out[n * P : (n + 1) * P, start : start + width], in_=result[:])
+            results[n, start] = scalar_tile([P, width], F32, "result_%d" % n)
+            nc.scalar.activation(out=results[n, start][:], in_=sums[n, start][:], func=ACT.Silu, bias=bias[0][:, n : n + 1])
 
-        load_bias()
-        load_scales()
-        load_words()
-        for a in range(PASSES):
-            load("wt", a, 0)
-        pick_scales()
-        load("wt", 0, 1)
-        move_scales()
-        for a in range(PASSES):
-            load("x", a, 0)
-            load("wx", a, 0)
-        load("wt", 1, 1)
-        for name in ("x", "wx"):
-            for a in range(PASSES):
-                load(name, a, 1)
+        def store(n, h, first=0, width=WIDTH):
+            start = h * WIDTH + first
+            nc.sync.dma_start(out=out[n * P : (n + 1) * P, start : start + width], in_=results[n, start][:])
 
-        bias = turn_bias()
-        pick_words(0)
-        pick_words(1)
-        round_chunk("wt", 0, 0, on_vector=True)
-        part_words(0)
-        quantize_chunk("wt", 0, 0)
-        round_chunk("wt", 0, PAIR)
+        def rounding(name, a, first, on="scalar", count=PAIR):
+            return round_chunk, (name, a, first, on, count), [("raw", name, a, first)], [("rounded", name, a, first)]
 
-        early = [(a, side * GROUPS + first) for a, side in ((0, 0), (1, 0), (0, 1)) for first in (0, PAIR)]
-        for a, first in early[2:]:
-            round_chunk("wt", a, first)
-        for name in ("x", "wx"):
-            for first in (0, PAIR):
-                round_chunk(name, 0, first)
-        round_chunk("x", 1, 0)
-        round_chunk("wx", 1, PAIR)
+        def quantising(name, a, first, count=PAIR):
+            if name == "wr":
+                needs = [("rest", a, first + g) for g in range(count)]
+            else:
+                needs = [("rounded", name, a, first)]
+            return quantize_chunk, (name, a, first), needs, [(name, a, first + g) for g in range(count)]
 
-        def bring_back_chunk(a, first):
-            for n in (first, first + 1):
-                bring_back(n, a)
+        def bringing(n, a):
+            return bring_back, (n, a), ["identity", ("wt", a, n)], [("back", a, n)]
 
-        def first_half_passes(operand, a, first):
-            if first < GROUPS:
-                for n in (first, first + 1):
-                    table_pass(n, 0, a, operand)
+        def subtracting(n, a, alone=False):
+            return subtract, (n, a, alone), [("back", a, n)], [("rest", a, n)]
 
-        bring_back_chunk(*early[0])
-        quantize_chunk("wt", *early[1])
-        part_words(1)
-        bring_back_chunk(*early[1])
-        for n in range(GROUPS):
-            open_sum(n, 0)
-            table_pass(n, 0, 0, "wt")
+        def opening(n, h, first=0, width=WIDTH):
+            return open_sum, (n, h, first, width), [], []
 
-        tiles = [(n, a) for a, first in early for n in (first, first + 1)]
-        brought, opened = 2 * PAIR, 0
-        waiting = []
-        for i, (a, first) in enumerate(early[:-1]):
-            at_hand = set(weights)
-            subtract(first, a)
-            if i > 0:
-                quantize_chunk("wr", *early[i - 1])
-            subtract(first + 1, a)
-            if i + 2 < len(early):
-                quantize_chunk("wt", *early[i + 2])
-            for spent in (PAIR * i, PAIR * i + 1):
-                if brought < len(tiles) and (tiles[brought][0] < GROUPS or brought - spent <= BACK_AHEAD):
-                    bring_back(*tiles[brought])
-                    brought += 1
-                else:
-                    open_sum(opened, 1)
-                    table_pass(opened, 1, 0, "wt")
-                    waiting += [("wr", opened, 0), ("wt", opened, 1), ("wr", opened, 1)]
-                    opened += 1
-            for operand, n, a_pass in [key for key in waiting if key in at_hand]:
-                table_pass(n, 1, a_pass, operand)
-                waiting.remove((operand, n, a_pass))
-            if i > 0:
-                first_half_passes("wr", *early[i - 1])
-                first_half_passes("wt", *early[i + 1])
+        def with_table(n, h, a, operand, first=0, width=WIDTH):
+            return table_pass, (n, h, a, operand, first, width), [(operand, a, n), ("table", h), ("plane", a)], [("pass", n, h, first, operand, a)]
 
-        a, first = early[-1]
-        for chunk in (0, PAIR):
-            quantize_chunk("x", 0, chunk)
-        subtract(first, a, alone=True)
-        round_chunk("x", 1, PAIR, on_vector=True)
-        for chunk in (0, PAIR):
-            quantize_chunk("wx", 0, chunk)
-        round_chunk("wx", 1, 0, on_vector=True)
-        for chunk in (PAIR, 0):
-            quantize_chunk("x", 1, chunk)
-        quantize_chunk("wx", 1, 0)
-        subtract(first + 1, a, alone=True)
-        quantize_chunk("wx", 1, PAIR)
-        for a_x in range(PASSES):
-            for n in range(GROUPS):
-                x_pass(n, 0, a_x)
-        for n in range(opened, GROUPS):
-            open_sum(n, 1)
-            table_passes(n, 1)
-        for n in range(GROUPS):
-            finish(n, 0)
+        def with_x(n, h, a, first=0, width=WIDTH):
+            needs = [("wx", a, n)] + [("x", a, h * SIDE + g) for g in range(SIDE)]
+            return x_pass, (n, h, a, first, width), needs, [("pass", n, h, first, "wx", a)]
 
-        late = [(1, GROUPS), (1, GROUPS + PAIR)]
-        round_chunk("wt", *late[0], on_vector=True)
-        quantize_chunk("wr", *early[-2])
-        quantize_chunk("wt", *late[0])
-        round_chunk("wt", *late[1], on_vector=True)
-        quantize_chunk("wr", a, first)
-        quantize_chunk("wt", *late[1])
-        quantize_chunk("wr", a, first + 1)
-        for name, a_late, chunk in (("x", 0, GROUPS), ("x", 0, GROUPS + PAIR), ("x", 1, GROUPS), ("wx", 0, GROUPS + PAIR)):
-            round_chunk(name, a_late, chunk)
+        def finishing(n, h, first=0, width=WIDTH):
+            needs = ["bias"] + [("pass", n, h, first, operand, a) for operand in ("wt", "wr", "wx") for a in range(PASSES)]
+            return finish, (n, h, first, width), needs, [("result", n, h, first)]
 
-        pair = range(GROUPS, GROUPS + PAIR)
-        bring_back_chunk(*late[0])
-        for n in pair:
-            open_sum(n, 0)
-            for operand in ("wt", "wr"):
-                table_pass(n, 0, 0, operand)
-        for n in pair:
-            subtract(n, 1)
-        quantize_chunk("wr", *late[0])
-        bring_back_chunk(*late[1])
-        for operand in ("wt", "wr"):
-            for n in pair:
-                table_pass(n, 0, 1, operand)
-        for chunk in range(PAIR):
-            subtract(GROUPS + PAIR + chunk, 1)
-            quantize_chunk("x", 0, GROUPS + chunk * PAIR)
+        def storing(n, h, first=0, width=WIDTH):
+            return store, (n, h, first, width), [("result", n, h, first)], []
 
-        round_chunk("x", 1, GROUPS + PAIR, on_vector=True)
-        quantize_chunk("wr", *late[1])
-        for chunk in (GROUPS, GROUPS + PAIR):
-            quantize_chunk("x", 1, chunk)
-        round_chunk("wx", 0, GROUPS, on_vector=True)
-        for chunk in (GROUPS + PAIR, GROUPS):
-            quantize_chunk("wx", 0, chunk)
-        for chunk in (GROUPS, GROUPS + PAIR):
-            round_chunk("wx", 1, chunk, on_vector=True)
-        for chunk in (GROUPS, GROUPS + PAIR):
-            quantize_chunk("wx", 1, chunk)
-        for a_x in range(PASSES):
-            for n in range(GROUPS):
-                x_pass(n, 1, a_x)
-        for n in range(GROUPS + PAIR, N // P):
-            open_sum(n, 0)
-            table_passes(n, 0)
-        for n in range(GROUPS):
-            finish(n, 1)
+        def loading(name, a, first, place=None, needs=()):
+            return load, (name, a, first, PAIR, place), list(needs), [("raw", name, a, first + g) for g in range(PAIR)]
 
-        for a_x in range(PASSES):
-            for n in range(GROUPS, N // P):
-                x_pass(n, 0, a_x)
-        for n in range(GROUPS, N // P):
-            finish(n, 0)
-        pieces = [(n, 0, WIDTH) for n in range(GROUPS, N // P - 1)]
-        pieces += [(N // P - 1, 0, 2 * P), (N // P - 1, 2 * P, P), (N // P - 1, 3 * P, P)]
-        for n, start, width in pieces:
-            open_sum(n, 1, start, width)
-            table_passes(n, 1, start, width)
-            for a_x in range(PASSES):
-                x_pass(n, 1, a_x, start, width)
-            finish(n, 1, start, width)
+        def write_out(queues, made):
+            while any(queues):
+                moved = False
+                for queue in queues:
+                    while queue and all(key in made for key in queue[0][2]):
+                        call, arguments, needs, makes = queue.pop(0)
+                        call(*arguments)
+                        made.extend(makes)
+                        moved = True
+                assert moved
+
+        R, Q, I, S, O, TB, X, F, LD = rounding, quantising, bringing, subtracting, opening, with_table, with_x, finishing, loading
+        V = "vector"
+        pieces = ((0, 2 * P), (2 * P, P), (3 * P, P))
+        sync = [(load_bias, (), [], []), (load_scales, (), [], []), LD("wt", 0, 0, "a"), (load_words, (), [], ["words"]), LD("wt", 0, 2, "b"), LD("wt", 1, 0, "c"), LD("wt", 1, 2, "d")]
+        sync += [(move_scales, (), [("plane", 0)], [("plane", 1)])]
+        sync += [LD("x", 0, 0), LD("x", 0, 2), LD("wx", 0, 0), LD("wx", 0, 2), LD("x", 1, 0), LD("wx", 1, 0), LD("x", 1, 2), LD("wx", 1, 2)]
+        sync += [LD("wt", 0, 4), LD("wt", 0, 6)] + [LD("x", a, first) for a in range(PASSES) for first in (4, 6)]
+        sync += [LD("wt", 1, 4, "a", [("rest", 0, 1)]), LD("wt", 1, 6, "b", [("rest", 0, 3)]), LD("wx", 0, 4, "c", [("rest", 1, 1)])]
+        sync += [LD("wx", 1, 4, "place_ones", ["identity"]), LD("wx", 0, 6, "d", [("rest", 1, 3)]), LD("wx", 1, 6, "place_words", [("table", 1)])]
+        sync += [storing(n, h) for h in (0, 1) for n in range(SIDE)]
+        sync += [storing(n, h) for n, h in ((4, 0), (5, 0), (4, 1), (5, 1), (6, 0), (7, 0), (6, 1))]
+        sync += [storing(7, 1, start, width) for start, width in pieces]
+
+        vector = [
+            (pick_scales, (), [], [("plane", 0)]), (quantize_identity, (), [], ["identity"]), Q("wt", 0, 0),
+            (pick_words, (0,), ["words"], []), S(0, 0), (part_words, (0,), [], [("table", 0)]), S(1, 0), Q("wt", 0, 2), Q("wr", 0, 0),
+            (pick_words, (1,), [], []), Q("wt", 1, 0), (part_words, (1,), [], [("table", 1)]), S(2, 0), Q("wt", 1, 2), S(3, 0),
+            S(0, 1), Q("wr", 0, 2), S(1, 1), Q("x", 0, 0), Q("wr", 1, 0), S(2, 1), Q("x", 0, 2), S(3, 1), Q("wx", 0, 0), Q("wr", 1, 2), Q("wx", 0, 2),
+            Q("x", 1, 0), R("x", 1, 2, V), Q("wx", 1, 0), Q("x", 1, 2), R("wx", 1, 2, V), Q("wx", 1, 2),
+            R("wt", 0, 4, V, 1), R("wt", 0, 5, V, 1), Q("wt", 0, 4, 1), Q("wt", 0, 5, 1), R("wt", 0, 6, V), S(4, 0), Q("wt", 0, 6), S(5, 0),
+            Q("wr", 0, 4), S(6, 0), S(7, 0), Q("x", 0, 4), Q("wr", 0, 6), Q("x", 0, 6),
+            R("x", 1, 6, V), Q("x", 1, 4), Q("x", 1, 6),
+            R("wt", 1, 4, V, 1), R("wt", 1, 5, V, 1), Q("wt", 1, 4, 1), Q("wt", 1, 5, 1), R("wt", 1, 6, V), Q("wt", 1, 6), R("wx", 0, 4, V), S(4, 1), S(5, 1), Q("wx", 0, 4), Q("wr", 1, 4), S(6, 1), S(7, 1),
+            Q("wx", 1, 4), Q("wr", 1, 6), R("wx", 1, 6, V), Q("wx", 0, 6), Q("wx", 1, 6),
+        ]
+        scalar = [(turn_bias, (), [], ["bias"])] + [R("wt", a, first) for a in range(PASSES) for first in (0, 2)]
+        scalar += [R("x", 0, 0), R("x", 0, 2), R("wx", 0, 0), R("wx", 0, 2), R("x", 1, 0), R("wx", 1, 0)]
+        scalar += [F(n, 0) for n in range(SIDE)] + [R("x", 0, 4), R("x", 0, 6), R("x", 1, 4)]
+        scalar += [F(n, 1) for n in range(SIDE)] + [R("wx", 1, 4), R("wx", 0, 6)]
+        scalar += [F(n, h) for n, h in ((4, 0), (5, 0), (4, 1), (5, 1), (6, 0), (7, 0), (6, 1))] + [F(7, 1, start, width) for start, width in pieces]
+
+        both = [(a, operand) for a in range(PASSES) for operand in ("wt", "wr")]
+        tensor = [I(0, 0), I(1, 0), O(0, 0), TB(0, 0, 0, "wt"), O(1, 0), TB(1, 0, 0, "wt"), I(2, 0), I(3, 0)]
+        tensor += [O(2, 0), TB(2, 0, 0, "wt"), O(3, 0), TB(3, 0, 0, "wt"), TB(0, 0, 0, "wr"), TB(1, 0, 0, "wr")]
+        tensor += [I(0, 1), I(1, 1), TB(0, 0, 1, "wt"), TB(1, 0, 1, "wt")]
+        tensor += [O(0, 1)] + [TB(0, 1, a, operand) for a, operand in both[:3]]
+        tensor += [O(1, 1), TB(1, 1, 0, "wt"), TB(1, 1, 0, "wr"), I(2, 1), TB(1, 1, 1, "wt"), TB(2, 0, 0, "wr"), I(3, 1), TB(3, 0, 0, "wr")]
+        tensor += [TB(2, 0, 1, "wt"), TB(3, 0, 1, "wt")] + [TB(n, 0, 1, "wr") for n in range(SIDE)]
+        tensor += [X(n, 0, 0) for n in range(SIDE)]
+        tensor += [TB(0, 1, 1, "wr"), TB(1, 1, 1, "wr"), O(2, 1), TB(2, 1, 0, "wt"), TB(2, 1, 0, "wr"), X(0, 0, 1), X(1, 0, 1), TB(2, 1, 1, "wt"), TB(2, 1, 1, "wr"), X(2, 0, 1), X(3, 0, 1)]
+        tensor += [I(4, 0), I(5, 0), O(3, 1)] + [TB(3, 1, a, operand) for a, operand in both]
+        tensor += [I(6, 0), I(7, 0)]
+        for n in (4, 5):
+            tensor += [O(n, 0), TB(n, 0, 0, "wt"), TB(n, 0, 0, "wr")]
+        tensor += [O(6, 0), TB(6, 0, 0, "wt"), O(7, 0), TB(7, 0, 0, "wt")]
+        tensor += [X(n, 1, 0) for n in range(SIDE)] + [TB(6, 0, 0, "wr"), TB(7, 0, 0, "wr")] + [X(n, 1, 1) for n in range(SIDE)]
+        tensor += [TB(4, 0, 1, "wt"), I(4, 1), TB(5, 0, 1, "wt"), I(5, 1), TB(6, 0, 1, "wt"), TB(7, 0, 1, "wt")]
+        tensor += [O(4, 1), TB(4, 1, 0, "wt"), TB(4, 1, 0, "wr"), O(5, 1), TB(5, 1, 0, "wt"), I(6, 1), TB(5, 1, 0, "wr"), TB(4, 1, 1, "wt"), I(7, 1), TB(5, 1, 1, "wt")]
+        tensor += [TB(n, h, 1, "wr") for h in (0, 1) for n in (4, 5)]
+        tensor += [O(6, 1), TB(6, 1, 0, "wt")] + [X(n, h, a) for a in range(PASSES) for h in (0, 1) for n in (4, 5)]
+        tensor += [TB(6, 0, 1, "wr"), TB(7, 0, 1, "wr")] + [X(n, 0, a) for a in range(PASSES) for n in (6, 7)]
+        tensor += [TB(6, 1, a, operand) for a, operand in both[1:]] + [X(6, 1, a) for a in range(PASSES)]
+        for start, width in pieces:
+            tensor += [O(7, 1, start, width)] + [TB(7, 1, a, operand, start, width) for a, operand in both]
+            tensor += [X(7, 1, a, start, width) for a in range(PASSES)]
+        write_out([sync, vector, scalar, tensor], [])

from contextlib import ExitStack

import concourse.mybir as mybir

K, L, N, T, J = 1024, 1024, 1024, 2048, 1024
FLOPS = 2 * N * J * (2 * K + L) + 2 * 512 * K * N

F32 = mybir.dt.float32
BF16 = mybir.dt.bfloat16
I32 = mybir.dt.int32
U32 = mybir.dt.uint32
U16 = mybir.dt.uint16
U8 = mybir.dt.uint8
FP8X4 = mybir.dt.float8_e4m3fn_x4
FP4X4 = mybir.dt.float4_e2m1fn_x4
ACT = mybir.ActivationFunctionType
ALU = mybir.AluOpType

P = 128
PACK = 4
K_PASS = P * PACK
PASSES = K // K_PASS
WIDTH = 512
TILES = N // P
SIDE = TILES // 2
PAIR = 2
RUN = 4
DMA_ALIGN = 256
LIST_ROWS = 16
PASS_GAP = 16
BANKS = 8
VECTOR_SLOTS = 45
SCALAR_SLOTS = 17


def tile_list_tiert_silu_kernel(tc, tab_words, tab_scales, wt, x, wx, b, offs, out):
    nc = tc.nc
    with ExitStack() as ctx:
        keep = ctx.enter_context(tc.tile_pool(name="keep", bufs=1))
        psum = ctx.enter_context(tc.psum_pool(name="psum", bufs=1))

        def bank(shape):
            return psum.tile(shape, F32, name="bank", tag="bank", bufs=BANKS)

        def vector_tile(shape, dtype, name):
            return keep.tile(shape, dtype, name=name, tag="vector_turn", bufs=VECTOR_SLOTS, align_bytes=64)

        def scalar_tile(shape, dtype, name):
            return keep.tile(shape, dtype, name=name, tag="scalar_turn", bufs=SCALAR_SLOTS, align_bytes=DMA_ALIGN)

        def load_tile(shape, dtype, name, place):
            return keep.tile(shape, dtype, name=name, tag=place, align_bytes=DMA_ALIGN)

        def quantize(rounded, name):
            width = rounded.shape[1] // PACK
            if width < WIDTH:
                both = vector_tile([P, (PACK + 1) * width], U8, name + "_codes")
                codes, scales = both[:, 0 : PACK * width].bitcast(U32), both[:, PACK * width :]
            else:
                codes = vector_tile([P, width], U32, name + "_codes")[:]
                scales = keep.tile([P, width], U8, name=name + "_scales", align_bytes=64)[:]
            nc.vector.quantize_mx(out=codes.bitcast(FP8X4), scales=scales, in_=rounded)
            return codes, scales

        offsets = keep.tile([P, J // LIST_ROWS], U16, name="offsets")
        nc.sync.dma_start(offsets[:], offs)

        zero = keep.tile([P, 1], F32, name="zero")
        nc.vector.memset(zero[:], 0.0)
        warm = keep.tile([P, 1], F32, name="warm")
        nc.scalar.activation(out=warm[:], in_=zero[:], func=ACT.Silu)

        bias_rows = keep.tile([P, P], F32, name="bias_rows")
        nc.vector.memset(bias_rows[:], 0.0)
        scale_window = keep.tile([P, T], U8, name="scale_window", align_bytes=64)
        nc.vector.memset(scale_window[:].bitcast(I32), 0)
        moved_scales = keep.tile([P, J], U8, name="moved_scales", align_bytes=64)
        nc.vector.memset(moved_scales[:].bitcast(I32), 0)

        ahead = keep.tile([P, K_PASS], BF16, name="ahead", align_bytes=64)
        nc.gpsimd.iota(ahead[:], [[1, K_PASS]], base=0, channel_multiplier=-PACK, allow_small_or_imprecise_dtypes=True)
        ones = load_tile([P, PACK, K_PASS], BF16, "ones", "place_ones")
        for t in range(PACK):
            nc.vector.tensor_scalar(out=ones[:, t, :], in0=ahead[:], scalar1=float(t), scalar2=None, op0=ALU.is_equal)
        unit = vector_tile([P, P], F32, "unit")
        nc.vector.tensor_scalar(out=unit[:], in0=ahead[:, 0:K_PASS:PACK], scalar1=0.0, scalar2=None, op0=ALU.is_equal)
        ident = {}

        def quantize_identity():
            ident["codes"], ident["scales"] = quantize(ones[:].rearrange("p t w -> p (t w)"), "ident")

        inputs = {"wt": wt, "wx": wx, "x": x}
        raw = {}

        def load(name, a, first, count, place=None):
            label = "raw_%s_%d_%d" % (name, first, a)
            tile = load_tile([P, PACK, count * P], F32, label, place or label)
            rows = inputs[name][a * K_PASS : (a + 1) * K_PASS, first * P : (first + count) * P]
            nc.sync.dma_start(out=tile[:], in_=rows.rearrange("(p t) w -> p t w", t=PACK))
            for g in range(count):
                raw[name, a, first + g] = tile, g

        def raw_columns(name, a, first, count):
            tile, g = raw[name, a, first]
            return tile[:, :, g * P : (g + count) * P]

        def load_bias():
            nc.sync.dma_start(out=bias_rows[0:TILES, :], in_=b.rearrange("(c p) -> c p", p=P))

        def load_scales():
            for r in range(4):
                nc.sync.dma_start(
                    out=scale_window[r:P:PASS_GAP, :].bitcast(I32),
                    in_=tab_scales[:, r:16:4, :].rearrange("a q t -> q a t").bitcast(I32),
                )

        word_window = load_tile([P, T], U32, "word_window", "place_words")

        def load_words():
            nc.sync.dma_start(out=word_window[:].bitcast(I32), in_=tab_words[0].rearrange("p t z -> p (t z)").bitcast(I32))

        tab_planes = {}

        def pick_scales():
            tab_planes[0] = vector_tile([P, J], U8, "picked_scales")
            nc.vector.tensor_copy(tab_planes[0][:], scale_window[:].indirect(offsets[:]))

        def move_scales():
            for r in range(4):
                nc.sync.dma_start(out=moved_scales[r:P:32, :].bitcast(I32), in_=tab_planes[0][PASS_GAP + r : P : 32, :].bitcast(I32))
            tab_planes[1] = moved_scales

        bias = {}

        def turn_bias():
            turned = bank([P, PACK, P])
            nc.tensor.transpose(turned[:, 0, :], bias_rows[:], unit[:])
            bias[0] = scalar_tile([P, TILES], F32, "bias")
            nc.scalar.copy(out=bias[0][:], in_=turned[:, 0, 0:TILES])

        def woven(ap):
            return ap.rearrange("p (c i t) -> p c t i", i=RUN, t=PACK)

        def by_runs(ap):
            return ap.rearrange("p t (c i) -> p c t i", i=RUN)

        picked = {}
        tab_codes = {}

        def pick_words(h):
            picked[h] = vector_tile([P, WIDTH], U32, "picked_%d" % h)[:]
            entries = offsets[:, h * WIDTH // LIST_ROWS : (h + 1) * WIDTH // LIST_ROWS]
            nc.vector.tensor_copy(picked[h], word_window[:].indirect(entries))

        def part_words(h):
            tab_codes[h] = vector_tile([P, PASSES, 2 * WIDTH], U8, "parted_%d" % h)
            nc.vector.tensor_copy(out=tab_codes[h][:].bitcast(U16), in_=picked[h].bitcast(U16).rearrange("p (s a) -> p a s", a=PASSES))

        rounded = {}

        def round_chunk(name, a, first, on="scalar", count=PAIR):
            source = by_runs(raw_columns(name, a, first, count))
            if on == "vector":
                tile = vector_tile([P, count * P * PACK], BF16, "rounded")
                nc.vector.tensor_copy(out=woven(tile[:]), in_=source)
            else:
                tile = scalar_tile([P, count * P * PACK], BF16, "rounded")
                nc.scalar.copy(out=woven(tile[:]), in_=source)
            rounded[name, a, first] = tile

        weights = {}
        tokens = {}

        def quantize_chunk(name, a, first):
            source = rounded[name, a, first][:]
            count = source.shape[1] // (P * PACK)
            if name == "x":
                h, start = divmod(first * P, WIDTH)
                if (h, a) not in tokens:
                    codes = vector_tile([P, WIDTH], U32, "x_%d_%d_codes" % (h, a))
                    scales = keep.tile([P, WIDTH], U8, name="x_%d_%d_scales" % (h, a), align_bytes=64)
                    tokens[h, a] = codes, scales
                codes, scales = tokens[h, a]
                cols = slice(start, start + count * P)
                nc.vector.quantize_mx(out=codes[:, cols].bitcast(FP8X4), scales=scales[:, cols], in_=source)
            else:
                codes, scales = quantize(source, "%s_%d_%d" % (name, first, a))
                for g in range(count):
                    weights[name, first + g, a] = codes[:, g * P : (g + 1) * P], scales[:, g * P : (g + 1) * P]

        backs = {}

        def bring_back(n, a):
            codes, scales = weights["wt", n, a]
            backs[n, a] = bank([P, PACK, P])
            for t in range(PACK):
                nc.tensor.matmul_mx(
                    out=backs[n, a][:, t, :],
                    lhsT=ident["codes"][:, t * P : (t + 1) * P].bitcast(FP8X4),
                    lhsT_scale=ident["scales"][:, t * P : (t + 1) * P],
                    rhs=codes.bitcast(FP8X4),
                    rhs_scale=scales,
                    start=True,
                    stop=True,
                )

        def subtract(n, a, alone=False):
            first, count = (n, 1) if alone else (n - n % PAIR, PAIR)
            if n == first:
                rounded["wr", a, first] = vector_tile([P, count * P * PACK], BF16, "rest")
            tile, g = rounded["wr", a, first], n - first
            nc.vector.tensor_tensor(
                out=woven(tile[:, g * P * PACK : (g + 1) * P * PACK]),
                in0=by_runs(raw_columns("wt", a, n, 1)),
                in1=by_runs(backs[n, a][:]),
                op=ALU.subtract,
            )

        sums = {}
        done = {}

        def add_pass(n, first, operand, a, rhs, rhs_scale):
            codes, scales = weights[operand, n, a]
            nc.tensor.matmul_mx(
                out=sums[n, first][:],
                lhsT=codes.bitcast(FP8X4),
                lhsT_scale=scales,
                rhs=rhs,
                rhs_scale=rhs_scale,
                start=done[n, first] == 0,
                stop=done[n, first] == 3 * PASSES - 1,
            )
            done[n, first] += 1

        def open_sum(n, h, first=0, width=WIDTH):
            sums[n, h * WIDTH + first] = bank([P, width])
            done[n, h * WIDTH + first] = 0

        def table_pass(n, h, a, operand, first=0, width=WIDTH):
            rhs = tab_codes[h][:, a, 2 * first : 2 * (first + width)].bitcast(FP4X4)
            plane = tab_planes[a][:, h * WIDTH + first : h * WIDTH + first + width]
            add_pass(n, h * WIDTH + first, operand, a, rhs, plane)

        def table_passes(n, h, first=0, width=WIDTH, passes=range(PASSES)):
            for a in passes:
                for operand in ("wt", "wr"):
                    table_pass(n, h, a, operand, first, width)

        def x_pass(n, h, a, first=0, width=WIDTH):
            codes, scales = tokens[h, a]
            cols = slice(first, first + width)
            add_pass(n, h * WIDTH + first, "wx", a, codes[:, cols].bitcast(FP8X4), scales[:, cols])

        results = {}

        def finish(n, h, first=0, width=WIDTH):
            start = h * WIDTH + first
            results[n, start] = scalar_tile([P, width], F32, "result_%d" % n)
            nc.scalar.activation(out=results[n, start][:], in_=sums[n, start][:], func=ACT.Silu, bias=bias[0][:, n : n + 1])

        def store(n, h, first=0, width=WIDTH):
            start = h * WIDTH + first
            nc.sync.dma_start(out=out[n * P : (n + 1) * P, start : start + width], in_=results[n, start][:])

        def rounding(name, a, first, on="scalar", count=PAIR):
            return round_chunk, (name, a, first, on, count), [("raw", name, a, first)], [("rounded", name, a, first)]

        def quantising(name, a, first, count=PAIR):
            if name == "wr":
                needs = [("rest", a, first + g) for g in range(count)]
            else:
                needs = [("rounded", name, a, first)]
            return quantize_chunk, (name, a, first), needs, [(name, a, first + g) for g in range(count)]

        def bringing(n, a):
            return bring_back, (n, a), ["identity", ("wt", a, n)], [("back", a, n)]

        def subtracting(n, a, alone=False):
            return subtract, (n, a, alone), [("back", a, n)], [("rest", a, n)]

        def opening(n, h, first=0, width=WIDTH):
            return open_sum, (n, h, first, width), [], []

        def with_table(n, h, a, operand, first=0, width=WIDTH):
            return table_pass, (n, h, a, operand, first, width), [(operand, a, n), ("table", h), ("plane", a)], [("pass", n, h, first, operand, a)]

        def with_x(n, h, a, first=0, width=WIDTH):
            needs = [("wx", a, n)] + [("x", a, h * SIDE + g) for g in range(SIDE)]
            return x_pass, (n, h, a, first, width), needs, [("pass", n, h, first, "wx", a)]

        def finishing(n, h, first=0, width=WIDTH):
            needs = ["bias"] + [("pass", n, h, first, operand, a) for operand in ("wt", "wr", "wx") for a in range(PASSES)]
            return finish, (n, h, first, width), needs, [("result", n, h, first)]

        def storing(n, h, first=0, width=WIDTH):
            return store, (n, h, first, width), [("result", n, h, first)], []

        def loading(name, a, first, place=None, needs=()):
            return load, (name, a, first, PAIR, place), list(needs), [("raw", name, a, first + g) for g in range(PAIR)]

        def write_out(queues, made):
            while any(queues):
                moved = False
                for queue in queues:
                    while queue and all(key in made for key in queue[0][2]):
                        call, arguments, needs, makes = queue.pop(0)
                        call(*arguments)
                        made.extend(makes)
                        moved = True
                assert moved

        R, Q, I, S, O, TB, X, F, LD = rounding, quantising, bringing, subtracting, opening, with_table, with_x, finishing, loading
        V = "vector"
        pieces = ((0, 2 * P), (2 * P, P), (3 * P, P))
        sync = [(load_bias, (), [], []), (load_scales, (), [], []), LD("wt", 0, 0, "a"), (load_words, (), [], ["words"]), LD("wt", 0, 2, "b"), LD("wt", 1, 0, "c"), LD("wt", 1, 2, "d")]
        sync += [(move_scales, (), [("plane", 0)], [("plane", 1)])]
        sync += [LD("x", 0, 0), LD("x", 0, 2), LD("wx", 0, 0), LD("wx", 0, 2), LD("x", 1, 0), LD("wx", 1, 0), LD("x", 1, 2), LD("wx", 1, 2)]
        sync += [LD("wt", 0, 4), LD("wt", 0, 6)] + [LD("x", a, first) for a in range(PASSES) for first in (4, 6)]
        sync += [LD("wt", 1, 4, "a", [("rest", 0, 1)]), LD("wt", 1, 6, "b", [("rest", 0, 3)]), LD("wx", 0, 4, "c", [("rest", 1, 1)])]
        sync += [LD("wx", 1, 4, "place_ones", ["identity"]), LD("wx", 0, 6, "d", [("rest", 1, 3)]), LD("wx", 1, 6, "place_words", [("table", 1)])]
        sync += [storing(n, h) for h in (0, 1) for n in range(SIDE)]
        sync += [storing(n, h) for n, h in ((4, 0), (5, 0), (4, 1), (5, 1), (6, 0), (7, 0), (6, 1))]
        sync += [storing(7, 1, start, width) for start, width in pieces]

        vector = [
            (pick_scales, (), [], [("plane", 0)]), (quantize_identity, (), [], ["identity"]), Q("wt", 0, 0),
            (pick_words, (0,), ["words"], []), S(0, 0), (part_words, (0,), [], [("table", 0)]), S(1, 0), Q("wt", 0, 2), Q("wr", 0, 0),
            (pick_words, (1,), [], []), Q("wt", 1, 0), (part_words, (1,), [], [("table", 1)]), S(2, 0), Q("wt", 1, 2), S(3, 0),
            S(0, 1), Q("wr", 0, 2), S(1, 1), Q("x", 0, 0), Q("wr", 1, 0), S(2, 1), Q("x", 0, 2), S(3, 1), Q("wx", 0, 0), Q("wr", 1, 2), Q("wx", 0, 2),
            Q("x", 1, 0), R("x", 1, 2, V), Q("wx", 1, 0), Q("x", 1, 2), R("wx", 1, 2, V), Q("wx", 1, 2),
            R("wt", 0, 4, V, 1), R("wt", 0, 5, V, 1), Q("wt", 0, 4, 1), Q("wt", 0, 5, 1), R("wt", 0, 6, V), S(4, 0), Q("wt", 0, 6), S(5, 0),
            Q("wr", 0, 4), S(6, 0), S(7, 0), Q("x", 0, 4), Q("wr", 0, 6), Q("x", 0, 6),
            R("x", 1, 6, V), Q("x", 1, 4), Q("x", 1, 6),
            R("wt", 1, 4, V, 1), R("wt", 1, 5, V, 1), Q("wt", 1, 4, 1), Q("wt", 1, 5, 1), R("wt", 1, 6, V), Q("wt", 1, 6), R("wx", 0, 4, V), S(4, 1), S(5, 1), Q("wx", 0, 4), Q("wr", 1, 4), S(6, 1), S(7, 1),
            Q("wx", 1, 4), Q("wr", 1, 6), R("wx", 1, 6, V), Q("wx", 0, 6), Q("wx", 1, 6),
        ]
        scalar = [(turn_bias, (), [], ["bias"])] + [R("wt", a, first) for a in range(PASSES) for first in (0, 2)]
        scalar += [R("x", 0, 0), R("x", 0, 2), R("wx", 0, 0), R("wx", 0, 2), R("x", 1, 0), R("wx", 1, 0)]
        scalar += [F(n, 0) for n in range(SIDE)] + [R("x", 0, 4), R("x", 0, 6), R("x", 1, 4)]
        scalar += [F(n, 1) for n in range(SIDE)] + [R("wx", 1, 4), R("wx", 0, 6)]
        scalar += [F(n, h) for n, h in ((4, 0), (5, 0), (4, 1), (5, 1), (6, 0), (7, 0), (6, 1))] + [F(7, 1, start, width) for start, width in pieces]

        both = [(a, operand) for a in range(PASSES) for operand in ("wt", "wr")]
        tensor = [I(0, 0), I(1, 0), O(0, 0), TB(0, 0, 0, "wt"), O(1, 0), TB(1, 0, 0, "wt"), I(2, 0), I(3, 0)]
        tensor += [O(2, 0), TB(2, 0, 0, "wt"), O(3, 0), TB(3, 0, 0, "wt"), TB(0, 0, 0, "wr"), TB(1, 0, 0, "wr")]
        tensor += [I(0, 1), I(1, 1), TB(0, 0, 1, "wt"), TB(1, 0, 1, "wt")]
        tensor += [O(0, 1)] + [TB(0, 1, a, operand) for a, operand in both[:3]]
        tensor += [O(1, 1), TB(1, 1, 0, "wt"), TB(1, 1, 0, "wr"), I(2, 1), TB(1, 1, 1, "wt"), TB(2, 0, 0, "wr"), I(3, 1), TB(3, 0, 0, "wr")]
        tensor += [TB(2, 0, 1, "wt"), TB(3, 0, 1, "wt")] + [TB(n, 0, 1, "wr") for n in range(SIDE)]
        tensor += [X(n, 0, 0) for n in range(SIDE)]
        tensor += [TB(0, 1, 1, "wr"), TB(1, 1, 1, "wr"), O(2, 1), TB(2, 1, 0, "wt"), TB(2, 1, 0, "wr"), X(0, 0, 1), X(1, 0, 1), TB(2, 1, 1, "wt"), TB(2, 1, 1, "wr"), X(2, 0, 1), X(3, 0, 1)]
        tensor += [I(4, 0), I(5, 0), O(3, 1)] + [TB(3, 1, a, operand) for a, operand in both]
        tensor += [I(6, 0), I(7, 0)]
        for n in (4, 5):
            tensor += [O(n, 0), TB(n, 0, 0, "wt"), TB(n, 0, 0, "wr")]
        tensor += [O(6, 0), TB(6, 0, 0, "wt"), O(7, 0), TB(7, 0, 0, "wt")]
        tensor += [X(n, 1, 0) for n in range(SIDE)] + [TB(6, 0, 0, "wr"), TB(7, 0, 0, "wr")] + [X(n, 1, 1) for n in range(SIDE)]
        tensor += [TB(4, 0, 1, "wt"), I(4, 1), TB(5, 0, 1, "wt"), I(5, 1), TB(6, 0, 1, "wt"), TB(7, 0, 1, "wt")]
        tensor += [O(4, 1), TB(4, 1, 0, "wt"), TB(4, 1, 0, "wr"), O(5, 1), TB(5, 1, 0, "wt"), I(6, 1), TB(5, 1, 0, "wr"), TB(4, 1, 1, "wt"), I(7, 1), TB(5, 1, 1, "wt")]
        tensor += [TB(n, h, 1, "wr") for h in (0, 1) for n in (4, 5)]
        tensor += [O(6, 1), TB(6, 1, 0, "wt")] + [X(n, h, a) for a in range(PASSES) for h in (0, 1) for n in (4, 5)]
        tensor += [TB(6, 0, 1, "wr"), TB(7, 0, 1, "wr")] + [X(n, 0, a) for a in range(PASSES) for n in (6, 7)]
        tensor += [TB(6, 1, a, operand) for a, operand in both[1:]] + [X(6, 1, a) for a in range(PASSES)]
        for start, width in pieces:
            tensor += [O(7, 1, start, width)] + [TB(7, 1, a, operand, start, width) for a, operand in both]
            tensor += [X(7, 1, a, start, width) for a in range(PASSES)]
        write_out([sync, vector, scalar, tensor], [])
